import numpy as np, ml_dtypes
CORES = [40,41,42,43,44,45,46,47]
N = 8
import mx_ref
BF = ml_dtypes.bfloat16
def gcols(t, e):
    v = np.concatenate([t.reshape(8, 16, -1, 4), np.zeros((8, 16, 1, 4), BF)], axis=2)
    return np.ascontiguousarray(np.stack([v[g][:, e[g]] for g in range(8)])).reshape(128, -1)
def tile(rs):
    return np.stack(rs, axis=2).reshape(128, -1).astype(BF)
def pick(q, e):
    c = np.concatenate([q[0].reshape(128, -1, 4), np.zeros((128, 1, 4), np.uint8)], axis=1); s = np.concatenate([q[1], np.ones((16, 1), np.uint8)], axis=1)
    return (np.ascontiguousarray(c[:, e].reshape(128, -1)), np.ascontiguousarray(s[:, e]))
def join(*qs):
    return (np.concatenate([q[0] for q in qs], axis=1), np.concatenate([q[1] for q in qs], axis=1))
def put(q, e, v):
    c, s = q[0].reshape(128, -1, 4).copy(), q[1].copy(); c[:, e] = v[0].reshape(128, -1, 4); s[:, e] = v[1]
    return (c.reshape(128, -1), s)
def pk(c, s):
    return (np.ascontiguousarray(c), mx_ref.live(s))
def emit(q):
    return q[0], q[1]
def packed(v, rng):
    q = [mx_ref.quantize(np.ascontiguousarray(v[r])) for r in range(N)]
    return np.stack([a for a, b in q]), np.stack([mx_ref.plane(b, rng) for a, b in q])
def values_of_codes():
    e, c = np.zeros((128, 128, 4), np.float32), np.zeros((128, 2, 4), np.uint8)
    e[np.arange(128), np.arange(128), 0] = 1
    c[:127, :, 0] = np.arange(256).reshape(2, 128).T[:127]
    return mx_ref.matmul(mx_ref.quantize(e.reshape(128, 512).astype(BF)), (c.reshape(128, 8), np.full((16, 2), 127, np.uint8))).T.reshape(-1).astype(np.float64)
CODE_VALUE, SCALE_VALUE = values_of_codes(), 2.0 ** (np.arange(256) - 127.0)
def decode(q):
    return (CODE_VALUE[q[0]].reshape(16, 8, -1, 4) * SCALE_VALUE[q[1]][:, None, :, None] + 0.0).reshape(128, -1).astype(np.float32)
def f(rng, *shape):
    return mx_ref.flush((rng.standard_normal(shape, dtype=np.float32) * np.exp2(rng.integers(-2, 3, shape[:-1] + (1,)))).astype(BF))
def wide(rng, *shape, cols=0):
    v = rng.standard_normal(shape, dtype=np.float32) * np.exp2(rng.integers(-12, 13, shape)).astype(np.float32)
    if cols: v *= np.repeat(np.exp2(rng.integers(-cols, cols + 1, shape[:-2] + (1, shape[-1] // 4))) * (rng.random(shape[:-2] + (1, shape[-1] // 4)) > 0.0625), 4, axis=-1).astype(np.float32)
    return mx_ref.flush(v.astype(BF))
C, B = 384, 256
def big(v):
    v = v.astype(np.float32)
    v[np.abs(v) < np.float32(2.0 ** -16)] = 0
    return v.astype(BF)
def shared(u):
    u = np.array(u).reshape(8, 16, 8, 16, 4)
    for g in range(8): u[np.arange(8) != g, :, g, 0] = 0
    return np.repeat(u.reshape(1, 128, 512), N, axis=0)
def numbers_of(rng):
    return {"x": big(f(rng, N, 128, 4 * C)), "h": np.array(f(rng, N, 128, 4 * B)), "u": shared(f(rng, 128, 512)), "v": np.array(f(rng, N, 128, 512))}
def layers(rng, still=[]):
    w = np.array(f(rng, N, 128, 2048)).reshape(N, 8, 16, 4, 8, 16, 4)
    for i in still:
        w[:, :, i] = 0
        w[:, :, :, :, :, i] = 0
    return w
def weights(rng, w):
    c, p = packed(np.ascontiguousarray(w).reshape(N, 128, 2048), rng)
    return {"wc": c, "ws": p}
def tiles(x, h, u, v):
    return {"x": x.reshape(N, 128, 4 * C).astype(BF), "h": h.reshape(N, 128, 4 * B).astype(BF), "u": shared(u), "v": v}
def setup_inputs(rng):
    return {**numbers_of(rng), **weights(rng, layers(rng))}
def setup_inputs_ties(rng):
    d = numbers_of(rng)
    e = rng.permutation(N)
    a = (rng.integers(4, 8, (8, 8, 3, 4)) * rng.choice([-1.0, 1.0], (8, 8, 3, 4))).astype(np.float32).astype(BF)
    a[:, :, 2] = 0
    x, h = d["x"].reshape(N, 8, 16, C, 4), d["h"].reshape(N, 8, 16, B, 4)
    for r in range(N):
        for g in range(8):
            x[r, g, :8] = a[g][:, np.zeros(C, int) if r == e[0] else rng.permutation(C) % 3]
            h[r, g, :8] = a[g][:, rng.permutation(B) % 3]
    x[e[1]] = 0
    u = d["u"][0].copy().reshape(8, 16, 8, 16, 4)
    u[:, 8:, :, 0] = 0
    return {**tiles(x, h, u, d["v"]), **weights(rng, layers(rng, range(8)))}
def setup_inputs_near(rng):
    d = numbers_of(rng)
    a, c = rng.permutation(8), rng.permutation(8) % 2 * 2.0 - 1.0
    o = a % 4
    size = np.where(o == 3, 2.0 ** -6, 1.0)[:, None, None]
    x, h = d["x"].astype(np.float32).reshape(N, 8, 16, C, 4), d["h"].astype(np.float32).reshape(N, 8, 16, B, 4)
    shift = rng.integers(0, C, (N, 8, 1))
    for t, s in ((x, (np.arange(C) + shift) % C // 2), (h, np.argsort(rng.random((N, 8, B)), axis=2) * (C // 2) // (B - 1))):
        k = ((s[..., None] >> np.arange(8)) & 1) * np.exp2(np.arange(8) - 23.0) * size
        t[:, :, 0] = 0
        t[:, :, 0, :, 0] = np.where(o < 2, c, 0)[:, None]
        t[:, :, 8] = k[..., :4]
        t[:, :, 9] = k[..., 4:]
        t[:, :, 10:] = rng.integers(4, 8, (N, 8, 6, s.shape[2], 4)) * 2.0 ** -20 * size[..., None]
        t[:, :, 10, :, 0] = np.where(o < 2, 2.0 ** -16, 0)[:, None]
        t[:, :, 11, :, 0] = 2.0 ** -20 * size[..., 0]
    h[:, o == 3, 10, 1::2, 0] = 2.0 ** -30
    at = np.argsort(a)
    for r in range(N):
        for g in np.concatenate([rng.permutation(at[:4])[:2], rng.permutation(at[4:])[:2]]):
            x[r, g, 0, (C // 4 + rng.integers(C // 2) - shift[r, g, 0]) % C, 0] = rng.choice([-1.0, 1.0]) * 2.0 ** 30
    u = d["u"][0].astype(np.float32).reshape(128, 128, 4)
    u[:, ::16] = 0
    for g in range(8):
        k = 1.0 if o[g] == 0 else 2.0 ** -30
        u[16 * g, 16 * g, 0] = k
        u[16 * g + 8:16 * g + 10, 16 * g] = k
        u[16 * g + 10, 16 * g, 0] = k * (64.0 if o[g] < 2 else 1.0)
        u[16 * g + 11, 16 * g, 0] = k
    w = layers(rng, [0, 8, 9, 10, 11, 12, 13, 14, 15])
    change = np.array([0.0, -1, -2, 1])[(rng.permutation(N)[:, None] + 2 * (a // 4)) % 4]
    for g in range(8): w[:, g, 11, 0, g, 11, 0] = (4 * change[:, g]).astype(np.float32).astype(BF)
    return {**tiles(x, h, u.astype(BF), d["v"]), **weights(rng, w)}
def setup_inputs_ends(rng):
    d = numbers_of(rng)
    x, h = d["x"].astype(np.float32).reshape(N, 8, 16, C, 4), d["h"].astype(np.float32).reshape(N, 8, 16, B, 4)
    for t, s in ((x, np.argsort(rng.random((N, 8, C)), axis=2)), (h, rng.integers(0, C, (N, 8, B)))):
        z = ((s[..., None] >> np.arange(12)) & 1) * np.exp2(np.arange(12.0))
        t[:, :, 0] = 0
        for i in range(3): t[:, :, 8 + i] = z[..., 4 * i:4 * i + 4]
    k = np.stack([rng.permutation(8) for r in range(N)])
    x[:, :, 0, :, 0] = ((rng.permutation(8) < 2) * 512.0 * (np.arange(N) % 2)[:, None])[:, :, None]
    h[:, :, 0, :, 0] = np.array([-1024.0, -1024, 1024, 1024, 0, 0, 0, 0])[k][:, :, None]
    x[:, :, 4] = 0
    x[:, :, 4, :, 0] = 64
    w = layers(rng, [0, 8, 9, 10, 11, 12, 13, 14, 15])
    for g in range(8): w[:, g, 4, 0, g, 0, 0] = np.array([1024.0, 0, -1024, 0, 1024, -1024, 0, 0])[k[:, g]].astype(np.float32).astype(BF)
    u = d["u"][0].astype(np.float32).reshape(128, 128, 4)
    u[:, ::16] = 0
    for g in range(8):
        u[16 * g, 16 * g, 0] = 1
        u[16 * g + 8:16 * g + 11, 16 * g] = 1
    return {**tiles(x, h, u.astype(BF), d["v"]), **weights(rng, w)}
def setup_inputs_huge(rng):
    d = numbers_of(rng)
    k = rng.permutation(8)
    def sized(n):
        s = np.where((k < 4)[:, None, None, None], rng.choice([-1.0, 1.0], (N, 8, 1, n, 1)), 1.0)
        return ((0.7 + 0.2 * rng.random((N, 8, 1, n, 1))) * (0.95 + 0.05 * rng.random((N, 8, 16, n, 4))) * s * 2.0 ** 30).astype(np.float32)
    u = d["u"][0].astype(np.float32).reshape(8, 16, 8, 16, 4)
    u[:, :, :, 0] = 2.0 ** 30 * (1 - 0.1 * rng.random((8, 16, 8, 4))) * (k % 2 * 2.0 - 1.0)[:, None]
    w = np.zeros((N, 128, 4, 128, 4), np.float32)
    i = np.arange(128)
    for b in range(4): w[:, i, b, i, b] = -1
    return {**tiles(sized(C), sized(B), u.astype(BF), d["v"]), **weights(rng, w.astype(BF))}
def setup_inputs_spread(rng):
    d = setup_inputs(rng)
    d["x"] = big(wide(rng, N, 128, 4 * C, cols=6))
    d["h"] = wide(rng, N, 128, 4 * B)
    return d
def check_inputs(d):
    b = []
    for k in ("x", "h", "u", "v"):
        a = np.abs(d[k].astype(np.float32))
        if not (np.isfinite(a).all() and ((a == 0) | (a >= 2.0 ** -30) & (a <= 2.0 ** 30)).all()): b.append("a value of " + k)
    a = d["u"].astype(np.float32)
    if (a != a[:1]).any(): b.append("u: not the same on all ranks")
    a = a.reshape(N, 8, 16, 8, 16, 4)
    for g in range(8):
        if (a[:, np.arange(8) != g, :, g, 0] != 0).any(): b.append("u: column 16 * g outside group g")
    none, least, most = [emit(mx_ref.quantize(np.full((128, 16), k, np.float32).astype(BF)))[1][0, 0] for k in (0.0, 2.0 ** -30, 2.0 ** 30)]
    for r in range(N):
        if ((d["wc"][r] == 0x7F) | (d["wc"][r] == 0xFF)).any(): b.append("wc: a code that is no number")
        s = mx_ref.live(d["ws"][r])
        if ((s != none) & ((s < least) | (s > most))).any(): b.append("ws: a scale out of range")
    return b
def keys(qu, c):
    return mx_ref.matmul(qu, c)[::16] + np.float32(0.0)
def order(k):
    return np.argsort(k, axis=1, kind="stable")
def step(t, m, p, a, w):
    lower = gcols(t, np.take_along_axis(m, np.maximum(p - 1, 0), axis=1)).astype(np.float32)
    upper = gcols(t, np.take_along_axis(m, np.minimum(p, m.shape[1] - 1), axis=1)).astype(np.float32)
    z = mx_ref.quantize(((lower + upper) * np.float32(0.5)).astype(BF))
    d = decode(a)
    return tile([mx_ref.matmul(pick(w, np.arange(128 * b, 128 * b + 128)), z) * np.float32(0.03125) + d[:, b::4] for b in range(4)])
def reference(x, h, u, v, wc, ws):
    qu = [mx_ref.quantize(u[r]) for r in range(N)]
    lay = [pk(wc[r], ws[r]) for r in range(N)]
    k0 = [keys(qu[r], mx_ref.quantize(x[r])) for r in range(N)]
    m0 = [order(k0[r]) for r in range(N)]
    sample = [mx_ref.quantize(gcols(x[r], m0[r][:, 1::2])) for r in range(N)]
    sent, bridge = [], []
    for r in range(N):
        came = sample[(r + 1) % N]
        k1 = np.concatenate([k0[r], keys(qu[r], came)], axis=1)
        a = mx_ref.quantize(h[r])
        below = k1[:, None, :] < keys(qu[r], a)[:, :, None]
        t = np.concatenate([x[r], decode(came).astype(BF)], axis=1)
        sent.append(mx_ref.quantize(step(t, order(k1), np.sum(below, axis=2), a, lay[r])))
        bridge.append(2 * np.sum(below[:, :, C:], axis=2))
    y, ov = np.zeros((N, 128, B), np.float32), np.zeros((N, 8, B), np.float32)
    oc, osc = np.zeros((N, 128, 4 * B), np.uint8), np.zeros((N, 16, B), np.uint8)
    for r in range(N):
        a, i = sent[r - 1], np.clip(bridge[r - 1], 1, C - 1)
        s, k = keys(qu[r], a), np.take_along_axis(k0[r], m0[r], axis=1)
        p = i + (s > np.take_along_axis(k, i, axis=1)) - (s < np.take_along_axis(k, i - 1, axis=1))
        last = mx_ref.quantize(step(x[r], m0[r], p, a, lay[r]))
        y[r] = mx_ref.matmul(mx_ref.quantize(v[r]), last)
        ov[r] = p
        oc[r], osc[r] = emit(last)
    return {"y": y, "ov": ov, "oc": oc, "osc": osc}

@@ -1,0 +1,541 @@
+from concourse.mybir import dt, AluOpType as A, ActivationFunctionType as F
+
+C, B = 384, 256
+HB = B // 2
+NS = C // 2
+H = 2.0 ** 80
+PL = 608
+NA = 208
+f32, bf, u16, i32, cod, u8 = "float32", "bfloat16", "uint16", "int32", "float8_e4m3fn_x4", "uint8"
+
+TILES = [(0, 384, [None, 23, 22, 21]), (1280, 128, [4, 3, 2, 1]), (384, 320, [20, 19, 18, 17]),
+         (704, 256, [16, 15, 14, 13]), (960, 192, [12, 11, 10, 9]), (1152, 128, [8, 7, 6, 5])]
+ON_SCALAR = (23, 22, 21)
+WF = {"own": 0, "pre": 32, "br": 80, "cb": 112, "rt": 136, "rowl": 160, "tla": 184}
+WU = {"lpos": 0, "lo": 24, "lc": 56, "l1": 88, "li": 104, "lp": 136, "lm": 152}
+
+
+def _s(n, d):
+    return ("sbuf", [128, n], d)
+
+
+SCRATCH = {
+    "xt": _s(4 * C, bf), "ht": _s(4 * B, bf), "ut": _s(512, bf), "vt": _s(512, bf),
+    "qx": _s(C, cod), "sx": _s(C, u8), "qxn": _s(C, cod), "sxn": _s(C, u8),
+    "qh": _s(B, cod), "sh": _s(B, u8), "qu": _s(128, cod), "su": _s(128, u8), "qr": _s(128, cod), "sr": _s(128, u8),
+    "qv": _s(128, cod), "sv": _s(128, u8), "qw": _s(512, cod), "sw": _s(512, u8),
+    "one": _s(512, bf), "t32": _s(516, bf), "g1a": _s(512, bf), "g1": _s(512, bf), "c4": _s(512, bf), "et": _s(1040, bf),
+    "qg": _s(128, cod), "sg": _s(128, u8), "qc": _s(128, cod), "sc4": _s(128, u8), "qe": _s(512, cod), "se": _s(512, u8),
+    "ci": _s(8, i32), "cf": _s(32, f32), "ic": _s(32, f32), "jm": _s(400, f32), "jm4": _s(192, f32), "jj": _s(400, f32),
+    "m0": _s(C, f32), "rz": _s(C, f32), "rs": _s(C, f32), "ms": _s(C, f32), "tmpa": _s(400, f32), "tmpb": _s(400, f32),
+    "cp": _s(400, f32), "cp4": _s(192, f32), "cp4o": _s(64, f32), "wf": _s(216, f32), "wu": _s(284, u16), "lst": _s(72, u16),
+    "fl": _s(64, f32), "fd": _s(64, f32), "ix": _s(64, f32),
+    "km": _s(C, f32), "kc": _s(C, f32), "ksb": _s(C, f32), "knb": _s(C, f32), "srep": _s(B, f32),
+    "ts": _s(4 * 1408, bf), "qs": _s(1408, cod), "ss": _s(1408, u8), "junk": _s(4416, bf), "rk": _s(C, f32),
+    "mt": _s(400, f32), "lout": _s(16, u16), "lin": _s(16, u16), "sp": _s(400, f32), "sexp": _s(B, f32),
+    "dn": _s(4 * C, bf), "tb": _s(4 * PL, bf), "ws0": _s(C, f32), "b0": _s(B, f32), "b0s": _s(B, f32),
+    "bt": _s(768, bf), "qb": _s(192, cod), "sb": _s(192, u8), "n0": _s(64, f32),
+    "kl": _s(2 * B, f32), "gn": _s(NA, f32), "mw": _s(400, f32), "wa": _s(NA, f32), "b1": _s(B, f32), "b1s": _s(B, f32),
+    "bt1": _s(768, bf), "qb1": _s(192, cod), "sb1": _s(192, u8), "n1": _s(192, f32), "lb": _s(4 * B, bf),
+    "z1": _s(4 * B, bf), "qz1": _s(B, cod), "sz1": _s(B, u8), "y1": _s(4 * B, bf), "qy1": _s(B, cod), "sy1": _s(B, u8),
+    "bout": _s(32, u16), "bin": _s(32, u16), "qa": _s(B, cod), "sa": _s(B, u8),
+    "zt": _s(1600, bf), "th": _s(2 * B, f32), "tq": _s(3 * B, bf), "cp2": _s(B, f32), "p3s": _s(B, f32),
+    "sm": _s(B, f32), "ssc": _s(B, f32), "pv": _s(B, f32),
+    "z2": _s(4 * B, bf), "qz2": _s(B, cod), "sz2": _s(B, u8), "y2": _s(4 * B, bf), "qy2": _s(B, cod), "sy2": _s(B, u8), "yo": _s(B, f32),
+}
+for _b in range(8):
+    SCRATCH["ps%d" % _b] = ("psum", [128, 512], f32)
+
+SEMAPHORES = ["eV", "eS", "eP", "eG", "dx", "du", "dh", "dv", "dw", "dws", "ax", "al", "ab", "ay0", "ay1", "left", "so1", "so2"]
+
+
+def rank_program(g, core, T, topo):
+    rank = T.rank_of(core)
+    if rank is None:
+        return
+    n = len(T.cores)
+    nxt, prv = T.cores[(rank + 1) % n], T.cores[(rank - 1) % n]
+    V, S, P = g.vector, g.scalar, g.tensor
+    Q = {"V": V, "S": S, "P": P, "G": g, "Y": g.sync}
+    cnt = {"V": 0, "S": 0, "P": 0, "G": 0}
+    wrote, read, waited = {}, {}, {e: {} for e in Q}
+
+    def need(e, r, w):
+        want = {}
+        for t in list(r) + list(w):
+            ds = [wrote[t]] if t in wrote else []
+            if t in w or t.startswith("ps"):
+                ds = ds + read.get(t, [])
+            for sem, c in ds:
+                if t.startswith("ps") and sem == "e" + e:
+                    continue
+                want[sem] = max(want.get(sem, 0), c)
+        for sem, c in want.items():
+            if waited[e].get(sem, 0) < c:
+                Q[e].wait_ge(T.sem[sem], c)
+                waited[e][sem] = c
+
+    def note(mark, r, w):
+        for t in r:
+            read.setdefault(t, []).append(mark)
+        for t in w:
+            wrote[t] = mark
+            read[t] = []
+
+    def op(e, call, r=(), w=()):
+        need(e, r, w)
+        cnt[e] += 1
+        call().then_inc(T.sem["e" + e], 1)
+        note(("e" + e, cnt[e]), r, w)
+
+    dcnt = {}
+
+    def dma(e, out, in_, sem, r=(), w=()):
+        need(e, r, w)
+        dcnt[sem] = dcnt.get(sem, 0) + 16
+        Q[e].dma_start(out, in_).then_inc(T.sem[sem], 16)
+        note((sem, dcnt[sem]), r, w)
+
+    def send(dst, out, in_, sem, r):
+        need("G", r, ())
+        rid, pid = topo.addr(dst)[:2]
+        g.remote_dma(out, in_, T.sem[sem], T.sem.left, pid, rid, topo.mask(core, dst))
+        dcnt["left"] = dcnt.get("left", 0) + len(topo.engines(core, dst))
+
+    def ts(out, in0, s1, op0, s2=None, op1=None, r=(), w=()):
+        if op1 is None:
+            op("V", lambda: V.tensor_scalar(out, in0, s1, None, op0), r, w)
+        else:
+            op("V", lambda: V.tensor_scalar(out, in0, s1, s2, op0, op1), r, w)
+
+    def tt(out, a, b, o, r, w):
+        op("V", lambda: V.tensor_tensor(out, a, b, o), r, w)
+
+    def scan(out, d0, d1, init, o0, o1, r, w):
+        op("V", lambda: V.tensor_tensor_scan(out, d0, d1, init, o0, o1), r, w)
+
+    def cpy(out, in_, r, w):
+        op("V", lambda: V.tensor_copy(out, in_), r, w)
+
+    def fill(ap, c, w):
+        op("V", lambda: V.memset(ap, c), (), w)
+
+    def quant(q, s, t, r, w):
+        op("V", lambda: V.quantize_mx(q, s, t), r, w)
+
+    def act(out, in_, func, r, w, bias=0.0, scale=1.0, acc=None):
+        if func == F.Copy:
+            op("S", lambda: S.activation(out, in_, func, scale=scale, accum_out=acc), r, w)
+        else:
+            op("S", lambda: S.activation(out, in_, func, bias=bias, scale=scale, accum_out=acc), r, w)
+
+    def mm(bank, m, lq, ls, rq, rs_, start, stop, r):
+        op("P", lambda: P.matmul_mx(T["ps%d" % bank][:, 0:m], lq, ls, rq, rs_, start, stop), r, ["ps%d" % bank])
+
+    def by(v):
+        return v.bitcast(dt.uint8)
+
+    def wf(k, a, b):
+        return T.wf[:, WF[k] + a:WF[k] + b]
+
+    def wu(k, a, b):
+        return T.wu[:, WU[k] + a:WU[k] + b]
+
+    def cf(k):
+        return T.cf[:, k:k + 1]
+
+    def unit(bank, m, b, q, s, stop, r):
+        mm(bank, m, T.qe[:, 128 * b:128 * b + 128], T.se[:, 128 * b:128 * b + 128], q, s, True, stop, ["qe%d" % b] + r)
+
+    en, ep = len(topo.engines(nxt, core)), len(topo.engines(prv, core))
+    wrote["qxn"], wrote["lin"], wrote["bin"] = ("ax", 2 * en), ("al", en), ("ab", ep)
+    wrote["qa0"], wrote["qa1"] = ("ay0", 2 * ep), ("ay1", 2 * ep)
+
+    dma("Y", T.xt[:], T.x[:], "dx", w=["xt"])
+    dma("S", T.ut[:], T.u[:], "du", w=["ut"])
+    dma("Y", T.ht[:], T.h[:], "dh", r=["xt"], w=["ht"])
+
+    def iota(out, pat, cm, w, small=True):
+        if small:
+            op("G", lambda: g.iota(out, pat, 0, cm, allow_small_or_imprecise_dtypes=True), (), w)
+        else:
+            op("G", lambda: g.iota(out, pat, 0, cm), (), w)
+
+    def select(out, in_, pat, cmp_, base, cm, r, w):
+        op("G", lambda: g.affine_select(out, in_, pat, cmp_, 0.0, base, cm), r, w)
+
+    def holding(outs, j, m, col, r, between):
+        act(T.tmpa[:, 0:m], j, F.Relu, r, ["tmpa"], scale=-2048.0, bias=col)
+        between[0]()
+        act(T.tmpb[:, 0:m], T.tmpa[:, 0:m], F.Square, ["tmpa"], ["tmpb"], scale=1.0 / 32, bias=-48.0)
+        between[1]()
+        for out, k, w in outs:
+            act(out, T.tmpb[:, 0:k], F.Identity, ["tmpb"], w, scale=-1.0, bias=2304.0)
+
+    def unit_codes(b):
+        o = 520 * (b % 2) + 2 - 2 * (b // 2)
+        quant(T.qe[:, 128 * b:128 * b + 128], T.se[:, 128 * b:128 * b + 128], T.et[:, o:o + 512], ["et%d" % (b % 2)], ["qe%d" % b])
+
+    iota(T.ci[:, 0:1], [[0, 1]], 1, ["ci0"], False)
+    iota(T.ic[:], [[1, 32]], 0, ["ic"])
+    iota(T.jm[:], [[0, 25], [1, 16]], 0, ["jm"])
+    fill(T.t32[:], 32.0, ["t32"])
+    ts(T.ci[:, 1:2], T.ci[:, 0:1], 15, A.bitwise_and, r=["ci0"], w=["ci1"])
+    ts(T.lst[:, 0:8], T.ic[:, 0:8], 16.0, A.mult, r=["ic"], w=["lu"])
+    cpy(cf(0), T.ci[:, 1:2], ["ci1"], ["cf0"])
+    ts(T.ci[:, 2:3], T.ci[:, 1:2], 2, A.logical_shift_right, r=["ci1"], w=["ci2"])
+    fill(T.one[:], 1.0, ["one"])
+    cpy(cf(4), T.ci[:, 2:3], ["ci2"], ["cf4"])
+    for k in range(2):
+        select(T.et[:, 520 * k:520 * k + 516], T.t32[:], [[-1, 516]], A.is_equal, 2 + k, 4, ["t32"], ["et%d" % k])
+    select(T.g1a[:], T.one[:], [[-16, 8], [0, 64]], A.is_ge, 0, 1, ["one"], ["g1a"])
+    act(cf(16), cf(0), F.Identity, ["cf0"], ["cf16"], scale=-2 * H)
+    act(cf(17), cf(0), F.Identity, ["cf0"], ["cf17"], scale=4 * H, bias=4 * H)
+    act(cf(18), cf(0), F.Identity, ["cf0"], ["cf18"], scale=2048.0, bias=2048.0)
+    act(cf(19), cf(4), F.Identity, ["cf4"], ["cf19"], scale=2048.0, bias=2048.0)
+    act(T.rz[:], T.jm[:, 0:C], F.Sign, ["jm"], ["rz"])
+    holding([(T.cp[:], 400, ["cp", "cp15"]), (T.cp2[:], B, ["cp2"])], T.jm[:], 400, cf(18), ["jm", "cf18"],
+            [lambda: act(T.m0[:], T.jm[:, 0:C], F.Abs, ["jm", "cf16"], ["m0"], scale=2 * H, bias=cf(16)),
+             lambda: act(T.rs[:], T.rz[:], F.Identity, ["rz"], ["rs"], scale=-4 * H, bias=4 * H)])
+    for lo, wd, blocks in TILES:
+        fill(T.ts[:, 4 * (lo + 16 * blocks[3]):4 * (lo + wd)], 0.0, ["tz%d" % lo])
+    ts(cf(6), cf(0), 15.0, A.is_equal, 2048.0, A.mult, r=["cf0"], w=["cf6"])
+    ts(cf(9), cf(0), 11.0, A.is_ge, 1000.0, A.mult, r=["cf0"], w=["cf9"])
+    ts(cf(12), cf(0), 16.0, A.mult, 7.0, A.add, r=["cf0"], w=["cf12"])
+    ts(wf("tla", 0, 13), T.ic[:, 0:13], 15.0, A.mult, cf(0), A.add, r=["ic", "cf0"], w=["tla0"])
+    ts(cf(7), cf(6), -4096.0, A.add, r=["cf6"], w=["cf7"])
+    ts(cf(8), cf(6), cf(0), A.subtract, -4080.0, A.add, r=["cf6", "cf0"], w=["cf8"])
+    quant(T.qu[:], T.su[:], T.ut[:], ["ut"], ["qu"])
+    ts(cf(11), cf(0), 32.0, A.mult, cf(9), A.add, r=["cf0", "cf9"], w=["cf11"])
+    cpy(T.qr[:].bitcast(dt.uint32), T.qu[:].bitcast(dt.uint32).indirect(T.lst[:, 0:8]), ["qu", "lu"], ["qr"])
+    cpy(T.sr[:], T.su[:].indirect(T.lst[:, 0:8]), ["qu", "lu"], ["sr"])
+    later = [
+        lambda: ts(cf(15), cf(12), NS - 9.0, A.min, r=["cf12"], w=["cf15"]),
+        lambda: ts(wf("tla", 16, 29), wf("tla", 0, 13), 1.0, A.max, float(NS), A.min, r=["tla0"], w=["tla1"]),
+        lambda: ts(cf(13), cf(4), 3.0, A.is_equal, 2048.0, A.mult, r=["cf4"], w=["cf13"]),
+        lambda: ts(T.lst[:, 8:24], T.ic[:, 0:16], 16.0, A.mult, 15.0, A.add, r=["ic"], w=["lx"]),
+        lambda: ts(cf(14), cf(11), 32.0, A.add, 385.0, A.min, r=["cf11"], w=["cf14"]),
+        lambda: fill(wf("rowl", 0, 1), 0.0, ["rowl0"]),
+        lambda: ts(wf("cb", 0, 24), T.ic[:, 0:24], 16.0, A.mult, cf(8), A.add, r=["ic", "cf8"], w=["cb"]),
+        lambda: fill(T.mt[:, 384:400], 0.0, ["mt"]),
+        lambda: ts(T.lst[:, 56:69], wf("tla", 16, 29), 2.0, A.mult, r=["tla1"], w=["la"]),
+        lambda: fill(T.lout[:], 0, ["lout"]),
+        lambda: ts(T.lst[:, 24:40], T.ic[:, 0:16], 0.0, A.mult, cf(14), A.add, r=["ic", "cf14"], w=["lc0"]),
+        lambda: ts(T.lst[:, 40:56], T.ic[:, 0:16], 0.0, A.mult, cf(15), A.add, r=["ic", "cf15"], w=["lc1"]),
+        lambda: ts(cf(5), cf(13), -3072.0, A.add, r=["cf13"], w=["cf5"]),
+        lambda: fill(T.fl[:], 0.0, ["flz"]),
+        lambda: fill(T.bt[:, 512:768], 0.0, ["btz"])]
+
+    def some(k):
+        for _ in range(k):
+            later.pop(0)()
+
+    unit_codes(0)
+    unit_codes(2)
+    some(3)
+
+    quant(T.qx[:], T.sx[:], T.xt[:], ["xt"], ["qx"])
+    mm(0, C, T.qr[:], T.sr[:], T.qx[:], T.sx[:], True, True, ["qr", "sr", "qx"])
+    mm(2, C, T.qr[:], T.sr[:], T.qx[:], T.sx[:], True, True, ["qr", "sr", "qx"])
+    send(prv, by(T.qxn[:]), by(T.qx[:]), "ax", ["qx"])
+    send(prv, T.sxn[:], T.sx[:], "ax", ["qx"])
+    select(T.g1[:], T.g1a[:], [[16, 8], [0, 64]], A.is_ge, 15, -1, ["g1a"], ["g1"])
+    iota(T.jj[:], [[1, 400]], 0, ["jj"])
+    iota(T.jm4[:], [[0, 48], [1, 4]], 0, ["jm4"])
+    select(T.c4[:], T.g1[:], [[0, 32], [1, 4], [-1, 4]], A.is_equal, 0, 0, ["g1"], ["c4"])
+    unit_codes(1)
+    unit_codes(3)
+    some(2)
+    act(T.ksb[:], T.ps2[:, 0:C], F.Copy, ["ps2"], ["ksb"])
+
+    tt(T.km[:], T.ps0[:, 0:C], T.m0[:], A.add, ["ps0", "m0"], ["km"])
+    some(1)
+    scan(T.kc[:], T.rs[:], T.km[:], 0.0, A.add, A.min, ["rs", "km"], ["kc"])
+    some(1)
+    at = [0]
+
+    def close(k):
+        lo, wd, blocks = TILES[k]
+        quant(T.qs[:, lo:lo + wd], T.ss[:, lo:lo + wd], T.ts[:, 4 * lo:4 * (lo + wd)],
+              ["tz%d" % lo] + ["t%d_%d" % (lo, t) for t in range(4)], ["qs%d" % lo])
+        if k:
+            P.wait_ge(T.sem.eP, cnt["P"])
+        mm(1, wd, T.qg[:], T.sg[:], T.qs[:, lo:lo + wd], T.ss[:, lo:lo + wd], k == 0, k == len(TILES) - 1, ["qg", "qs%d" % lo])
+
+    def block(k, t):
+        lo, wd, blocks = TILES[k]
+        c, name = blocks[t], "t%d_%d" % (lo, t)
+        if c is None:
+            tt(T.ts[:, 0:4 * C:4], T.ps0[:, 0:C], T.kc[:], A.is_ge, ["ps0", "kc", "tz0"], [name])
+            return None
+        m = 16 * c
+        bits, key, spare = T.ts[:, 4 * lo + t:4 * (lo + m):4], T.kc[:, m + 15:m + 16], T.junk[:, at[0]:at[0] + m]
+        at[0] += m
+        if c in ON_SCALAR:
+            act(spare, T.ksb[:, 0:m], F.Sign, ["ksb", "kc"], ["sg%d" % c], scale=-1.0, bias=key)
+            return lambda: act(bits, spare, F.Relu, ["sg%d" % c, "tz%d" % lo], [name, "rowl%d" % c], scale=-1.0, acc=wf("rowl", c, c + 1))
+        ts(bits, T.ps0[:, 0:m], key, A.is_gt, r=["ps0", "kc", "tz%d" % lo], w=[name])
+        act(spare, bits, F.Copy, [name], ["rowl%d" % c], acc=wf("rowl", c, c + 1))
+        return None
+
+    for second in [block(0, t) for t in (1, 2, 3)]:
+        second()
+    block(0, 0)
+    block(2, 0)
+    scan(T.tmpb[:, 0:C], T.rz[:], T.ts[:, 0:4 * C:4], 0.0, A.mult, A.add, ["rz", "t0_0"], ["tmpb"])
+    for t in range(1, 4):
+        block(2, t)
+    for t in range(4):
+        block(1, t)
+    quant(T.qg[:], T.sg[:], T.g1[:], ["g1"], ["qg"])
+    tt(wf("rt", 0, 24), wf("cb", 0, 24), T.tmpb[:, 15:C:16], A.subtract, ["cb", "tmpb"], ["rt"])
+    block(3, 0)
+    block(3, 1)
+    close(0)
+    dma("Y", by(T.qw[:]), T.wc[:], "dw", r=["qs0"], w=["qw"])
+    dma("Y", T.sw[:], T.ws[:], "dws", w=["sw"])
+    dma("Y", T.vt[:], T.v[:], "dv", w=["vt"])
+    close(2)
+    block(3, 2)
+    block(3, 3)
+    close(1)
+    for k in (4, 5):
+        for t in range(4):
+            block(k, t)
+            if t == 1:
+                close(k - 1)
+    some(2)
+    close(5)
+    quant(T.qh[:], T.sh[:], T.ht[:], ["ht"], ["qh"])
+    tt(T.cp[:, 15:C:16], wf("rt", 0, 24), wf("rowl", 0, 24), A.subtract, ["rt"] + ["rowl%d" % c for c in range(24)], ["cp15"])
+    some(1)
+    scan(T.rk[:], T.ps1[:, 0:C], T.cp[:, 0:C], -1.0, A.max, A.add, ["ps1", "cp", "cp15"], ["rk"])
+    ts(wu("lpos", 0, 24), T.rk[:, 15:C:16], 2048.0, A.add, r=["rk"], w=["lpos"])
+    some(1)
+    ts(T.cp[:, 15:400:16], T.ic[:, 0:25], 0.0, A.mult, cf(7), A.add, r=["ic", "cf7"], w=["cp15"])
+    cpy(T.mt[:].indirect(wu("lpos", 0, 24)), T.jj[:, 0:C], ["lpos", "jj"], ["mt"])
+
+    mm(2, C, T.qr[:], T.sr[:], T.qxn[:], T.sxn[:], True, True, ["qr", "sr", "qxn"])
+    mm(3, B, T.qr[:], T.sr[:], T.qh[:], T.sh[:], True, True, ["qr", "sr", "qh"])
+    act(T.knb[:], T.ps2[:, 0:C], F.Copy, ["ps2"], ["knb"])
+    act(T.ms[:], T.jm[:, 0:C], F.Relu, ["jm", "cf17"], ["ms"], scale=-4 * H, bias=cf(17))
+
+    def arrived_plane(b):
+        bank = (0, 2)[b % 2]
+        unit(bank, C, b, T.qxn[:], T.sxn[:], True, ["qxn"])
+        act(T.dn[:, C * b:C * b + C], T["ps%d" % bank][:, 0:C], F.Copy, ["ps%d" % bank], ["dn%d" % b], scale=1.0 / 64)
+
+    arrived_plane(0)
+    act(T.srep[:], T.ps3[:, 0:B], F.Copy, ["ps3"], ["srep"])
+    arrived_plane(1)
+    holding([(T.cp4o[:], 64, ["cp4o"]), (T.cp4[:], 192, ["cp4"])], T.jm4[:], 192, cf(19), ["jm4", "cf19"],
+            [lambda: arrived_plane(2), lambda: arrived_plane(3)])
+    for b in range(4):
+        unit(4 + b, HB, b, T.qh[:, 0:HB], T.sh[:, 0:HB], False, ["qh"])
+
+    cpy(T.mt[:, 0:386:385], T.mt[:, 1:385:383], ["mt"], ["mt"])
+    some(2)
+    scan(T.mw[:], T.mt[:], T.cp[:], -1.0, A.max, A.add, ["mt", "cp", "cp15"], ["mw"])
+    cpy(T.km[:, 0:NA], T.mt[:].indirect(T.lst[:, 56:69]), ["mt", "la"], ["km"])
+    ts(wu("lm", 0, 25), T.mw[:, 15:400:16], 2048.0, A.add, r=["mw"], w=["lm"])
+    act(T.sp[:], T.ksb[:].indirect(wu("lm", 0, 25)), F.Copy, ["ksb", "lm"], ["sp"])
+    act(T.sp[:, 0:1], cf(0), F.Identity, ["cf0", "sp"], ["spa"], scale=0.0, bias=-H)
+    act(T.sp[:, 385:386], cf(0), F.Identity, ["cf0", "sp"], ["spb"], scale=0.0, bias=3 * H)
+    scan(T.rk[:, 0:NA], T.km[:, 0:NA], T.cp[:, 0:NA], -1.0, A.max, A.add, ["km", "cp", "cp15"], ["rk"])
+    tt(T.sm[:], T.ps3[:, 0:B], T.m0[:, 0:B], A.add, ["ps3", "m0"], ["sm"])
+    ts(T.lout[:, 0:13], T.rk[:, 15:NA:16], 2048.0, A.add, r=["rk"], w=["lout"])
+    send(prv, T.lin[:], T.lout[:], "al", ["lout"])
+    scan(T.ssc[:], T.rs[:, 0:B], T.sm[:], 0.0, A.add, A.min, ["rs", "sm"], ["ssc"])
+    act(T.sexp[:], T.ssc[:].indirect(T.lst[:, 8:24]), F.Copy, ["ssc", "lx"], ["sexp"])
+
+    def own_plane(t):
+        act(T.tb[:, PL * t + NA:PL * t + PL], T.xt[:].indirect(wu("lm", 26 * t + 26, 26 * t + 51)), F.Copy, ["xt", "lm%d" % t], ["xs%d" % t], scale=0.5)
+
+    def means(t):
+        tt(T.zt[:, 400 * t:400 * t + C + 1], T.tb[:, PL * t + NA:PL * t + NA + C + 1], T.tb[:, PL * t + NA + 1:PL * t + NA + C + 2],
+           A.add, ["xs%d" % t], ["zt%d" % t])
+
+    scan(T.ws0[:], T.ms[:], T.sp[:, 1:C + 1], 0.0, A.add, A.min, ["ms", "sp"], ["ws0"])
+    for t in range(4):
+        ts(wu("lm", 26 * t + 26, 26 * t + 51), T.mw[:, 15:400:16], 2048.0 + t / 4, A.add, 4.0, A.mult, r=["mw"], w=["lm%d" % t])
+    own_plane(0)
+    own_plane(1)
+    ends = ["sp", "spa", "spb"]
+    tt(T.b0[:], T.sp[:].indirect(T.lst[:, 24:40]), T.sexp[:], A.is_lt, ends + ["lc0", "sexp"], ["b0"])
+    quant(T.qc[:], T.sc4[:], T.c4[:], ["c4"], ["qc"])
+    scan(T.b0s[:], T.rz[:, 0:B], T.b0[:], 0.0, A.mult, A.add, ["rz", "b0"], ["b0s"])
+    some(2)
+    ts(wu("lo", 0, 16), T.b0s[:, 15:B:16], 32.0, A.mult, 15.0, A.add, r=["b0s"], w=["loa"])
+    ts(wu("lo", 16, 32), T.b0s[:, 15:B:16], 32.0, A.mult, 31.0, A.add, r=["b0s"], w=["lob"])
+    tt(T.bt[:, 0:B], T.ws0[:].indirect(wu("lo", 0, 16)), T.srep[:], A.is_lt, ["ws0", "loa", "srep"], ["bta"])
+    tt(T.bt[:, B:2 * B], T.ws0[:].indirect(wu("lo", 16, 32)), T.srep[:], A.is_lt, ["ws0", "lob", "srep"], ["btb"])
+    ts(T.cp4o[:, 3:64:4], T.b0s[:, 15:B:16], 32.0, A.mult, cf(5), A.add, r=["b0s", "cf5"], w=["cp4o"])
+    quant(T.qb[:], T.sb[:], T.bt[:], ["bta", "btb", "btz"], ["qb"])
+    mm(0, 128, T.qc[:], T.sc4[:], T.qb[:, 0:128], T.sb[:, 0:128], True, False, ["qc", "qb"])
+    mm(0, 128, T.qc[:], T.sc4[:], T.qb[:, 64:192], T.sb[:, 64:192], False, True, ["qc", "qb"])
+    for b in (1, 2, 3):
+        unit(b, HB, b, T.qh[:, HB:B], T.sh[:, HB:B], False, ["qh"])
+
+    act(T.gn[:], T.knb[:].indirect(T.lin[:, 0:13]), F.Copy, ["knb", "lin"], ["gn"])
+    act(cf(20), T.gn[:, 0:1], F.Sign, ["gn", "sp"], ["xe0"], scale=-1.0, bias=T.sp[:, 1:2])
+    act(T.cf[:, 24:27], T.gn[:, NA - 3:NA], F.Sign, ["gn", "sp"], ["xe1"], scale=-1.0, bias=T.sp[:, C:C + 1])
+    act(T.gn[:, 0:1], cf(20), F.Identity, ["xe0"], ["gn0"], scale=H, bias=-2 * H)
+    act(T.gn[:, NA - 3:NA], T.cf[:, 24:27], F.Identity, ["xe1"], ["gn1"], scale=H, bias=2 * H)
+    own_plane(2)
+
+    tt(T.b1[:], T.gn[:, 8:200].indirect(T.lst[:, 40:56]), T.sexp[:], A.is_lt, ["gn", "lc1", "sexp"], ["b1"])
+    scan(T.n0[:], T.ps0[:, 0:64], T.cp4o[:], -1.0, A.max, A.add, ["ps0", "cp4o"], ["n0"])
+    scan(T.b1s[:], T.rz[:, 0:B], T.b1[:], 0.0, A.mult, A.add, ["rz", "b1"], ["b1s"])
+    ts(wu("lc", 0, 16), T.n0[:, 3:64:4], 1024.0, A.add, r=["n0"], w=["lca"])
+    ts(wu("lc", 16, 32), T.n0[:, 3:64:4], 1025.0, A.add, r=["n0"], w=["lcb"])
+    act(T.kl[:, 0:B], T.sp[:].indirect(wu("lc", 0, 16)), F.Copy, ends + ["lca"], ["kl"])
+    act(T.kl[:, B:2 * B], T.sp[:].indirect(wu("lc", 16, 32)), F.Copy, ends + ["lcb"], ["ku"])
+    for t in range(4):
+        act(T.tb[:, PL * t:PL * t + NA], T.dn[:, C * t:C * t + C].indirect(T.lin[:, 0:13]), F.Copy, ["dn%d" % t, "lin"], ["ds%d" % t])
+    own_plane(3)
+    bucket = T.b1s[:, 11:B:16]
+    ts(wu("l1", 0, 16), bucket, 16.0, A.mult, 15.0, A.add, r=["b1s"], w=["l1"])
+    scan(T.wa[:], T.ms[:, 0:NA], T.gn[:], 0.0, A.add, A.min, ["ms", "gn", "gn0", "gn1"], ["wa"])
+    ts(wf("own", 0, 16), T.n0[:, 3:64:4], 1024.0 + NA, A.add, r=["n0"], w=["owna"])
+    near = T.wa[:].indirect(wu("l1", 0, 16))
+    tt(T.bt1[:, B:2 * B], near, T.srep[:], A.is_lt, ["wa", "l1", "srep"], ["bt1b"])
+    ts(wf("pre", 0, 16), bucket, 16.0, A.mult, cf(13), A.add, r=["b1s", "cf13"], w=["pre0"])
+    tt(T.bt1[:, 0:B], near, T.kl[:, 0:B], A.is_lt, ["wa", "l1", "kl"], ["bt1a"])
+    tt(wf("pre", 16, 32), wf("pre", 0, 16), wf("own", 0, 16), A.subtract, ["pre0", "owna"], ["pre1"])
+    tt(T.bt1[:, 2 * B:3 * B], near, T.kl[:, B:2 * B], A.is_lt, ["wa", "l1", "ku"], ["bt1c"])
+    ts(T.cp4[:, 3:64:4], wf("pre", 16, 32), -2049.0, A.add, r=["pre1", "cp4"], w=["cp4a"])
+    quant(T.qb1[:], T.sb1[:], T.bt1[:], ["bt1a", "bt1b", "bt1c"], ["qb1"])
+    mm(0, 192, T.qc[:], T.sc4[:], T.qb1[:], T.sb1[:], True, True, ["qc", "qb1"])
+    ts(T.cp4[:, 67:128:4], wf("pre", 16, 32), -2049.0, A.add, r=["pre1", "cp4"], w=["cp4b"])
+    ts(T.cp4[:, 131:192:4], wf("pre", 16, 32), -2049.0, A.add, r=["pre1", "cp4"], w=["cp4c"])
+    ts(T.fd[:, 1:32:2], T.n0[:, 3:64:4], 1024.0 + NA, A.add, r=["n0"], w=["fdc"])
+    ts(T.fd[:, 33:64:2], T.n0[:, 3:64:4], 1025.0 + NA, A.add, r=["n0"], w=["fdd"])
+    tt(wf("pre", 32, 48), wf("own", 0, 16), bucket, A.subtract, ["owna", "b1s"], ["pre2"])
+    scan(T.n1[:], T.ps0[:, 0:192], T.cp4[:], -1.0, A.max, A.add, ["ps0", "cp4", "cp4a", "cp4b", "cp4c"], ["n1"])
+    unit(0, HB, 0, T.qh[:, HB:B], T.sh[:, HB:B], False, ["qh"])
+    tt(T.fl[:, 1:64:2], T.n1[:, 3:128:4], T.n1[:, 67:192:4], A.not_equal, ["n1", "flz"], ["fl"])
+    cpy(T.fd[:, 0:32:2], T.n1[:, 67:128:4], ["n1"], ["fda"])
+    cpy(T.fd[:, 32:64:2], T.n1[:, 67:128:4], ["n1"], ["fdb"])
+    tt(wf("br", 0, 16), T.n1[:, 67:128:4], wf("pre", 32, 48), A.add, ["n1", "pre2"], ["br0"])
+    scan(T.ix[:], T.fl[:], T.fd[:], 0.0, A.mult, A.add, ["fl", "fda", "fdb", "fdc", "fdd"], ["ix"])
+    ts(wf("br", 16, 32), wf("br", 0, 16), 2.0, A.mult, 1.0, A.max, r=["br0"], w=["br1"])
+    cpy(wu("li", 0, 32), T.ix[:, 1:64:2], ["ix"], ["li"])
+    ts(T.bout[:, 0:16], wf("br", 16, 32), C - 1.0, A.min, r=["br1"], w=["bo0"])
+    ts(T.bout[:, 16:32], wf("br", 16, 32), C - 1.0, A.min, 1.0, A.add, r=["br1"], w=["bo1"])
+    send(nxt, T.bin[:], T.bout[:], "ab", ["bo0", "bo1"])
+
+    def bank_of(h, b):
+        return 4 * (1 - h) + b
+
+    def half(name, h, k=1):
+        return T[name][:, k * HB * h:k * HB * (h + 1)]
+
+    def products(s, h):
+        quant(half("qz" + s, h), half("sz" + s, h), half("z" + s, h, 4), ["z%s%d%d" % (s, h, t) for t in range(4)], ["qz%s%d" % (s, h)])
+        for b in range(4):
+            mm(bank_of(h, b), HB, T.qw[:, 128 * b:128 * b + 128], T.sw[:, 128 * b:128 * b + 128], half("qz" + s, h), half("sz" + s, h),
+               False, True, ["qw", "sw", "qz%s%d" % (s, h)])
+
+    def results(s, h, on_vector):
+        for b in range(4):
+            bank, out = "ps%d" % bank_of(h, b), T["y" + s][:, 4 * HB * h + b:4 * HB * (h + 1):4]
+            if b in on_vector:
+                ts(out, T[bank][:, 0:HB], 0.03125, A.mult, r=[bank], w=["y%s%d%d" % (s, h, b)])
+            else:
+                act(out, T[bank][:, 0:HB], F.Copy, [bank], ["y%s%d%d" % (s, h, b)], scale=0.03125)
+
+    def pack(s, h):
+        quant(half("qy" + s, h), half("sy" + s, h), half("y" + s, h, 4), ["y%s%d%d" % (s, h, b) for b in range(4)], ["qy%s%d" % (s, h)])
+
+    def hand_on(h):
+        pack("1", h)
+        send(nxt, by(half("qa", h)), by(half("qy1", h)), "ay%d" % h, ["qy1%d" % h])
+        send(nxt, half("sa", h), half("sy1", h), "ay%d" % h, ["qy1%d" % h])
+
+    for h in range(2):
+        for t in range(4):
+            win, low, have = T.tb[:, PL * t:PL * t + PL], T.lb[:, B * t + HB * h:B * t + HB * h + HB], ["xs%d" % t, "ds%d" % t, "li"]
+            act(low, win.indirect(wu("li", 8 * h, 8 * h + 8)), F.Copy, have, ["lb%d%d" % (h, t)])
+            tt(T.z1[:, 4 * HB * h + t:4 * HB * (h + 1):4], win.indirect(wu("li", 16 + 8 * h, 24 + 8 * h)), low, A.add,
+               have + ["lb%d%d" % (h, t)], ["z1%d%d" % (h, t)])
+            if h and t == 0:
+                products("1", 0)
+    results("1", 0, ())
+    products("1", 1)
+    hand_on(0)
+    results("1", 1, (1, 3))
+    hand_on(1)
+
+    for k in range(2):
+        act(T.th[:, B * k:B * k + B], T.sp[:].indirect(T.bin[:, 16 * k:16 * k + 16]), F.Copy, ends + ["bin"], ["th%d" % k])
+    for t in range(4):
+        means(t)
+    ts(T.cp2[:, 15:B:16], T.bin[:, 0:16], cf(7), A.add, -1.0, A.add, r=["bin", "cf7"], w=["cp2"])
+    quant(T.qv[:], T.sv[:], T.vt[:], ["vt"], ["qv"])
+
+    def scores(h, bank):
+        mm(bank, HB, T.qr[:], T.sr[:], half("qa", h), half("sa", h), True, True, ["qr", "sr", "qa%d" % h])
+
+    def units(h, bs):
+        for b in bs:
+            unit(bank_of(h, b), HB, b, half("qa", h), half("sa", h), False, ["qa%d" % h])
+
+    def stage(h, k, bank=None):
+        a, z = HB * h, HB * (h + 1)
+        if k == 0:
+            tt(T.tq[:, a:z], T["ps%d" % bank][:, 0:HB], T.th[:, a:z], A.is_ge, ["ps%d" % bank, "th0"], ["tql%d" % h])
+            tt(T.tq[:, B + a:B + z], T["ps%d" % bank][:, 0:HB], T.th[:, B + a:B + z], A.is_gt, ["ps%d" % bank, "th1"], ["tqu%d" % h])
+        if k == 1:
+            tt(T.tq[:, 2 * B + a:2 * B + z], T.tq[:, a:z], T.tq[:, B + a:B + z], A.add, ["tql%d" % h, "tqu%d" % h], ["tq%d" % h])
+        if k == 2:
+            scan(T.p3s[:, a:z], T.tq[:, 2 * B + a:2 * B + z], T.cp2[:, a:z], -1.0, A.max, A.add, ["tq%d" % h, "cp2"], ["p3s%d" % h])
+        if k == 3:
+            ts(wu("lp", 8 * h, 8 * h + 8), T.p3s[:, a + 15:z:16], 2048.0, A.add, r=["p3s%d" % h], w=["lp%d" % h])
+
+    def picks(h, on_vector):
+        for t in range(4):
+            out, win = T.z2[:, 4 * HB * h + t:4 * HB * (h + 1):4], T.zt[:, 400 * t:400 * t + C + 1].indirect(wu("lp", 8 * h, 8 * h + 8))
+            if t in on_vector:
+                cpy(out, win, ["zt%d" % t, "lp%d" % h], ["z2%d%d" % (h, t)])
+            else:
+                act(out, win, F.Copy, ["zt%d" % t, "lp%d" % h], ["z2%d%d" % (h, t)])
+
+    def last(h):
+        pack("2", h)
+        mm(4 + h, HB, T.qv[:], T.sv[:], half("qy2", h), half("sy2", h), True, True, ["qv", "qy2%d" % h])
+        dma("Y", T.oc[:, 4 * HB * h:4 * HB * (h + 1)], by(half("qy2", h)), "so1", r=["qy2%d" % h])
+
+    def store(h):
+        dma("Y", T.y[:, HB * h:HB * (h + 1)], half("yo", h), "so1", r=["yo%d" % h])
+
+    scores(0, 3)
+    units(0, range(4))
+    for k in range(4):
+        stage(0, k, 3)
+    scores(1, 2)
+    units(1, (0, 1, 3))
+    picks(0, (1, 3))
+    stage(1, 0, 2)
+    units(1, (2,))
+    products("2", 0)
+    for k in range(1, 4):
+        stage(1, k)
+    results("2", 0, ())
+    picks(1, (0, 1, 3))
+    products("2", 1)
+    last(0)
+    act(T.pv[:], T.jj[:].indirect(wu("lp", 0, 16)), F.Copy, ["jj", "lp0", "lp1"], ["pv"])
+    dma("Y", T.ov[:], T.pv[0:128:16, :], "so1", r=["pv"])
+    results("2", 1, (1, 3))
+    act(half("yo", 0), T.ps4[:, 0:HB], F.Copy, ["ps4"], ["yo0"])
+    store(0)
+    last(1)
+    cpy(half("yo", 1), T.ps5[:, 0:HB], ["ps5"], ["yo1"])
+    store(1)
+    for k in range(4):
+        dma("S", T.osc[4 * k:4 * k + 4, :], T.sy2[32 * k:32 * k + 4, :], "so2", r=["qy20", "qy21"])
+
+    for e in cnt:
+        g.wait_ge(T.sem["e" + e], cnt[e])
+    for sem in ("left", "so1", "so2"):
+        g.wait_ge(T.sem[sem], dcnt[sem])

@@ -4,15 +4,19 @@ C, B = 384, 256
 HB = B // 2
 NS = C // 2
 H = 2.0 ** 80
-PL = 608
 NA = 208
+PL = NA + 400
+K = 1024.0
+OFF = 2048.0
 f32, bf, u16, i32, cod, u8 = "float32", "bfloat16", "uint16", "int32", "float8_e4m3fn_x4", "uint8"
 
-TILES = [(0, 384, [None, 23, 22, 21]), (1280, 128, [4, 3, 2, 1]), (384, 320, [20, 19, 18, 17]),
-         (704, 256, [16, 15, 14, 13]), (960, 192, [12, 11, 10, 9]), (1152, 128, [8, 7, 6, 5])]
-ON_SCALAR = (23, 22, 21)
-WF = {"own": 0, "pre": 32, "br": 80, "cb": 112, "rt": 136, "rowl": 160, "tla": 184}
-WU = {"lpos": 0, "lo": 24, "lc": 56, "l1": 88, "li": 104, "lp": 136, "lm": 152}
+TILES = [(0, 384, [None, 23, 22, 21]), (384, 320, [20, 19, 18, 17]), (704, 256, [16, 15, 14, 13]),
+         (960, 192, [12, 11, 10, 9]), (1152, 128, [5, 6, 7, 8]), (1280, 128, [1, 2, 3, 4])]
+OPT = {"low": (), "p0": (1, 3), "p1": (0, 1, 3), "r11": (1, 3), "r21": (1, 3), "scalar": (23, 22, 21, 20), "short": True, "pl": 3,
+       "gaps": "11010001000111"}
+HI = 256
+WF = {"pre": 0, "br": 48, "cb": 80, "rt": 104, "rowl": 128, "tla": 152, "spl": 184, "spa": 208}
+WU = {"lpos": 0, "lo": 24, "lc": 56, "l1": 88, "li": 104, "lp": 136, "bl": 152, "lm": 184}
 
 
 def _s(n, d):
@@ -24,23 +28,24 @@ SCRATCH = {
     "qx": _s(C, cod), "sx": _s(C, u8), "qxn": _s(C, cod), "sxn": _s(C, u8),
     "qh": _s(B, cod), "sh": _s(B, u8), "qu": _s(128, cod), "su": _s(128, u8), "qr": _s(128, cod), "sr": _s(128, u8),
     "qv": _s(128, cod), "sv": _s(128, u8), "qw": _s(512, cod), "sw": _s(512, u8),
-    "one": _s(512, bf), "t32": _s(516, bf), "g1a": _s(512, bf), "g1": _s(512, bf), "c4": _s(512, bf), "et": _s(1040, bf),
+    "t32": _s(516, bf), "g1a": _s(512, bf), "g1": _s(512, bf), "c4": _s(512, bf), "et": _s(1040, bf),
     "qg": _s(128, cod), "sg": _s(128, u8), "qc": _s(128, cod), "sc4": _s(128, u8), "qe": _s(512, cod), "se": _s(512, u8),
-    "ci": _s(8, i32), "cf": _s(32, f32), "ic": _s(32, f32), "jm": _s(400, f32), "jm4": _s(192, f32), "jj": _s(400, f32),
-    "m0": _s(C, f32), "rz": _s(C, f32), "rs": _s(C, f32), "ms": _s(C, f32), "tmpa": _s(400, f32), "tmpb": _s(400, f32),
-    "cp": _s(400, f32), "cp4": _s(192, f32), "cp4o": _s(64, f32), "wf": _s(216, f32), "wu": _s(284, u16), "lst": _s(72, u16),
+    "ci": _s(8, i32), "cf": _s(40, f32), "ic": _s(32, f32), "jm": _s(400, f32), "jm4": _s(192, f32), "jj": _s(400, f32),
+    "m0": _s(C, f32), "rz": _s(C, bf), "rs": _s(C, f32), "ms": _s(C, f32),
+    "cp": _s(400, f32), "cq": _s(400, f32), "cp4": _s(192, f32), "cp4o": _s(128, f32), "cp2": _s(B, f32),
+    "wf": _s(224, f32), "wu": _s(316, u16), "lst": _s(72, u16),
     "fl": _s(64, f32), "fd": _s(64, f32), "ix": _s(64, f32),
     "km": _s(C, f32), "kc": _s(C, f32), "ksb": _s(C, f32), "knb": _s(C, f32), "srep": _s(B, f32),
-    "ts": _s(4 * 1408, bf), "qs": _s(1408, cod), "ss": _s(1408, u8), "junk": _s(4416, bf), "rk": _s(C, f32),
-    "mt": _s(400, f32), "lout": _s(16, u16), "lin": _s(16, u16), "sp": _s(400, f32), "sexp": _s(B, f32),
-    "dn": _s(4 * C, bf), "tb": _s(4 * PL, bf), "ws0": _s(C, f32), "b0": _s(B, f32), "b0s": _s(B, f32),
-    "bt": _s(768, bf), "qb": _s(192, cod), "sb": _s(192, u8), "n0": _s(64, f32),
-    "kl": _s(2 * B, f32), "gn": _s(NA, f32), "mw": _s(400, f32), "wa": _s(NA, f32), "b1": _s(B, f32), "b1s": _s(B, f32),
+    "ts": _s(4 * 1408, bf), "qs": _s(1408, cod), "ss": _s(1408, u8), "junk": _s(4416, bf), "dj": _s(C, bf), "sj": _s(768, bf),
+    "rk": _s(C, f32), "mt": _s(400, f32), "sa1": _s(NA, f32), "sa2": _s(NA, f32), "lout": _s(16, u16), "lin": _s(16, u16), "sp": _s(400, f32),
+    "dn": _s(4 * C, bf), "tb": _s(4 * PL, bf), "ws0": _s(C, f32),
+    "bt": _s(768, bf), "qb": _s(192, cod), "sb": _s(192, u8), "nb": _s(64, f32),
+    "bt2": _s(512, bf), "qb2": _s(128, cod), "sb2": _s(128, u8), "n0": _s(128, f32),
+    "kl": _s(2 * B, f32), "gn": _s(NA, f32), "mw": _s(400, f32), "wa": _s(NA, f32),
     "bt1": _s(768, bf), "qb1": _s(192, cod), "sb1": _s(192, u8), "n1": _s(192, f32), "lb": _s(4 * B, bf),
     "z1": _s(4 * B, bf), "qz1": _s(B, cod), "sz1": _s(B, u8), "y1": _s(4 * B, bf), "qy1": _s(B, cod), "sy1": _s(B, u8),
-    "bout": _s(32, u16), "bin": _s(32, u16), "qa": _s(B, cod), "sa": _s(B, u8),
-    "zt": _s(1600, bf), "th": _s(2 * B, f32), "tq": _s(3 * B, bf), "cp2": _s(B, f32), "p3s": _s(B, f32),
-    "sm": _s(B, f32), "ssc": _s(B, f32), "pv": _s(B, f32),
+    "bout": _s(16, u16), "bin": _s(16, u16), "qa": _s(B, cod), "sa": _s(B, u8),
+    "zt": _s(1600, bf), "th": _s(2 * B, f32), "tq": _s(3 * B, bf), "p3s": _s(B, f32), "pv": _s(B, f32),
     "z2": _s(4 * B, bf), "qz2": _s(B, cod), "sz2": _s(B, u8), "y2": _s(4 * B, bf), "qy2": _s(B, cod), "sy2": _s(B, u8), "yo": _s(B, f32),
 }
 for _b in range(8):
@@ -114,6 +119,9 @@ def rank_program(g, core, T, topo):
     def scan(out, d0, d1, init, o0, o1, r, w):
         op("V", lambda: V.tensor_tensor_scan(out, d0, d1, init, o0, o1), r, w)
 
+    def hold(out, data, row, r, w):
+        scan(out, data, row, -1.0, A.max, A.add, r, w)
+
     def cpy(out, in_, r, w):
         op("V", lambda: V.tensor_copy(out, in_), r, w)
 
@@ -128,6 +136,12 @@ def rank_program(g, core, T, topo):
             op("S", lambda: S.activation(out, in_, func, scale=scale, accum_out=acc), r, w)
         else:
             op("S", lambda: S.activation(out, in_, func, bias=bias, scale=scale, accum_out=acc), r, w)
+
+    def move(on_vector, out, in_, r, w):
+        if on_vector:
+            cpy(out, in_, r, w)
+        else:
+            act(out, in_, F.Copy, r, w)
 
     def mm(bank, m, lq, ls, rq, rs_, start, stop, r):
         op("P", lambda: P.matmul_mx(T["ps%d" % bank][:, 0:m], lq, ls, rq, rs_, start, stop), r, ["ps%d" % bank])
@@ -147,6 +161,17 @@ def rank_program(g, core, T, topo):
     def unit(bank, m, b, q, s, stop, r):
         mm(bank, m, T.qe[:, 128 * b:128 * b + 128], T.se[:, 128 * b:128 * b + 128], q, s, True, stop, ["qe%d" % b] + r)
 
+    def keys(bank, m, q, s, r):
+        mm(bank, m, T.qr[:], T.sr[:], q, s, True, True, ["qr", "sr"] + r)
+
+    spare = []
+
+    def gap(k=4):
+        while spare and k > 0:
+            length, call = spare.pop(0)
+            call()
+            k -= length
+
     en, ep = len(topo.engines(nxt, core)), len(topo.engines(prv, core))
     wrote["qxn"], wrote["lin"], wrote["bin"] = ("ax", 2 * en), ("al", en), ("ab", ep)
     wrote["qa0"], wrote["qa1"] = ("ay0", 2 * ep), ("ay1", 2 * ep)
@@ -164,265 +189,310 @@ def rank_program(g, core, T, topo):
     def select(out, in_, pat, cmp_, base, cm, r, w):
         op("G", lambda: g.affine_select(out, in_, pat, cmp_, 0.0, base, cm), r, w)
 
-    def holding(outs, j, m, col, r, between):
-        act(T.tmpa[:, 0:m], j, F.Relu, r, ["tmpa"], scale=-2048.0, bias=col)
-        between[0]()
-        act(T.tmpb[:, 0:m], T.tmpa[:, 0:m], F.Square, ["tmpa"], ["tmpb"], scale=1.0 / 32, bias=-48.0)
-        between[1]()
-        for out, k, w in outs:
-            act(out, T.tmpb[:, 0:k], F.Identity, ["tmpb"], w, scale=-1.0, bias=2304.0)
-
     def unit_codes(b):
         o = 520 * (b % 2) + 2 - 2 * (b // 2)
         quant(T.qe[:, 128 * b:128 * b + 128], T.se[:, 128 * b:128 * b + 128], T.et[:, o:o + 512], ["et%d" % (b % 2)], ["qe%d" % b])
 
+    def pad(k):
+        lo, wd, blocks = TILES[k]
+        fill(T.ts[:, 4 * (lo + 16 * min(c for c in blocks if c)):4 * (lo + wd)], 0.0, ["tz%d" % lo])
+
     iota(T.ci[:, 0:1], [[0, 1]], 1, ["ci0"], False)
     iota(T.ic[:], [[1, 32]], 0, ["ic"])
     iota(T.jm[:], [[0, 25], [1, 16]], 0, ["jm"])
-    fill(T.t32[:], 32.0, ["t32"])
+    iota(T.g1a[:], [[1, 8], [0, 64]], 0, ["g1a"])
+    for k in range(3):
+        pad(k)
     ts(T.ci[:, 1:2], T.ci[:, 0:1], 15, A.bitwise_and, r=["ci0"], w=["ci1"])
+    ts(T.ci[:, 2:3], T.ci[:, 0:1], 15, A.bitwise_and, 2, A.logical_shift_right, r=["ci0"], w=["ci2"])
+    ts(T.ci[:, 3:4], T.ci[:, 0:1], 4, A.logical_shift_right, r=["ci0"], w=["ci3"])
     ts(T.lst[:, 0:8], T.ic[:, 0:8], 16.0, A.mult, r=["ic"], w=["lu"])
-    cpy(cf(0), T.ci[:, 1:2], ["ci1"], ["cf0"])
-    ts(T.ci[:, 2:3], T.ci[:, 1:2], 2, A.logical_shift_right, r=["ci1"], w=["ci2"])
-    fill(T.one[:], 1.0, ["one"])
-    cpy(cf(4), T.ci[:, 2:3], ["ci2"], ["cf4"])
-    for k in range(2):
-        select(T.et[:, 520 * k:520 * k + 516], T.t32[:], [[-1, 516]], A.is_equal, 2 + k, 4, ["t32"], ["et%d" % k])
-    select(T.g1a[:], T.one[:], [[-16, 8], [0, 64]], A.is_ge, 0, 1, ["one"], ["g1a"])
-    act(cf(16), cf(0), F.Identity, ["cf0"], ["cf16"], scale=-2 * H)
-    act(cf(17), cf(0), F.Identity, ["cf0"], ["cf17"], scale=4 * H, bias=4 * H)
-    act(cf(18), cf(0), F.Identity, ["cf0"], ["cf18"], scale=2048.0, bias=2048.0)
-    act(cf(19), cf(4), F.Identity, ["cf4"], ["cf19"], scale=2048.0, bias=2048.0)
+    pad(5)
+    cpy(T.cf[:, 1:4], T.ci[:, 1:4], ["ci1", "ci2", "ci3"], ["r"])
+    fill(T.t32[:], 32.0, ["t32"])
+    select(T.et[:, 0:516], T.t32[:], [[-1, 516]], A.is_equal, 2, 4, ["t32"], ["et0"])
+    act(cf(16), cf(1), F.Identity, ["r"], ["cf16"], scale=-2 * H)
+    act(cf(21), cf(1), F.Square, ["r"], ["cf21"], bias=-15.0)
+    act(cf(22), cf(2), F.Square, ["r"], ["cf22"], bias=-3.0)
+    act(cf(18), cf(1), F.Identity, ["r"], ["cf18"], scale=-K, bias=K / 2)
+    act(cf(17), cf(1), F.Identity, ["r"], ["cf17"], scale=4 * H, bias=4 * H)
+    act(T.rs[:], T.jm[:, 0:C], F.Relu, ["jm"], ["rs"], scale=-4 * H, bias=4 * H)
+    act(cf(7), cf(21), F.Identity, ["cf21"], ["cf7"], scale=-K / 2, bias=-OFF)
+    act(cf(5), cf(22), F.Identity, ["cf22"], ["cf5"], scale=-K / 2, bias=-OFF)
+    act(T.m0[:], T.jm[:, 0:C], F.Abs, ["jm", "cf16"], ["m0"], scale=2 * H, bias=cf(16))
+    act(cf(8), cf(1), F.Identity, ["r", "cf7"], ["cf8"], scale=-1.0, bias=cf(7))
     act(T.rz[:], T.jm[:, 0:C], F.Sign, ["jm"], ["rz"])
-    holding([(T.cp[:], 400, ["cp", "cp15"]), (T.cp2[:], B, ["cp2"])], T.jm[:], 400, cf(18), ["jm", "cf18"],
-            [lambda: act(T.m0[:], T.jm[:, 0:C], F.Abs, ["jm", "cf16"], ["m0"], scale=2 * H, bias=cf(16)),
-             lambda: act(T.rs[:], T.rz[:], F.Identity, ["rz"], ["rs"], scale=-4 * H, bias=4 * H)])
-    for lo, wd, blocks in TILES:
-        fill(T.ts[:, 4 * (lo + 16 * blocks[3]):4 * (lo + wd)], 0.0, ["tz%d" % lo])
-    ts(cf(6), cf(0), 15.0, A.is_equal, 2048.0, A.mult, r=["cf0"], w=["cf6"])
-    ts(cf(9), cf(0), 11.0, A.is_ge, 1000.0, A.mult, r=["cf0"], w=["cf9"])
-    ts(cf(12), cf(0), 16.0, A.mult, 7.0, A.add, r=["cf0"], w=["cf12"])
-    ts(wf("tla", 0, 13), T.ic[:, 0:13], 15.0, A.mult, cf(0), A.add, r=["ic", "cf0"], w=["tla0"])
-    ts(cf(7), cf(6), -4096.0, A.add, r=["cf6"], w=["cf7"])
-    ts(cf(8), cf(6), cf(0), A.subtract, -4080.0, A.add, r=["cf6", "cf0"], w=["cf8"])
+    act(wf("cb", 0, 24), T.ic[:, 1:25], F.Identity, ["ic", "cf8"], ["cb"], scale=16.0, bias=cf(8))
+    act(T.cp[:], T.jm[:], F.Identity, ["jm", "cf18"], ["cp"], scale=K, bias=cf(18))
+    act(T.cq[:], T.jm[:], F.Identity, ["jm", "cf18"], ["cq"], scale=K, bias=cf(18))
+    act(T.ms[:], T.jm[:, 0:C], F.Relu, ["jm", "cf17"], ["ms"], scale=-4 * H, bias=cf(17))
+    act(T.cq[:, 15:400:16], T.ic[:, 0:25], F.Identity, ["ic", "cf7"], ["cq"], scale=0.0, bias=cf(7))
+    pad(3)
+    pad(4)
     quant(T.qu[:], T.su[:], T.ut[:], ["ut"], ["qu"])
-    ts(cf(11), cf(0), 32.0, A.mult, cf(9), A.add, r=["cf0", "cf9"], w=["cf11"])
+    ts(wf("tla", 0, 13), T.ic[:, 0:13], 15.0, A.mult, cf(1), A.add, r=["ic", "r"], w=["tla0"])
+    ts(cf(9), cf(1), 7.0, A.is_lt, r=["r"], w=["cf9"])
+    ts(cf(10), cf(1), 12.0, A.is_lt, r=["r"], w=["cf10"])
     cpy(T.qr[:].bitcast(dt.uint32), T.qu[:].bitcast(dt.uint32).indirect(T.lst[:, 0:8]), ["qu", "lu"], ["qr"])
     cpy(T.sr[:], T.su[:].indirect(T.lst[:, 0:8]), ["qu", "lu"], ["sr"])
-    later = [
-        lambda: ts(cf(15), cf(12), NS - 9.0, A.min, r=["cf12"], w=["cf15"]),
-        lambda: ts(wf("tla", 16, 29), wf("tla", 0, 13), 1.0, A.max, float(NS), A.min, r=["tla0"], w=["tla1"]),
-        lambda: ts(cf(13), cf(4), 3.0, A.is_equal, 2048.0, A.mult, r=["cf4"], w=["cf13"]),
-        lambda: ts(T.lst[:, 8:24], T.ic[:, 0:16], 16.0, A.mult, 15.0, A.add, r=["ic"], w=["lx"]),
-        lambda: ts(cf(14), cf(11), 32.0, A.add, 385.0, A.min, r=["cf11"], w=["cf14"]),
-        lambda: fill(wf("rowl", 0, 1), 0.0, ["rowl0"]),
-        lambda: ts(wf("cb", 0, 24), T.ic[:, 0:24], 16.0, A.mult, cf(8), A.add, r=["ic", "cf8"], w=["cb"]),
-        lambda: fill(T.mt[:, 384:400], 0.0, ["mt"]),
-        lambda: ts(T.lst[:, 56:69], wf("tla", 16, 29), 2.0, A.mult, r=["tla1"], w=["la"]),
-        lambda: fill(T.lout[:], 0, ["lout"]),
-        lambda: ts(T.lst[:, 24:40], T.ic[:, 0:16], 0.0, A.mult, cf(14), A.add, r=["ic", "cf14"], w=["lc0"]),
-        lambda: ts(T.lst[:, 40:56], T.ic[:, 0:16], 0.0, A.mult, cf(15), A.add, r=["ic", "cf15"], w=["lc1"]),
-        lambda: ts(cf(5), cf(13), -3072.0, A.add, r=["cf13"], w=["cf5"]),
-        lambda: fill(T.fl[:], 0.0, ["flz"]),
-        lambda: fill(T.bt[:, 512:768], 0.0, ["btz"])]
-
-    def some(k):
-        for _ in range(k):
-            later.pop(0)()
-
-    unit_codes(0)
-    unit_codes(2)
-    some(3)
+    ts(wf("tla", 16, 29), wf("tla", 0, 13), 1.0, A.max, float(NS), A.min, r=["tla0"], w=["tla1"])
+    fill(T.mt[:, 384:400], 0.0, ["mta"])
+    ts(T.g1[:], T.g1a[:], cf(3), A.is_equal, r=["g1a", "r"], w=["g1"])
 
     quant(T.qx[:], T.sx[:], T.xt[:], ["xt"], ["qx"])
-    mm(0, C, T.qr[:], T.sr[:], T.qx[:], T.sx[:], True, True, ["qr", "sr", "qx"])
-    mm(2, C, T.qr[:], T.sr[:], T.qx[:], T.sx[:], True, True, ["qr", "sr", "qx"])
+    keys(0, C, T.qx[:], T.sx[:], ["qx"])
+    keys(2, C, T.qx[:], T.sx[:], ["qx"])
     send(prv, by(T.qxn[:]), by(T.qx[:]), "ax", ["qx"])
     send(prv, T.sxn[:], T.sx[:], "ax", ["qx"])
-    select(T.g1[:], T.g1a[:], [[16, 8], [0, 64]], A.is_ge, 15, -1, ["g1a"], ["g1"])
+    select(T.et[:, 520:1036], T.t32[:], [[-1, 516]], A.is_equal, 3, 4, ["t32"], ["et1"])
     iota(T.jj[:], [[1, 400]], 0, ["jj"])
     iota(T.jm4[:], [[0, 48], [1, 4]], 0, ["jm4"])
     select(T.c4[:], T.g1[:], [[0, 32], [1, 4], [-1, 4]], A.is_equal, 0, 0, ["g1"], ["c4"])
-    unit_codes(1)
-    unit_codes(3)
-    some(2)
-    act(T.ksb[:], T.ps2[:, 0:C], F.Copy, ["ps2"], ["ksb"])
+    quant(T.qg[:], T.sg[:], T.g1[:], ["g1"], ["qg"])
+    ts(T.lst[:, 56:69], wf("tla", 16, 29), 2.0, A.mult, r=["tla1"], w=["la"])
+    fill(wf("rowl", 0, 1), 0.0, ["rowl0"])
+    fill(T.mt[:, 0:1], 0.0, ["mtb"])
+    fill(T.lout[:], 0, ["lout"])
+    unit_codes(0)
 
-    tt(T.km[:], T.ps0[:, 0:C], T.m0[:], A.add, ["ps0", "m0"], ["km"])
-    some(1)
-    scan(T.kc[:], T.rs[:], T.km[:], 0.0, A.add, A.min, ["rs", "km"], ["kc"])
-    some(1)
-    at = [0]
+    def masked(a, z, name):
+        tt(T.km[:, a:z], T.ps0[:, a:z], T.m0[:, a:z], A.add, ["ps0", "m0"], ["km" + name])
+
+    def own_key(a, z, name):
+        scan(T.kc[:, a:z], T.rs[:, a:z], T.km[:, a:z], 0.0, A.add, A.min, ["rs", "km" + name], ["kc" + name])
+
+    at, closed = [0], [0]
 
     def close(k):
         lo, wd, blocks = TILES[k]
         quant(T.qs[:, lo:lo + wd], T.ss[:, lo:lo + wd], T.ts[:, 4 * lo:4 * (lo + wd)],
               ["tz%d" % lo] + ["t%d_%d" % (lo, t) for t in range(4)], ["qs%d" % lo])
-        if k:
+        if closed[0]:
             P.wait_ge(T.sem.eP, cnt["P"])
-        mm(1, wd, T.qg[:], T.sg[:], T.qs[:, lo:lo + wd], T.ss[:, lo:lo + wd], k == 0, k == len(TILES) - 1, ["qg", "qs%d" % lo])
+        closed[0] += 1
+        mm(1, wd, T.qg[:], T.sg[:], T.qs[:, lo:lo + wd], T.ss[:, lo:lo + wd], closed[0] == 1, closed[0] == len(TILES), ["qg", "qs%d" % lo])
 
     def block(k, t):
         lo, wd, blocks = TILES[k]
         c, name = blocks[t], "t%d_%d" % (lo, t)
         if c is None:
-            tt(T.ts[:, 0:4 * C:4], T.ps0[:, 0:C], T.kc[:], A.is_ge, ["ps0", "kc", "tz0"], [name])
+            tt(T.ts[:, 0:4 * C:4], T.ps0[:, 0:C], T.kc[:], A.is_ge, ["ps0", "kch", "kcl", "tz0"], [name])
             return None
         m = 16 * c
-        bits, key, spare = T.ts[:, 4 * lo + t:4 * (lo + m):4], T.kc[:, m + 15:m + 16], T.junk[:, at[0]:at[0] + m]
+        kc = "kch" if m >= HI else "kcl"
+        bits, key, spare_ = T.ts[:, 4 * lo + t:4 * (lo + m):4], T.kc[:, m + 15:m + 16], T.junk[:, at[0]:at[0] + m]
         at[0] += m
-        if c in ON_SCALAR:
-            act(spare, T.ksb[:, 0:m], F.Sign, ["ksb", "kc"], ["sg%d" % c], scale=-1.0, bias=key)
-            return lambda: act(bits, spare, F.Relu, ["sg%d" % c, "tz%d" % lo], [name, "rowl%d" % c], scale=-1.0, acc=wf("rowl", c, c + 1))
-        ts(bits, T.ps0[:, 0:m], key, A.is_gt, r=["ps0", "kc", "tz%d" % lo], w=[name])
-        act(spare, bits, F.Copy, [name], ["rowl%d" % c], acc=wf("rowl", c, c + 1))
+        if c in OPT["scalar"]:
+            act(spare_, T.ps2[:, 0:m], F.Sign, ["ps2", kc], ["sg%d" % c], scale=-1.0, bias=key)
+            return lambda: act(bits, spare_, F.Relu, ["sg%d" % c, "tz%d" % lo], [name, "rowl%d" % c], scale=-1.0, acc=wf("rowl", c, c + 1))
+        ts(bits, T.ps0[:, 0:m], key, A.is_gt, r=["ps0", kc, "tz%d" % lo], w=[name])
+        if c > 8 or not OPT["short"]:
+            act(spare_, bits, F.Copy, [name], ["rowl%d" % c], acc=wf("rowl", c, c + 1))
         return None
 
-    for second in [block(0, t) for t in (1, 2, 3)]:
-        second()
-    block(0, 0)
-    block(2, 0)
-    scan(T.tmpb[:, 0:C], T.rz[:], T.ts[:, 0:4 * C:4], 0.0, A.mult, A.add, ["rz", "t0_0"], ["tmpb"])
-    for t in range(1, 4):
-        block(2, t)
-    for t in range(4):
-        block(1, t)
-    quant(T.qg[:], T.sg[:], T.g1[:], ["g1"], ["qg"])
-    tt(wf("rt", 0, 24), wf("cb", 0, 24), T.tmpb[:, 15:C:16], A.subtract, ["cb", "tmpb"], ["rt"])
-    block(3, 0)
-    block(3, 1)
-    close(0)
-    dma("Y", by(T.qw[:]), T.wc[:], "dw", r=["qs0"], w=["qw"])
-    dma("Y", T.sw[:], T.ws[:], "dws", w=["sw"])
-    dma("Y", T.vt[:], T.v[:], "dv", w=["vt"])
-    close(2)
-    block(3, 2)
-    block(3, 3)
-    close(1)
-    for k in (4, 5):
-        for t in range(4):
+    def short_rows(t):
+        bits = T.ts[:, 4 * 1152 + t:4 * 1344:4]
+        scan(T.sj[:, t:768:4], bits, bits, 0.0, A.add, A.max, ["tz1152", "tz1280", "t1152_%d" % t, "t1280_%d" % t], ["sj%d" % t])
+
+    def blocks(k, ts_=range(4)):
+        for t in ts_:
             block(k, t)
-            if t == 1:
-                close(k - 1)
-    some(2)
+
+    masked(HI, C, "h")
+    masked(0, HI, "l")
+    own_key(HI, C, "h")
+    own_key(0, HI, "l")
+    mine = [(k, t) for k in (0, 1) for t in range(4) if TILES[k][2][t] in OPT["scalar"]]
+    for second in [block(k, t) for k, t in mine]:
+        second()
+    rest = [t for t in range(4) if (1, t) not in mine]
+    blocks(1, rest[:2])
+    block(0, 0)
+    blocks(1, rest[2:])
+    block(2, 0)
+    scan(T.dj[:], T.rz[:], T.ts[:, 0:4 * C:4], 0.0, A.mult, A.add, ["rz", "t0_0"], ["dj"])
+    blocks(2, (1, 2))
+    tt(wf("rt", 0, 24), wf("cb", 0, 24), T.dj[:, 15:C:16], A.subtract, ["cb", "dj"], ["rt"])
+    block(2, 3)
+    blocks(3, (0, 1))
+    close(0)
+    blocks(3, (2, 3))
+    close(2)
+    blocks(4, (3, 2))
+    close(1)
+    blocks(4, (1, 0))
+    close(3)
+    blocks(5, (3, 2, 1, 0))
+    close(4)
+    if OPT["short"]:
+        for t in range(4):
+            short_rows(t)
+    else:
+        unit_codes(2)
     close(5)
     quant(T.qh[:], T.sh[:], T.ht[:], ["ht"], ["qh"])
-    tt(T.cp[:, 15:C:16], wf("rt", 0, 24), wf("rowl", 0, 24), A.subtract, ["rt"] + ["rowl%d" % c for c in range(24)], ["cp15"])
-    some(1)
-    scan(T.rk[:], T.ps1[:, 0:C], T.cp[:, 0:C], -1.0, A.max, A.add, ["ps1", "cp", "cp15"], ["rk"])
-    ts(wu("lpos", 0, 24), T.rk[:, 15:C:16], 2048.0, A.add, r=["rk"], w=["lpos"])
-    some(1)
-    ts(T.cp[:, 15:400:16], T.ic[:, 0:25], 0.0, A.mult, cf(7), A.add, r=["ic", "cf7"], w=["cp15"])
-    cpy(T.mt[:].indirect(wu("lpos", 0, 24)), T.jj[:, 0:C], ["lpos", "jj"], ["mt"])
+    if OPT["short"]:
+        sj = ["sj%d" % t for t in range(4)]
+        cpy(wf("rowl", 5, 9), T.sj[:, 508:512], sj, ["rowl5"])
+        tt(wf("rowl", 1, 5), T.sj[:, 764:768], T.sj[:, 508:512], A.subtract, sj, ["rowl1"])
+        unit_codes(2)
+    tt(T.cp[:, 15:C:16], wf("rt", 0, 24), wf("rowl", 0, 24), A.subtract, ["rt", "cp"] + ["rowl%d" % c for c in range(24)], ["cp15"])
+    unit_codes(1)
+    hold(T.rk[:], T.ps1[:, 0:C], T.cp[:, 0:C], ["ps1", "cp", "cp15"], ["rk"])
+    unit_codes(3)
+    ts(wu("lpos", 0, 24), T.rk[:, 15:C:16], OFF, A.add, r=["rk"], w=["lpos"])
+    quant(T.qc[:], T.sc4[:], T.c4[:], ["c4"], ["qc"])
+    cpy(T.mt[:].indirect(wu("lpos", 0, 24)), T.jj[:, 0:C], ["lpos", "jj", "mta", "mtb"], ["mt"])
 
-    mm(2, C, T.qr[:], T.sr[:], T.qxn[:], T.sxn[:], True, True, ["qr", "sr", "qxn"])
-    mm(3, B, T.qr[:], T.sr[:], T.qh[:], T.sh[:], True, True, ["qr", "sr", "qh"])
-    act(T.knb[:], T.ps2[:, 0:C], F.Copy, ["ps2"], ["knb"])
-    act(T.ms[:], T.jm[:, 0:C], F.Relu, ["jm", "cf17"], ["ms"], scale=-4 * H, bias=cf(17))
-
-    def arrived_plane(b):
-        bank = (0, 2)[b % 2]
+    def arrived_plane(b, bank):
         unit(bank, C, b, T.qxn[:], T.sxn[:], True, ["qxn"])
-        act(T.dn[:, C * b:C * b + C], T["ps%d" % bank][:, 0:C], F.Copy, ["ps%d" % bank], ["dn%d" % b], scale=1.0 / 64)
+        return lambda: act(T.dn[:, C * b:C * b + C], T["ps%d" % bank][:, 0:C], F.Copy, ["ps%d" % bank], ["dn%d" % b], scale=1.0 / 64)
 
-    arrived_plane(0)
-    act(T.srep[:], T.ps3[:, 0:B], F.Copy, ["ps3"], ["srep"])
-    arrived_plane(1)
-    holding([(T.cp4o[:], 64, ["cp4o"]), (T.cp4[:], 192, ["cp4"])], T.jm4[:], 192, cf(19), ["jm4", "cf19"],
-            [lambda: arrived_plane(2), lambda: arrived_plane(3)])
+    act(cf(19), cf(2), F.Identity, ["r"], ["cf19"], scale=-K, bias=K / 2)
+    act(cf(12), cf(1), F.Identity, ["r"], ["cf12"], scale=-K, bias=-OFF)
+    act(cf(11), cf(5), F.Identity, ["cf5"], ["cf11"], bias=16 * OFF)
+    act(T.ksb[:], T.ps2[:, 0:C], F.Copy, ["ps2"], ["ksb"])
+    keys(5, C, T.qxn[:], T.sxn[:], ["qxn"])
+    keys(4, B, T.qh[:], T.sh[:], ["qh"])
+    keys(3, B, T.qh[:], T.sh[:], ["qh"])
+    planes = [arrived_plane(b, bank) for b, bank in zip((0, 2, 1, 3), (6, 7, 0, 2))]
+    act(T.cp4[:], T.jm4[:], F.Identity, ["jm4", "cf19"], ["cp4"], scale=K, bias=cf(19))
+    act(T.knb[:], T.ps5[:, 0:C], F.Copy, ["ps5"], ["knb"])
+    act(T.cp4[:, 3:192:4], T.jm4[:, 0:48], F.Identity, ["jm4", "cf5"], ["cp4"], scale=0.0, bias=cf(5))
+    act(T.srep[:], T.ps4[:, 0:B], F.Copy, ["ps4"], ["srep"])
+    act(T.cp4o[:], T.cp4[:, 0:128], F.Copy, ["cp4"], ["cp4o"])
+    for k in range(OPT["pl"]):
+        planes.pop(0)()
+
+    act(T.sa1[:], T.mt[:].indirect(T.lst[:, 56:69]), F.Copy, ["mt", "la"], ["sa1"])
+    planes.pop(0)()
     for b in range(4):
         unit(4 + b, HB, b, T.qh[:, 0:HB], T.sh[:, 0:HB], False, ["qh"])
-
-    cpy(T.mt[:, 0:386:385], T.mt[:, 1:385:383], ["mt"], ["mt"])
-    some(2)
-    scan(T.mw[:], T.mt[:], T.cp[:], -1.0, A.max, A.add, ["mt", "cp", "cp15"], ["mw"])
-    cpy(T.km[:, 0:NA], T.mt[:].indirect(T.lst[:, 56:69]), ["mt", "la"], ["km"])
-    ts(wu("lm", 0, 25), T.mw[:, 15:400:16], 2048.0, A.add, r=["mw"], w=["lm"])
+    unit(0, HB, 0, T.qh[:, HB:B], T.sh[:, HB:B], False, ["qh"])
+    fill(T.bt[:, 512:768], 0.0, ["btz"])
+    hold(T.mw[:], T.mt[:], T.cq[:], ["mt", "cq"], ["mw"])
+    hold(T.sa2[:], T.sa1[:], T.cq[:, 0:NA], ["sa1", "cq"], ["sa2"])
+    ts(wu("lm", 0, 25), T.mw[:, 15:400:16], OFF, A.add, r=["mw"], w=["lm"])
     act(T.sp[:], T.ksb[:].indirect(wu("lm", 0, 25)), F.Copy, ["ksb", "lm"], ["sp"])
-    act(T.sp[:, 0:1], cf(0), F.Identity, ["cf0", "sp"], ["spa"], scale=0.0, bias=-H)
-    act(T.sp[:, 385:386], cf(0), F.Identity, ["cf0", "sp"], ["spb"], scale=0.0, bias=3 * H)
-    scan(T.rk[:, 0:NA], T.km[:, 0:NA], T.cp[:, 0:NA], -1.0, A.max, A.add, ["km", "cp", "cp15"], ["rk"])
-    tt(T.sm[:], T.ps3[:, 0:B], T.m0[:, 0:B], A.add, ["ps3", "m0"], ["sm"])
-    ts(T.lout[:, 0:13], T.rk[:, 15:NA:16], 2048.0, A.add, r=["rk"], w=["lout"])
+    fill(T.fl[:], 0.0, ["flz"])
+    ts(T.lout[:, 0:13], T.sa2[:, 15:NA:16], OFF, A.add, r=["sa2"], w=["lout"])
+    ts(T.mw[:, 15:16], T.mt[:, 1:2], cf(12), A.add, T.mw[:, 15:16], A.max, r=["mt", "cf12", "lm"], w=["mwa"])
+    ts(T.mw[:, 399:400], T.mt[:, C:C + 1], -OFF, A.add, r=["mt", "lm"], w=["mwb"])
     send(prv, T.lin[:], T.lout[:], "al", ["lout"])
-    scan(T.ssc[:], T.rs[:, 0:B], T.sm[:], 0.0, A.add, A.min, ["rs", "sm"], ["ssc"])
-    act(T.sexp[:], T.ssc[:].indirect(T.lst[:, 8:24]), F.Copy, ["ssc", "lx"], ["sexp"])
+    dma("Y", by(T.qw[:]), T.wc[:], "dw", r=["lin"], w=["qw"])
+    dma("Y", T.sw[:], T.ws[:], "dws", w=["sw"])
+    dma("Y", T.vt[:], T.v[:], "dv", w=["vt"])
+    for copy_out in planes:
+        copy_out()
+    act(T.sp[:, 385:386], cf(1), F.Identity, ["r", "sp"], ["spb"], scale=0.0, bias=3 * H)
+    act(T.sp[:, 0:1], cf(1), F.Identity, ["r", "sp"], ["spa"], scale=0.0, bias=-H)
+    ends = ["sp", "spa", "spb"]
+
+    def plane_list(t):
+        ts(wu("lm", 26 * t + 26, 26 * t + 51), T.mw[:, 15:400:16], OFF + t / 4, A.add, 4.0, A.mult, r=["mwa", "mwb"], w=["lm%d" % t])
 
     def own_plane(t):
         act(T.tb[:, PL * t + NA:PL * t + PL], T.xt[:].indirect(wu("lm", 26 * t + 26, 26 * t + 51)), F.Copy, ["xt", "lm%d" % t], ["xs%d" % t], scale=0.5)
 
-    def means(t):
-        tt(T.zt[:, 400 * t:400 * t + C + 1], T.tb[:, PL * t + NA:PL * t + NA + C + 1], T.tb[:, PL * t + NA + 1:PL * t + NA + C + 2],
-           A.add, ["xs%d" % t], ["zt%d" % t])
+    def arrived_keys(between):
+        act(T.gn[:], T.knb[:].indirect(T.lin[:, 0:13]), F.Copy, ["knb", "lin"], ["gn"])
+        between[0]()
+        act(cf(20), T.gn[:, 0:1], F.Sign, ["gn", "sp"], ["xe0"], scale=-1.0, bias=T.sp[:, 1:2])
+        act(T.cf[:, 24:27], T.gn[:, NA - 3:NA], F.Sign, ["gn", "sp"], ["xe1"], scale=-1.0, bias=T.sp[:, C:C + 1])
+        between[1]()
+        act(T.gn[:, 0:1], cf(20), F.Identity, ["xe0"], ["gn0"], scale=H, bias=-2 * H)
+        act(T.gn[:, NA - 3:NA], T.cf[:, 24:27], F.Identity, ["xe1"], ["gn1"], scale=H, bias=2 * H)
 
-    scan(T.ws0[:], T.ms[:], T.sp[:, 1:C + 1], 0.0, A.add, A.min, ["ms", "sp"], ["ws0"])
-    for t in range(4):
-        ts(wu("lm", 26 * t + 26, 26 * t + 51), T.mw[:, 15:400:16], 2048.0 + t / 4, A.add, 4.0, A.mult, r=["mw"], w=["lm%d" % t])
+    def arrived_entries(t):
+        act(T.tb[:, PL * t:PL * t + NA], T.dn[:, C * t:C * t + C].indirect(T.lin[:, 0:13]), F.Copy, ["dn%d" % t, "lin"], ["ds%d" % t])
+
+    def means(t):
+        for k in range(3):
+            a, z, o = 129 * k, min(129 * k + 129, C + 1), PL * t + NA
+            spare.append((4, lambda a=a, z=z, o=o, k=k: tt(T.zt[:, 400 * t + a:400 * t + z], T.tb[:, o + a:o + z], T.tb[:, o + a + 1:o + z + 1],
+                                                         A.add, ["xs%d" % t], ["zt%d%d" % (t, k)])))
+
+    gaps = list(OPT["gaps"])
+
+    def pause():
+        gap(4 * int(gaps.pop(0)))
+
+    plane_list(0)
+    plane_list(1)
     own_plane(0)
     own_plane(1)
-    ends = ["sp", "spa", "spb"]
-    tt(T.b0[:], T.sp[:].indirect(T.lst[:, 24:40]), T.sexp[:], A.is_lt, ends + ["lc0", "sexp"], ["b0"])
-    quant(T.qc[:], T.sc4[:], T.c4[:], ["c4"], ["qc"])
-    scan(T.b0s[:], T.rz[:, 0:B], T.b0[:], 0.0, A.mult, A.add, ["rz", "b0"], ["b0s"])
-    some(2)
-    ts(wu("lo", 0, 16), T.b0s[:, 15:B:16], 32.0, A.mult, 15.0, A.add, r=["b0s"], w=["loa"])
-    ts(wu("lo", 16, 32), T.b0s[:, 15:B:16], 32.0, A.mult, 31.0, A.add, r=["b0s"], w=["lob"])
-    tt(T.bt[:, 0:B], T.ws0[:].indirect(wu("lo", 0, 16)), T.srep[:], A.is_lt, ["ws0", "loa", "srep"], ["bta"])
-    tt(T.bt[:, B:2 * B], T.ws0[:].indirect(wu("lo", 16, 32)), T.srep[:], A.is_lt, ["ws0", "lob", "srep"], ["btb"])
-    ts(T.cp4o[:, 3:64:4], T.b0s[:, 15:B:16], 32.0, A.mult, cf(5), A.add, r=["b0s", "cf5"], w=["cp4o"])
+    scan(wf("spl", 0, 24), T.ms[:, 0:24], T.sp[:, 16:400:16], 0.0, A.add, A.min, ["ms", "sp"], ["spl"])
+    scan(T.ws0[:, 0:NS], T.ms[:, 0:NS], T.sp[:, 1:NS + 1], 0.0, A.add, A.min, ["ms", "sp"], ["ws0a"])
+    ts(T.bt[:, 0:B], T.ps3[:, 0:B], wf("spl", 15, 16), A.is_gt, r=["ps3", "spl"], w=["bta"])
+    ts(T.bt[:, B:2 * B], T.ps3[:, 0:B], wf("spl", 23, 24), A.is_gt, cf(9), A.mult, r=["ps3", "spl", "cf9"], w=["btb"])
+    scan(T.ws0[:, NS:C], T.ms[:, 0:NS], T.sp[:, NS + 1:C + 1], 0.0, A.add, A.min, ["ms", "sp"], ["ws0b"])
     quant(T.qb[:], T.sb[:], T.bt[:], ["bta", "btb", "btz"], ["qb"])
-    mm(0, 128, T.qc[:], T.sc4[:], T.qb[:, 0:128], T.sb[:, 0:128], True, False, ["qc", "qb"])
-    mm(0, 128, T.qc[:], T.sc4[:], T.qb[:, 64:192], T.sb[:, 64:192], False, True, ["qc", "qb"])
-    for b in (1, 2, 3):
-        unit(b, HB, b, T.qh[:, HB:B], T.sh[:, HB:B], False, ["qh"])
+    mm(1, 128, T.qc[:], T.sc4[:], T.qb[:, 0:128], T.sb[:, 0:128], True, False, ["qc", "qb"])
+    mm(1, 128, T.qc[:], T.sc4[:], T.qb[:, 64:192], T.sb[:, 64:192], False, True, ["qc", "qb"])
+    plane_list(2)
+    plane_list(3)
+    arrived_keys([lambda: own_plane(2), lambda: arrived_entries(0)])
+    means(0)
+    pause()
+    hold(T.nb[:], T.ps1[:, 0:64], T.cp4[:, 0:64], ["ps1", "cp4"], ["nb"])
+    pause()
+    ts(wu("lo", 0, 16), T.nb[:, 3:64:4], OFF + 15 / 16, A.add, 16.0, A.mult, r=["nb"], w=["lo"])
+    ts(T.cp4o[:, 3:64:4], T.nb[:, 3:64:4], 16.0, A.mult, cf(11), A.add, r=["nb", "cf11", "cp4o"], w=["cp4q"])
+    scan(wf("spa", 0, 12), T.ms[:, 0:12], T.gn[:, 15:192:16], 0.0, A.add, A.min, ["ms", "gn"], ["spa1"])
+    pause()
+    means(1)
+    tt(T.bt2[:, 0:B], T.ws0[:].indirect(wu("lo", 0, 16)), T.srep[:], A.is_lt, ["ws0a", "ws0b", "lo", "srep"], ["bt2a"])
 
-    act(T.gn[:], T.knb[:].indirect(T.lin[:, 0:13]), F.Copy, ["knb", "lin"], ["gn"])
-    act(cf(20), T.gn[:, 0:1], F.Sign, ["gn", "sp"], ["xe0"], scale=-1.0, bias=T.sp[:, 1:2])
-    act(T.cf[:, 24:27], T.gn[:, NA - 3:NA], F.Sign, ["gn", "sp"], ["xe1"], scale=-1.0, bias=T.sp[:, C:C + 1])
-    act(T.gn[:, 0:1], cf(20), F.Identity, ["xe0"], ["gn0"], scale=H, bias=-2 * H)
-    act(T.gn[:, NA - 3:NA], T.cf[:, 24:27], F.Identity, ["xe1"], ["gn1"], scale=H, bias=2 * H)
-    own_plane(2)
-
-    tt(T.b1[:], T.gn[:, 8:200].indirect(T.lst[:, 40:56]), T.sexp[:], A.is_lt, ["gn", "lc1", "sexp"], ["b1"])
-    scan(T.n0[:], T.ps0[:, 0:64], T.cp4o[:], -1.0, A.max, A.add, ["ps0", "cp4o"], ["n0"])
-    scan(T.b1s[:], T.rz[:, 0:B], T.b1[:], 0.0, A.mult, A.add, ["rz", "b1"], ["b1s"])
-    ts(wu("lc", 0, 16), T.n0[:, 3:64:4], 1024.0, A.add, r=["n0"], w=["lca"])
-    ts(wu("lc", 16, 32), T.n0[:, 3:64:4], 1025.0, A.add, r=["n0"], w=["lcb"])
+    ts(T.bt2[:, B:2 * B], T.ps3[:, 0:B], wf("spa", 11, 12), A.is_gt, cf(10), A.mult, r=["ps3", "spa1", "cf10"], w=["bt2b"])
+    scan(T.wa[:], T.ms[:, 0:NA], T.gn[:], 0.0, A.add, A.min, ["ms", "gn", "gn0", "gn1"], ["wa"])
+    quant(T.qb2[:], T.sb2[:], T.bt2[:], ["bt2a", "bt2b"], ["qb2"])
+    mm(2, 128, T.qc[:], T.sc4[:], T.qb2[:], T.sb2[:], True, True, ["qc", "qb2"])
+    unit(3, HB, 3, T.qh[:, HB:B], T.sh[:, HB:B], False, ["qh"])
+    own_plane(3)
+    pause()
+    hold(T.n0[:], T.ps2[:, 0:128], T.cp4o[:], ["ps2", "cp4o", "cp4q"], ["n0"])
+    unit(2, HB, 2, T.qh[:, HB:B], T.sh[:, HB:B], False, ["qh"])
+    pause()
+    means(2)
+    own, bucket = T.n0[:, 3:64:4], T.n0[:, 67:128:4]
+    ts(wu("lc", 0, 16), own, OFF, A.add, r=["n0"], w=["lca"])
+    ts(wu("l1", 0, 16), bucket, OFF + 15 / 16, A.add, 16.0, A.mult, r=["n0"], w=["l1"])
+    ts(wu("lc", 16, 32), own, OFF + 1, A.add, r=["n0"], w=["lcb"])
+    ts(wf("pre", 0, 16), bucket, 16.0, A.mult, 16 * OFF - 1 - NA, A.add, r=["n0"], w=["pre0"])
     act(T.kl[:, 0:B], T.sp[:].indirect(wu("lc", 0, 16)), F.Copy, ends + ["lca"], ["kl"])
     act(T.kl[:, B:2 * B], T.sp[:].indirect(wu("lc", 16, 32)), F.Copy, ends + ["lcb"], ["ku"])
-    for t in range(4):
-        act(T.tb[:, PL * t:PL * t + NA], T.dn[:, C * t:C * t + C].indirect(T.lin[:, 0:13]), F.Copy, ["dn%d" % t, "lin"], ["ds%d" % t])
-    own_plane(3)
-    bucket = T.b1s[:, 11:B:16]
-    ts(wu("l1", 0, 16), bucket, 16.0, A.mult, 15.0, A.add, r=["b1s"], w=["l1"])
-    scan(T.wa[:], T.ms[:, 0:NA], T.gn[:], 0.0, A.add, A.min, ["ms", "gn", "gn0", "gn1"], ["wa"])
-    ts(wf("own", 0, 16), T.n0[:, 3:64:4], 1024.0 + NA, A.add, r=["n0"], w=["owna"])
+    act(T.fd[:, 1:32:2], own, F.Identity, ["n0"], ["fdc"], bias=OFF + NA)
+    act(T.fd[:, 33:64:2], own, F.Identity, ["n0"], ["fdd"], bias=OFF + NA + 1)
+    act(wf("pre", 32, 48), bucket, F.Identity, ["n0"], ["pre2"], scale=15.0, bias=16 * OFF - 1)
+    for t in (1, 2, 3):
+        arrived_entries(t)
+    act(T.cp2[:], T.jm[:, 0:B], F.Identity, ["jm", "cf18"], ["cp2"], scale=K, bias=cf(18))
     near = T.wa[:].indirect(wu("l1", 0, 16))
+    pause()
     tt(T.bt1[:, B:2 * B], near, T.srep[:], A.is_lt, ["wa", "l1", "srep"], ["bt1b"])
-    ts(wf("pre", 0, 16), bucket, 16.0, A.mult, cf(13), A.add, r=["b1s", "cf13"], w=["pre0"])
     tt(T.bt1[:, 0:B], near, T.kl[:, 0:B], A.is_lt, ["wa", "l1", "kl"], ["bt1a"])
-    tt(wf("pre", 16, 32), wf("pre", 0, 16), wf("own", 0, 16), A.subtract, ["pre0", "owna"], ["pre1"])
     tt(T.bt1[:, 2 * B:3 * B], near, T.kl[:, B:2 * B], A.is_lt, ["wa", "l1", "ku"], ["bt1c"])
-    ts(T.cp4[:, 3:64:4], wf("pre", 16, 32), -2049.0, A.add, r=["pre1", "cp4"], w=["cp4a"])
+    tt(wf("pre", 16, 32), wf("pre", 0, 16), own, A.subtract, ["pre0", "n0"], ["pre1"])
+    pause()
     quant(T.qb1[:], T.sb1[:], T.bt1[:], ["bt1a", "bt1b", "bt1c"], ["qb1"])
-    mm(0, 192, T.qc[:], T.sc4[:], T.qb1[:], T.sb1[:], True, True, ["qc", "qb1"])
-    ts(T.cp4[:, 67:128:4], wf("pre", 16, 32), -2049.0, A.add, r=["pre1", "cp4"], w=["cp4b"])
-    ts(T.cp4[:, 131:192:4], wf("pre", 16, 32), -2049.0, A.add, r=["pre1", "cp4"], w=["cp4c"])
-    ts(T.fd[:, 1:32:2], T.n0[:, 3:64:4], 1024.0 + NA, A.add, r=["n0"], w=["fdc"])
-    ts(T.fd[:, 33:64:2], T.n0[:, 3:64:4], 1025.0 + NA, A.add, r=["n0"], w=["fdd"])
-    tt(wf("pre", 32, 48), wf("own", 0, 16), bucket, A.subtract, ["owna", "b1s"], ["pre2"])
-    scan(T.n1[:], T.ps0[:, 0:192], T.cp4[:], -1.0, A.max, A.add, ["ps0", "cp4", "cp4a", "cp4b", "cp4c"], ["n1"])
-    unit(0, HB, 0, T.qh[:, HB:B], T.sh[:, HB:B], False, ["qh"])
+    mm(1, 192, T.qc[:], T.sc4[:], T.qb1[:], T.sb1[:], True, True, ["qc", "qb1"])
+    means(3)
+    pause()
+    hold(T.n1[:], T.ps1[:, 0:192], T.cp4[:], ["ps1", "cp4"], ["n1"])
+    unit(1, HB, 1, T.qh[:, HB:B], T.sh[:, HB:B], False, ["qh"])
+    pause()
+    below = T.n1[:, 67:128:4]
     tt(T.fl[:, 1:64:2], T.n1[:, 3:128:4], T.n1[:, 67:192:4], A.not_equal, ["n1", "flz"], ["fl"])
-    cpy(T.fd[:, 0:32:2], T.n1[:, 67:128:4], ["n1"], ["fda"])
-    cpy(T.fd[:, 32:64:2], T.n1[:, 67:128:4], ["n1"], ["fdb"])
-    tt(wf("br", 0, 16), T.n1[:, 67:128:4], wf("pre", 32, 48), A.add, ["n1", "pre2"], ["br0"])
+    tt(T.fd[:, 0:32:2], below, wf("pre", 16, 32), A.add, ["n1", "pre1"], ["fda"])
+    tt(T.fd[:, 32:64:2], below, wf("pre", 16, 32), A.add, ["n1", "pre1"], ["fdb"])
+    tt(wf("br", 0, 16), below, wf("pre", 32, 48), A.add, ["n1", "pre2"], ["br0"])
+    pause()
     scan(T.ix[:], T.fl[:], T.fd[:], 0.0, A.mult, A.add, ["fl", "fda", "fdb", "fdc", "fdd"], ["ix"])
-    ts(wf("br", 16, 32), wf("br", 0, 16), 2.0, A.mult, 1.0, A.max, r=["br0"], w=["br1"])
+    ts(T.bout[:], wf("br", 0, 16), 2.0, A.mult, 1.0, A.max, r=["br0"], w=["bout"])
+    pause()
     cpy(wu("li", 0, 32), T.ix[:, 1:64:2], ["ix"], ["li"])
-    ts(T.bout[:, 0:16], wf("br", 16, 32), C - 1.0, A.min, r=["br1"], w=["bo0"])
-    ts(T.bout[:, 16:32], wf("br", 16, 32), C - 1.0, A.min, 1.0, A.add, r=["br1"], w=["bo1"])
-    send(nxt, T.bin[:], T.bout[:], "ab", ["bo0", "bo1"])
+    send(nxt, T.bin[:], T.bout[:], "ab", ["bout"])
+    pause()
 
     def bank_of(h, b):
         return 4 * (1 - h) + b
@@ -452,29 +522,42 @@ def rank_program(g, core, T, topo):
         send(nxt, by(half("qa", h)), by(half("qy1", h)), "ay%d" % h, ["qy1%d" % h])
         send(nxt, half("sa", h), half("sy1", h), "ay%d" % h, ["qy1%d" % h])
 
+    def entries(h, t):
+        return T.tb[:, PL * t:PL * t + PL], T.lb[:, B * t + HB * h:B * t + HB * h + HB], ["xs%d" % t, "ds%d" % t, "li"]
+
+    def lower(h, t):
+        win, low, have = entries(h, t)
+        move((h, t) in OPT["low"], low, win.indirect(wu("li", 8 * h, 8 * h + 8)), have, ["lb%d%d" % (h, t)])
+
+    def upper(h, t):
+        win, low, have = entries(h, t)
+        tt(T.z1[:, 4 * HB * h + t:4 * HB * (h + 1):4], win.indirect(wu("li", 16 + 8 * h, 24 + 8 * h)), low, A.add,
+           have + ["lb%d%d" % (h, t)], ["z1%d%d" % (h, t)])
+
     for h in range(2):
         for t in range(4):
-            win, low, have = T.tb[:, PL * t:PL * t + PL], T.lb[:, B * t + HB * h:B * t + HB * h + HB], ["xs%d" % t, "ds%d" % t, "li"]
-            act(low, win.indirect(wu("li", 8 * h, 8 * h + 8)), F.Copy, have, ["lb%d%d" % (h, t)])
-            tt(T.z1[:, 4 * HB * h + t:4 * HB * (h + 1):4], win.indirect(wu("li", 16 + 8 * h, 24 + 8 * h)), low, A.add,
-               have + ["lb%d%d" % (h, t)], ["z1%d%d" % (h, t)])
-            if h and t == 0:
-                products("1", 0)
+            lower(h, t)
+    for t in sorted(range(4), key=lambda t: (0, t) in OPT["low"]):
+        upper(0, t)
+    upper(1, 0)
+    upper(1, 1)
+    products("1", 0)
+    upper(1, 2)
+    upper(1, 3)
     results("1", 0, ())
-    products("1", 1)
-    hand_on(0)
-    results("1", 1, (1, 3))
-    hand_on(1)
-
-    for k in range(2):
-        act(T.th[:, B * k:B * k + B], T.sp[:].indirect(T.bin[:, 16 * k:16 * k + 16]), F.Copy, ends + ["bin"], ["th%d" % k])
-    for t in range(4):
-        means(t)
-    ts(T.cp2[:, 15:B:16], T.bin[:, 0:16], cf(7), A.add, -1.0, A.add, r=["bin", "cf7"], w=["cp2"])
+    ts(wu("bl", 0, 16), T.bin[:], C - 1.0, A.min, r=["bin"], w=["bl0"])
+    ts(wu("bl", 16, 32), T.bin[:], C - 1.0, A.min, 1.0, A.add, r=["bin"], w=["bl1"])
     quant(T.qv[:], T.sv[:], T.vt[:], ["vt"], ["qv"])
-
-    def scores(h, bank):
-        mm(bank, HB, T.qr[:], T.sr[:], half("qa", h), half("sa", h), True, True, ["qr", "sr", "qa%d" % h])
+    products("1", 1)
+    ts(T.cp2[:, 15:B:16], wu("bl", 0, 16), cf(7), A.add, -1.0, A.add, r=["bl0", "cf7"], w=["cp2"])
+    pause()
+    hand_on(0)
+    results("1", 1, OPT["r11"])
+    for k in range(2):
+        act(T.th[:, B * k:B * k + B], T.sp[:].indirect(wu("bl", 16 * k, 16 * k + 16)), F.Copy, ends + ["bl%d" % k], ["th%d" % k])
+    pause()
+    hand_on(1)
+    gap(99)
 
     def units(h, bs):
         for b in bs:
@@ -488,17 +571,14 @@ def rank_program(g, core, T, topo):
         if k == 1:
             tt(T.tq[:, 2 * B + a:2 * B + z], T.tq[:, a:z], T.tq[:, B + a:B + z], A.add, ["tql%d" % h, "tqu%d" % h], ["tq%d" % h])
         if k == 2:
-            scan(T.p3s[:, a:z], T.tq[:, 2 * B + a:2 * B + z], T.cp2[:, a:z], -1.0, A.max, A.add, ["tq%d" % h, "cp2"], ["p3s%d" % h])
+            hold(T.p3s[:, a:z], T.tq[:, 2 * B + a:2 * B + z], T.cp2[:, a:z], ["tq%d" % h, "cp2"], ["p3s%d" % h])
         if k == 3:
-            ts(wu("lp", 8 * h, 8 * h + 8), T.p3s[:, a + 15:z:16], 2048.0, A.add, r=["p3s%d" % h], w=["lp%d" % h])
+            ts(wu("lp", 8 * h, 8 * h + 8), T.p3s[:, a + 15:z:16], OFF, A.add, r=["p3s%d" % h], w=["lp%d" % h])
 
-    def picks(h, on_vector):
-        for t in range(4):
-            out, win = T.z2[:, 4 * HB * h + t:4 * HB * (h + 1):4], T.zt[:, 400 * t:400 * t + C + 1].indirect(wu("lp", 8 * h, 8 * h + 8))
-            if t in on_vector:
-                cpy(out, win, ["zt%d" % t, "lp%d" % h], ["z2%d%d" % (h, t)])
-            else:
-                act(out, win, F.Copy, ["zt%d" % t, "lp%d" % h], ["z2%d%d" % (h, t)])
+    def picks(h, on_vector, which=range(4)):
+        for t in which:
+            move(t in on_vector, T.z2[:, 4 * HB * h + t:4 * HB * (h + 1):4], T.zt[:, 400 * t:400 * t + C + 1].indirect(wu("lp", 8 * h, 8 * h + 8)),
+                 ["zt%d%d" % (t, k) for k in range(3)] + ["lp%d" % h], ["z2%d%d" % (h, t)])
 
     def last(h):
         pack("2", h)
@@ -506,34 +586,37 @@ def rank_program(g, core, T, topo):
         dma("Y", T.oc[:, 4 * HB * h:4 * HB * (h + 1)], by(half("qy2", h)), "so1", r=["qy2%d" % h])
 
     def store(h):
+        act(half("yo", h), T["ps%d" % (4 + h)][:, 0:HB], F.Copy, ["ps%d" % (4 + h)], ["yo%d" % h])
         dma("Y", T.y[:, HB * h:HB * (h + 1)], half("yo", h), "so1", r=["yo%d" % h])
 
-    scores(0, 3)
+    keys(3, HB, half("qa", 0), half("sa", 0), ["qa0"])
     units(0, range(4))
-    for k in range(4):
+    for k in range(3):
         stage(0, k, 3)
-    scores(1, 2)
+    keys(2, HB, half("qa", 1), half("sa", 1), ["qa1"])
     units(1, (0, 1, 3))
-    picks(0, (1, 3))
     stage(1, 0, 2)
+    stage(0, 3)
     units(1, (2,))
+    stage(1, 1)
+    picks(0, OPT["p0"], (0, 2, 1))
+    stage(1, 2)
+    picks(0, OPT["p0"], (3,))
+    stage(1, 3)
     products("2", 0)
-    for k in range(1, 4):
-        stage(1, k)
+    picks(1, OPT["p1"])
     results("2", 0, ())
-    picks(1, (0, 1, 3))
     products("2", 1)
     last(0)
     act(T.pv[:], T.jj[:].indirect(wu("lp", 0, 16)), F.Copy, ["jj", "lp0", "lp1"], ["pv"])
     dma("Y", T.ov[:], T.pv[0:128:16, :], "so1", r=["pv"])
-    results("2", 1, (1, 3))
-    act(half("yo", 0), T.ps4[:, 0:HB], F.Copy, ["ps4"], ["yo0"])
+    results("2", 1, OPT["r21"])
     store(0)
     last(1)
-    cpy(half("yo", 1), T.ps5[:, 0:HB], ["ps5"], ["yo1"])
-    store(1)
     for k in range(4):
         dma("S", T.osc[4 * k:4 * k + 4, :], T.sy2[32 * k:32 * k + 4, :], "so2", r=["qy20", "qy21"])
+    cpy(half("yo", 1), T.ps5[:, 0:HB], ["ps5"], ["yo1"])
+    dma("Y", T.y[:, HB:B], half("yo", 1), "so1", r=["yo1"])
 
     for e in cnt:
         g.wait_ge(T.sem["e" + e], cnt[e])

@@ -5,17 +5,18 @@ HB = B // 2
 NS = C // 2
 H = 2.0 ** 80
 NA = 208
-PL = NA + 400
+PL = 400
+AR = 4 * PL
 K = 1024.0
 OFF = 2048.0
 f32, bf, u16, i32, cod, u8 = "float32", "bfloat16", "uint16", "int32", "float8_e4m3fn_x4", "uint8"
 
 TILES = [(0, 384, [None, 23, 22, 21]), (384, 320, [20, 19, 18, 17]), (704, 256, [16, 15, 14, 13]),
          (960, 192, [12, 11, 10, 9]), (1152, 128, [5, 6, 7, 8]), (1280, 128, [1, 2, 3, 4])]
-OPT = {"low": (), "p0": (1, 3), "p1": (0, 1, 3), "r11": (1, 3), "r21": (1, 3), "scalar": (23, 22, 21, 20), "short": True, "pl": 3,
-       "gaps": "11010001000111"}
-HI = 256
-WF = {"pre": 0, "br": 48, "cb": 80, "rt": 104, "rowl": 128, "tla": 152, "spl": 184, "spa": 208}
+OPT = {"low": ((0, 3),), "p0": (3,), "p1": (1, 3), "r11": (1, 3), "r20": (), "r21": (1, 3), "scalar": (23, 22, 21, 12, 11, 10),
+       "gaps": "010100200011", "dma": (0,), "s1": "ac", "s2": "2", "s3": "3bd"}
+LO = 208
+WF = {"pre": 0, "br": 48, "cb": 80, "rt": 104, "rowl": 128, "tla": 152, "tlb": 184}
 WU = {"lpos": 0, "lo": 24, "lc": 56, "l1": 88, "li": 104, "lp": 136, "bl": 152, "lm": 184}
 
 
@@ -32,26 +33,26 @@ SCRATCH = {
     "qg": _s(128, cod), "sg": _s(128, u8), "qc": _s(128, cod), "sc4": _s(128, u8), "qe": _s(512, cod), "se": _s(512, u8),
     "ci": _s(8, i32), "cf": _s(40, f32), "ic": _s(32, f32), "jm": _s(400, f32), "jm4": _s(192, f32), "jj": _s(400, f32),
     "m0": _s(C, f32), "rz": _s(C, bf), "rs": _s(C, f32), "ms": _s(C, f32),
-    "cp": _s(400, f32), "cq": _s(400, f32), "cp4": _s(192, f32), "cp4o": _s(128, f32), "cp2": _s(B, f32),
+    "cp": _s(400, f32), "cq": _s(400, f32), "cp4": _s(192, f32), "cp4o": _s(64, f32), "rz3": _s(C, bf),
     "wf": _s(224, f32), "wu": _s(316, u16), "lst": _s(72, u16),
     "fl": _s(64, f32), "fd": _s(64, f32), "ix": _s(64, f32),
-    "km": _s(C, f32), "kc": _s(C, f32), "ksb": _s(C, f32), "knb": _s(C, f32), "srep": _s(B, f32),
+    "km": _s(C, f32), "kc": _s(C, f32), "ksb": _s(C + 2, f32), "knb": _s(C, f32), "srep": _s(B, f32),
     "ts": _s(4 * 1408, bf), "qs": _s(1408, cod), "ss": _s(1408, u8), "junk": _s(4416, bf), "dj": _s(C, bf), "sj": _s(768, bf),
     "rk": _s(C, f32), "mt": _s(400, f32), "sa1": _s(NA, f32), "sa2": _s(NA, f32), "lout": _s(16, u16), "lin": _s(16, u16), "sp": _s(400, f32),
-    "dn": _s(4 * C, bf), "tb": _s(4 * PL, bf), "ws0": _s(C, f32),
-    "bt": _s(768, bf), "qb": _s(192, cod), "sb": _s(192, u8), "nb": _s(64, f32),
-    "bt2": _s(512, bf), "qb2": _s(128, cod), "sb2": _s(128, u8), "n0": _s(128, f32),
-    "kl": _s(2 * B, f32), "gn": _s(NA, f32), "mw": _s(400, f32), "wa": _s(NA, f32),
+    "dn": _s(4 * C, bf), "tb": _s(AR + 3 * PL + NA, bf), "ws0": _s(C, f32),
+    "sm": _s(B, f32), "ssc": _s(B, f32), "sexp": _s(B, f32), "b0": _s(B, bf), "b0s": _s(B, bf), "b1": _s(B, bf), "b1s": _s(B, bf),
+    "bt": _s(768, bf), "qb": _s(192, cod), "sb": _s(192, u8), "n0": _s(64, f32),
+    "kl": _s(B, f32), "gn": _s(NA, f32), "mw": _s(400, f32), "wa": _s(NA, f32),
     "bt1": _s(768, bf), "qb1": _s(192, cod), "sb1": _s(192, u8), "n1": _s(192, f32), "lb": _s(4 * B, bf),
     "z1": _s(4 * B, bf), "qz1": _s(B, cod), "sz1": _s(B, u8), "y1": _s(4 * B, bf), "qy1": _s(B, cod), "sy1": _s(B, u8),
     "bout": _s(16, u16), "bin": _s(16, u16), "qa": _s(B, cod), "sa": _s(B, u8),
-    "zt": _s(1600, bf), "th": _s(2 * B, f32), "tq": _s(3 * B, bf), "p3s": _s(B, f32), "pv": _s(B, f32),
+    "zt": _s(1600, bf), "th": _s(2 * B, f32), "tq": _s(3 * B, bf), "p3s": _s(3 * B, bf), "pv": _s(B, f32),
     "z2": _s(4 * B, bf), "qz2": _s(B, cod), "sz2": _s(B, u8), "y2": _s(4 * B, bf), "qy2": _s(B, cod), "sy2": _s(B, u8), "yo": _s(B, f32),
 }
 for _b in range(8):
     SCRATCH["ps%d" % _b] = ("psum", [128, 512], f32)
 
-SEMAPHORES = ["eV", "eS", "eP", "eG", "dx", "du", "dh", "dv", "dw", "dws", "ax", "al", "ab", "ay0", "ay1", "left", "so1", "so2"]
+SEMAPHORES = ["eV", "eS", "eP", "eG", "dx", "dx2", "du", "dh", "dv", "dw", "dws", "dm0", "dm1", "ax", "al", "ab", "ay0", "ay1", "left", "so1", "so2"]
 
 
 def rank_program(g, core, T, topo):
@@ -95,10 +96,10 @@ def rank_program(g, core, T, topo):
 
     dcnt = {}
 
-    def dma(e, out, in_, sem, r=(), w=()):
+    def dma(e, out, in_, sem, r=(), w=(), **how):
         need(e, r, w)
         dcnt[sem] = dcnt.get(sem, 0) + 16
-        Q[e].dma_start(out, in_).then_inc(T.sem[sem], 16)
+        Q[e].dma_start(out, in_, **how).then_inc(T.sem[sem], 16)
         note((sem, dcnt[sem]), r, w)
 
     def send(dst, out, in_, sem, r):
@@ -176,8 +177,9 @@ def rank_program(g, core, T, topo):
     wrote["qxn"], wrote["lin"], wrote["bin"] = ("ax", 2 * en), ("al", en), ("ab", ep)
     wrote["qa0"], wrote["qa1"] = ("ay0", 2 * ep), ("ay1", 2 * ep)
 
-    dma("Y", T.xt[:], T.x[:], "dx", w=["xt"])
     dma("S", T.ut[:], T.u[:], "du", w=["ut"])
+    dma("Y", T.xt[:, 0:4 * LO], T.x[:, 0:4 * LO], "dx", w=["xta"])
+    dma("Y", T.xt[:, 4 * LO:4 * C], T.x[:, 4 * LO:4 * C], "dx2", w=["xt"])
     dma("Y", T.ht[:], T.h[:], "dh", r=["xt"], w=["ht"])
 
     def iota(out, pat, cm, w, small=True):
@@ -229,34 +231,32 @@ def rank_program(g, core, T, topo):
     act(T.cq[:, 15:400:16], T.ic[:, 0:25], F.Identity, ["ic", "cf7"], ["cq"], scale=0.0, bias=cf(7))
     pad(3)
     pad(4)
+    fill(T.mt[:, 0:1], float(C), ["mtb"])
+    fill(T.ksb[:, C:C + 1], -H, ["ksa"])
+    fill(T.ksb[:, C + 1:C + 2], 3 * H, ["ksz"])
     quant(T.qu[:], T.su[:], T.ut[:], ["ut"], ["qu"])
     ts(wf("tla", 0, 13), T.ic[:, 0:13], 15.0, A.mult, cf(1), A.add, r=["ic", "r"], w=["tla0"])
-    ts(cf(9), cf(1), 7.0, A.is_lt, r=["r"], w=["cf9"])
-    ts(cf(10), cf(1), 12.0, A.is_lt, r=["r"], w=["cf10"])
+    ts(cf(9), cf(1), 11.0, A.is_ge, 1000.0, A.mult, r=["r"], w=["cf9"])
+    ts(cf(10), cf(1), 16.0, A.mult, 7.0, A.add, r=["r"], w=["cf10"])
     cpy(T.qr[:].bitcast(dt.uint32), T.qu[:].bitcast(dt.uint32).indirect(T.lst[:, 0:8]), ["qu", "lu"], ["qr"])
     cpy(T.sr[:], T.su[:].indirect(T.lst[:, 0:8]), ["qu", "lu"], ["sr"])
     ts(wf("tla", 16, 29), wf("tla", 0, 13), 1.0, A.max, float(NS), A.min, r=["tla0"], w=["tla1"])
-    fill(T.mt[:, 384:400], 0.0, ["mta"])
-    ts(T.g1[:], T.g1a[:], cf(3), A.is_equal, r=["g1a", "r"], w=["g1"])
+    ts(cf(13), cf(1), 32.0, A.mult, cf(9), A.add, r=["r", "cf9"], w=["cf13"])
+    fill(T.mt[:, 384:400], C + 1.0, ["mta"])
+    ts(T.lst[:, 8:24], T.ic[:, 0:16], 16.0, A.mult, 15.0, A.add, r=["ic"], w=["lx"])
 
-    quant(T.qx[:], T.sx[:], T.xt[:], ["xt"], ["qx"])
-    keys(0, C, T.qx[:], T.sx[:], ["qx"])
-    keys(2, C, T.qx[:], T.sx[:], ["qx"])
-    send(prv, by(T.qxn[:]), by(T.qx[:]), "ax", ["qx"])
-    send(prv, T.sxn[:], T.sx[:], "ax", ["qx"])
-    select(T.et[:, 520:1036], T.t32[:], [[-1, 516]], A.is_equal, 3, 4, ["t32"], ["et1"])
-    iota(T.jj[:], [[1, 400]], 0, ["jj"])
-    iota(T.jm4[:], [[0, 48], [1, 4]], 0, ["jm4"])
-    select(T.c4[:], T.g1[:], [[0, 32], [1, 4], [-1, 4]], A.is_equal, 0, 0, ["g1"], ["c4"])
-    quant(T.qg[:], T.sg[:], T.g1[:], ["g1"], ["qg"])
+    quant(T.qx[:, 0:LO], T.sx[:, 0:LO], T.xt[:, 0:4 * LO], ["xta"], ["qxa"])
+    keys(0, LO, T.qx[:, 0:LO], T.sx[:, 0:LO], ["qxa"])
+    keys(2, LO, T.qx[:, 0:LO], T.sx[:, 0:LO], ["qxa"])
+    ts(T.g1[:], T.g1a[:], cf(3), A.is_equal, r=["g1a", "r"], w=["g1"])
+    ts(wf("tlb", 0, 16), T.ic[:, 0:16], 0.0, A.mult, cf(13), A.add, r=["ic", "cf13"], w=["tlb"])
+    ts(wf("tlb", 16, 32), T.ic[:, 0:16], 0.0, A.mult, cf(10), A.add, r=["ic", "cf10"], w=["tlc"])
     ts(T.lst[:, 56:69], wf("tla", 16, 29), 2.0, A.mult, r=["tla1"], w=["la"])
     fill(wf("rowl", 0, 1), 0.0, ["rowl0"])
-    fill(T.mt[:, 0:1], 0.0, ["mtb"])
-    fill(T.lout[:], 0, ["lout"])
-    unit_codes(0)
+    quant(T.qg[:], T.sg[:], T.g1[:], ["g1"], ["qg"])
 
-    def masked(a, z, name):
-        tt(T.km[:, a:z], T.ps0[:, a:z], T.m0[:, a:z], A.add, ["ps0", "m0"], ["km" + name])
+    def masked(a, z, bank, name):
+        tt(T.km[:, a:z], T["ps%d" % bank][:, a:z], T.m0[:, a:z], A.add, ["ps%d" % bank, "m0"], ["km" + name])
 
     def own_key(a, z, name):
         scan(T.kc[:, a:z], T.rs[:, a:z], T.km[:, a:z], 0.0, A.add, A.min, ["rs", "km" + name], ["kc" + name])
@@ -266,27 +266,22 @@ def rank_program(g, core, T, topo):
     def close(k):
         lo, wd, blocks = TILES[k]
         quant(T.qs[:, lo:lo + wd], T.ss[:, lo:lo + wd], T.ts[:, 4 * lo:4 * (lo + wd)],
-              ["tz%d" % lo] + ["t%d_%d" % (lo, t) for t in range(4)], ["qs%d" % lo])
-        if closed[0]:
-            P.wait_ge(T.sem.eP, cnt["P"])
+              ["tz%d" % lo, "dga", "dgb"] + ["t%d_%d" % (lo, t) for t in range(4)], ["qs%d" % lo])
         closed[0] += 1
         mm(1, wd, T.qg[:], T.sg[:], T.qs[:, lo:lo + wd], T.ss[:, lo:lo + wd], closed[0] == 1, closed[0] == len(TILES), ["qg", "qs%d" % lo])
 
     def block(k, t):
         lo, wd, blocks = TILES[k]
         c, name = blocks[t], "t%d_%d" % (lo, t)
-        if c is None:
-            tt(T.ts[:, 0:4 * C:4], T.ps0[:, 0:C], T.kc[:], A.is_ge, ["ps0", "kch", "kcl", "tz0"], [name])
-            return None
         m = 16 * c
-        kc = "kch" if m >= HI else "kcl"
+        kc, mine, theirs = ("kca", "ps0", "ps2") if m < LO else ("kcb", "ps6", "ps7")
         bits, key, spare_ = T.ts[:, 4 * lo + t:4 * (lo + m):4], T.kc[:, m + 15:m + 16], T.junk[:, at[0]:at[0] + m]
         at[0] += m
         if c in OPT["scalar"]:
-            act(spare_, T.ps2[:, 0:m], F.Sign, ["ps2", kc], ["sg%d" % c], scale=-1.0, bias=key)
+            act(spare_, T[theirs][:, 0:m], F.Sign, [theirs, kc], ["sg%d" % c], scale=-1.0, bias=key)
             return lambda: act(bits, spare_, F.Relu, ["sg%d" % c, "tz%d" % lo], [name, "rowl%d" % c], scale=-1.0, acc=wf("rowl", c, c + 1))
-        ts(bits, T.ps0[:, 0:m], key, A.is_gt, r=["ps0", kc, "tz%d" % lo], w=[name])
-        if c > 8 or not OPT["short"]:
+        ts(bits, T[mine][:, 0:m], key, A.is_gt, r=[mine, kc, "tz%d" % lo], w=[name])
+        if c > 8:
             act(spare_, bits, F.Copy, [name], ["rowl%d" % c], acc=wf("rowl", c, c + 1))
         return None
 
@@ -298,101 +293,118 @@ def rank_program(g, core, T, topo):
         for t in ts_:
             block(k, t)
 
-    masked(HI, C, "h")
-    masked(0, HI, "l")
-    own_key(HI, C, "h")
-    own_key(0, HI, "l")
-    mine = [(k, t) for k in (0, 1) for t in range(4) if TILES[k][2][t] in OPT["scalar"]]
-    for second in [block(k, t) for k, t in mine]:
-        second()
-    rest = [t for t in range(4) if (1, t) not in mine]
-    blocks(1, rest[:2])
-    block(0, 0)
-    blocks(1, rest[2:])
-    block(2, 0)
-    scan(T.dj[:], T.rz[:], T.ts[:, 0:4 * C:4], 0.0, A.mult, A.add, ["rz", "t0_0"], ["dj"])
-    blocks(2, (1, 2))
-    tt(wf("rt", 0, 24), wf("cb", 0, 24), T.dj[:, 15:C:16], A.subtract, ["cb", "dj"], ["rt"])
-    block(2, 3)
-    blocks(3, (0, 1))
-    close(0)
-    blocks(3, (2, 3))
-    close(2)
-    blocks(4, (3, 2))
-    close(1)
-    blocks(4, (1, 0))
-    close(3)
+    def on_scalar(k):
+        for second in [block(k, t) for t in range(4) if TILES[k][2][t] in OPT["scalar"]]:
+            second()
+
+    def on_vector(k, a, z):
+        blocks(k, [t for t in range(4) if TILES[k][2][t] not in OPT["scalar"]][a:z])
+
+    def diagonal(a, z, bank, name):
+        tt(T.ts[:, 4 * a:4 * z:4], T["ps%d" % bank][:, a:z], T.kc[:, a:z], A.is_ge, ["ps%d" % bank, "kc" + name, "tz0"], ["dg" + name])
+
+    masked(0, LO, 0, "a")
+    quant(T.qx[:, LO:C], T.sx[:, LO:C], T.xt[:, 4 * LO:4 * C], ["xt"], ["qx"])
+    keys(6, C, T.qx[:], T.sx[:], ["qxa", "qx"])
+    keys(7, C, T.qx[:], T.sx[:], ["qxa", "qx"])
+    send(prv, by(T.qxn[:]), by(T.qx[:]), "ax", ["qxa", "qx"])
+    send(prv, T.sxn[:], T.sx[:], "ax", ["qxa", "qx"])
+    select(T.et[:, 520:1036], T.t32[:], [[-1, 516]], A.is_equal, 3, 4, ["t32"], ["et1"])
+    iota(T.jj[:], [[1, 400]], 0, ["jj"])
+    iota(T.jm4[:], [[0, 48], [1, 4]], 0, ["jm4"])
+    select(T.c4[:], T.g1[:], [[0, 32], [1, 4], [-1, 4]], A.is_equal, 0, 0, ["g1"], ["c4"])
+    dma("G" if OPT["dma"] else "Y", T.vt[:], T.v[:], "dv", r=["c4"], w=["vt"])
+    own_key(0, LO, "a")
+    ts(T.lst[:, 24:40], wf("tlb", 0, 16), 32.0, A.add, 385.0, A.min, r=["tlb"], w=["lc0"])
+    ts(T.lst[:, 40:56], wf("tlb", 16, 32), NS - 9.0, A.min, r=["tlc"], w=["lc1"])
+    fill(T.lout[:], 0, ["lout"])
+    on_scalar(3)
+    on_vector(3, 0, 4)
+    blocks(4, (3, 2, 1, 0))
+    masked(LO, C, 6, "b")
     blocks(5, (3, 2, 1, 0))
-    close(4)
-    if OPT["short"]:
-        for t in range(4):
-            short_rows(t)
-    else:
-        unit_codes(2)
+    own_key(LO, C, "b")
+    diagonal(0, LO, 0, "a")
+    on_scalar(0)
+    on_vector(1, 0, 2)
+    diagonal(LO, C, 6, "b")
+    on_vector(1, 2, 4)
+    scan(T.dj[:], T.rz[:], T.ts[:, 0:4 * C:4], 0.0, A.mult, A.add, ["rz", "dga", "dgb"], ["dj"])
+    blocks(2, (0,))
+    for t in range(4):
+        short_rows(t)
+    tt(wf("rt", 0, 24), wf("cb", 0, 24), T.dj[:, 15:C:16], A.subtract, ["cb", "dj"], ["rt"])
+    blocks(2, (1,))
+    sj = ["sj%d" % t for t in range(4)]
+    cpy(wf("rowl", 5, 9), T.sj[:, 508:512], sj, ["rowl5"])
+    tt(wf("rowl", 1, 5), T.sj[:, 764:768], T.sj[:, 508:512], A.subtract, sj, ["rowl1"])
+    close(0)
+    close(1)
+    blocks(2, (2,))
     close(5)
+    close(4)
+    blocks(2, (3,))
+    close(3)
+    close(2)
     quant(T.qh[:], T.sh[:], T.ht[:], ["ht"], ["qh"])
-    if OPT["short"]:
-        sj = ["sj%d" % t for t in range(4)]
-        cpy(wf("rowl", 5, 9), T.sj[:, 508:512], sj, ["rowl5"])
-        tt(wf("rowl", 1, 5), T.sj[:, 764:768], T.sj[:, 508:512], A.subtract, sj, ["rowl1"])
-        unit_codes(2)
+    keys(3, B, T.qh[:], T.sh[:], ["qh"])
     tt(T.cp[:, 15:C:16], wf("rt", 0, 24), wf("rowl", 0, 24), A.subtract, ["rt", "cp"] + ["rowl%d" % c for c in range(24)], ["cp15"])
-    unit_codes(1)
+    unit_codes(0)
+    unit_codes(2)
     hold(T.rk[:], T.ps1[:, 0:C], T.cp[:, 0:C], ["ps1", "cp", "cp15"], ["rk"])
-    unit_codes(3)
+    tt(T.sm[:], T.ps3[:, 0:B], T.m0[:, 0:B], A.add, ["ps3", "m0"], ["sm"])
     ts(wu("lpos", 0, 24), T.rk[:, 15:C:16], OFF, A.add, r=["rk"], w=["lpos"])
-    quant(T.qc[:], T.sc4[:], T.c4[:], ["c4"], ["qc"])
+    unit_codes(1)
     cpy(T.mt[:].indirect(wu("lpos", 0, 24)), T.jj[:, 0:C], ["lpos", "jj", "mta", "mtb"], ["mt"])
+    scan(T.ssc[:], T.rs[:, 0:B], T.sm[:], 0.0, A.add, A.min, ["rs", "sm"], ["ssc"])
 
     def arrived_plane(b, bank):
         unit(bank, C, b, T.qxn[:], T.sxn[:], True, ["qxn"])
         return lambda: act(T.dn[:, C * b:C * b + C], T["ps%d" % bank][:, 0:C], F.Copy, ["ps%d" % bank], ["dn%d" % b], scale=1.0 / 64)
 
     act(cf(19), cf(2), F.Identity, ["r"], ["cf19"], scale=-K, bias=K / 2)
-    act(cf(12), cf(1), F.Identity, ["r"], ["cf12"], scale=-K, bias=-OFF)
-    act(cf(11), cf(5), F.Identity, ["cf5"], ["cf11"], bias=16 * OFF)
-    act(T.ksb[:], T.ps2[:, 0:C], F.Copy, ["ps2"], ["ksb"])
-    keys(5, C, T.qxn[:], T.sxn[:], ["qxn"])
+    act(cf(12), cf(1), F.Identity, ["r"], ["cf12"], scale=K, bias=-OFF)
+    act(T.ksb[:, 0:C], T.ps7[:, 0:C], F.Copy, ["ps7"], ["ksb"])
     keys(4, B, T.qh[:], T.sh[:], ["qh"])
-    keys(3, B, T.qh[:], T.sh[:], ["qh"])
-    planes = [arrived_plane(b, bank) for b, bank in zip((0, 2, 1, 3), (6, 7, 0, 2))]
+    keys(5, C, T.qxn[:], T.sxn[:], ["qxn"])
+    planes = [arrived_plane(b, bank) for b, bank in zip((0, 2), (0, 2))]
     act(T.cp4[:], T.jm4[:], F.Identity, ["jm4", "cf19"], ["cp4"], scale=K, bias=cf(19))
-    act(T.knb[:], T.ps5[:, 0:C], F.Copy, ["ps5"], ["knb"])
-    act(T.cp4[:, 3:192:4], T.jm4[:, 0:48], F.Identity, ["jm4", "cf5"], ["cp4"], scale=0.0, bias=cf(5))
+    for t in range(3):
+        act(T.tb[:, AR + PL * t + NA:AR + PL * (t + 1)], T.jm4[:], F.Copy, ["jm4"], ["gap%d" % t])
     act(T.srep[:], T.ps4[:, 0:B], F.Copy, ["ps4"], ["srep"])
-    act(T.cp4o[:], T.cp4[:, 0:128], F.Copy, ["cp4"], ["cp4o"])
-    for k in range(OPT["pl"]):
-        planes.pop(0)()
+    act(T.cp4[:, 3:192:4], T.jm4[:, 0:48], F.Identity, ["jm4", "cf5"], ["cp4"], scale=0.0, bias=cf(5))
+    act(T.knb[:], T.ps5[:, 0:C], F.Copy, ["ps5"], ["knb"])
+    planes.pop(0)()
+    planes.pop(0)()
 
     act(T.sa1[:], T.mt[:].indirect(T.lst[:, 56:69]), F.Copy, ["mt", "la"], ["sa1"])
-    planes.pop(0)()
-    for b in range(4):
-        unit(4 + b, HB, b, T.qh[:, 0:HB], T.sh[:, 0:HB], False, ["qh"])
-    unit(0, HB, 0, T.qh[:, HB:B], T.sh[:, HB:B], False, ["qh"])
-    fill(T.bt[:, 512:768], 0.0, ["btz"])
+    act(T.sexp[:], T.ssc[:].indirect(T.lst[:, 8:24]), F.Copy, ["ssc", "lx"], ["sexp"])
     hold(T.mw[:], T.mt[:], T.cq[:], ["mt", "cq"], ["mw"])
-    hold(T.sa2[:], T.sa1[:], T.cq[:, 0:NA], ["sa1", "cq"], ["sa2"])
+    unit_codes(3)
+    planes = [arrived_plane(b, bank) for b, bank in zip((1, 3), (6, 7))]
     ts(wu("lm", 0, 25), T.mw[:, 15:400:16], OFF, A.add, r=["mw"], w=["lm"])
-    act(T.sp[:], T.ksb[:].indirect(wu("lm", 0, 25)), F.Copy, ["ksb", "lm"], ["sp"])
+    hold(T.sa2[:], T.sa1[:], T.cq[:, 0:NA], ["sa1", "cq"], ["sa2"])
+    act(T.sp[:], T.ksb[:].indirect(wu("lm", 0, 25)), F.Copy, ["ksb", "ksa", "ksz", "lm"], ["sp"])
+    ts(T.mw[:, 15:16], T.mt[:, 1:2], cf(12), A.add, T.mw[:, 15:16], A.min, r=["mt", "cf12", "lm"], w=["mwa"])
+    ts(T.mw[:, 399:400], T.mt[:, C:C + 1], -OFF, A.add, r=["mt", "lm"], w=["mwb"])
     fill(T.fl[:], 0.0, ["flz"])
     ts(T.lout[:, 0:13], T.sa2[:, 15:NA:16], OFF, A.add, r=["sa2"], w=["lout"])
-    ts(T.mw[:, 15:16], T.mt[:, 1:2], cf(12), A.add, T.mw[:, 15:16], A.max, r=["mt", "cf12", "lm"], w=["mwa"])
-    ts(T.mw[:, 399:400], T.mt[:, C:C + 1], -OFF, A.add, r=["mt", "lm"], w=["mwb"])
     send(prv, T.lin[:], T.lout[:], "al", ["lout"])
     dma("Y", by(T.qw[:]), T.wc[:], "dw", r=["lin"], w=["qw"])
     dma("Y", T.sw[:], T.ws[:], "dws", w=["sw"])
-    dma("Y", T.vt[:], T.v[:], "dv", w=["vt"])
-    for copy_out in planes:
-        copy_out()
-    act(T.sp[:, 385:386], cf(1), F.Identity, ["r", "sp"], ["spb"], scale=0.0, bias=3 * H)
-    act(T.sp[:, 0:1], cf(1), F.Identity, ["r", "sp"], ["spa"], scale=0.0, bias=-H)
-    ends = ["sp", "spa", "spb"]
+    act(T.cp4o[:], T.cp4[:, 0:64], F.Copy, ["cp4"], ["cp4o"])
+    ends = ["sp"]
 
     def plane_list(t):
         ts(wu("lm", 26 * t + 26, 26 * t + 51), T.mw[:, 15:400:16], OFF + t / 4, A.add, 4.0, A.mult, r=["mwa", "mwb"], w=["lm%d" % t])
 
     def own_plane(t):
-        act(T.tb[:, PL * t + NA:PL * t + PL], T.xt[:].indirect(wu("lm", 26 * t + 26, 26 * t + 51)), F.Copy, ["xt", "lm%d" % t], ["xs%d" % t], scale=0.5)
+        act(T.tb[:, PL * t:PL * t + PL], T.xt[:].indirect(wu("lm", 26 * t + 26, 26 * t + 51)), F.Copy, ["xt", "lm%d" % t], ["xs%d" % t], scale=0.5)
+        if t % 2 and t // 2 in OPT["dma"]:
+            a, z, have = PL * (t - 1), PL * (t + 1) - 8, ["xs%d" % (t - 1), "xs%d" % t]
+            made = ["zt%d%d" % (i, k) for i in (t - 1, t) for k in range(3)]
+            select(T.zt[:, a:z], T.tb[:, a:z], [[0, z - a]], A.is_ge, 0, 0, have, made)
+            dma("G", T.zt[:, a:z], T.tb[:, a + 1:z + 1], "dm%d" % (t // 2), r=have, w=made, accum_op=A.add)
 
     def arrived_keys(between):
         act(T.gn[:], T.knb[:].indirect(T.lin[:, 0:13]), F.Copy, ["knb", "lin"], ["gn"])
@@ -404,78 +416,86 @@ def rank_program(g, core, T, topo):
         act(T.gn[:, NA - 3:NA], T.cf[:, 24:27], F.Identity, ["xe1"], ["gn1"], scale=H, bias=2 * H)
 
     def arrived_entries(t):
-        act(T.tb[:, PL * t:PL * t + NA], T.dn[:, C * t:C * t + C].indirect(T.lin[:, 0:13]), F.Copy, ["dn%d" % t, "lin"], ["ds%d" % t])
+        act(T.tb[:, AR + PL * t:AR + PL * t + NA], T.dn[:, C * t:C * t + C].indirect(T.lin[:, 0:13]), F.Copy, ["dn%d" % t, "lin"], ["ds%d" % t])
 
     def means(t):
-        for k in range(3):
-            a, z, o = 129 * k, min(129 * k + 129, C + 1), PL * t + NA
+        for k in range(3 if t // 2 not in OPT["dma"] else 0):
+            a, z, o = 129 * k, min(129 * k + 129, C + 1), PL * t
             spare.append((4, lambda a=a, z=z, o=o, k=k: tt(T.zt[:, 400 * t + a:400 * t + z], T.tb[:, o + a:o + z], T.tb[:, o + a + 1:o + z + 1],
                                                          A.add, ["xs%d" % t], ["zt%d%d" % (t, k)])))
+
+    def on_scalar_next(k):
+        if k in "abcd":
+            arrived_entries("abcd".index(k))
+        else:
+            own_plane(int(k))
 
     gaps = list(OPT["gaps"])
 
     def pause():
         gap(4 * int(gaps.pop(0)))
 
-    plane_list(0)
-    plane_list(1)
+    for t in range(4):
+        plane_list(t)
     own_plane(0)
     own_plane(1)
-    scan(wf("spl", 0, 24), T.ms[:, 0:24], T.sp[:, 16:400:16], 0.0, A.add, A.min, ["ms", "sp"], ["spl"])
+    planes.pop(0)()
+    fill(T.bt[:, 512:768], 0.0, ["btz"])
+    quant(T.qc[:], T.sc4[:], T.c4[:], ["c4"], ["qc"])
+    tt(T.b0[:], T.sp[:].indirect(T.lst[:, 24:40]), T.sexp[:], A.is_lt, ends + ["lc0", "sexp"], ["b0"])
     scan(T.ws0[:, 0:NS], T.ms[:, 0:NS], T.sp[:, 1:NS + 1], 0.0, A.add, A.min, ["ms", "sp"], ["ws0a"])
-    ts(T.bt[:, 0:B], T.ps3[:, 0:B], wf("spl", 15, 16), A.is_gt, r=["ps3", "spl"], w=["bta"])
-    ts(T.bt[:, B:2 * B], T.ps3[:, 0:B], wf("spl", 23, 24), A.is_gt, cf(9), A.mult, r=["ps3", "spl", "cf9"], w=["btb"])
+    scan(T.b0s[:], T.rz[:, 0:B], T.b0[:], 0.0, A.mult, A.add, ["rz", "b0"], ["b0s"])
     scan(T.ws0[:, NS:C], T.ms[:, 0:NS], T.sp[:, NS + 1:C + 1], 0.0, A.add, A.min, ["ms", "sp"], ["ws0b"])
+    ts(wu("lo", 0, 16), T.b0s[:, 15:B:16], 32.0, A.mult, 15.0, A.add, r=["b0s"], w=["loa"])
+    ts(wu("lo", 16, 32), T.b0s[:, 15:B:16], 32.0, A.mult, 31.0, A.add, r=["b0s"], w=["lob"])
+    ts(T.cp4o[:, 3:64:4], T.b0s[:, 15:B:16], 32.0, A.mult, cf(5), A.add, r=["b0s", "cf5"], w=["cp4o"])
+    arrived_keys([lambda: on_scalar_next(OPT["s1"][0]), lambda: on_scalar_next(OPT["s1"][1])])
+    means(0)
+    pause()
+    tt(T.bt[:, 0:B], T.ws0[:].indirect(wu("lo", 0, 16)), T.srep[:], A.is_lt, ["ws0a", "ws0b", "loa", "srep"], ["bta"])
+    tt(T.bt[:, B:2 * B], T.ws0[:].indirect(wu("lo", 16, 32)), T.srep[:], A.is_lt, ["ws0a", "ws0b", "lob", "srep"], ["btb"])
+    means(1)
+    pause()
     quant(T.qb[:], T.sb[:], T.bt[:], ["bta", "btb", "btz"], ["qb"])
     mm(1, 128, T.qc[:], T.sc4[:], T.qb[:, 0:128], T.sb[:, 0:128], True, False, ["qc", "qb"])
     mm(1, 128, T.qc[:], T.sc4[:], T.qb[:, 64:192], T.sb[:, 64:192], False, True, ["qc", "qb"])
-    plane_list(2)
-    plane_list(3)
-    arrived_keys([lambda: own_plane(2), lambda: arrived_entries(0)])
-    means(0)
-    pause()
-    hold(T.nb[:], T.ps1[:, 0:64], T.cp4[:, 0:64], ["ps1", "cp4"], ["nb"])
-    pause()
-    ts(wu("lo", 0, 16), T.nb[:, 3:64:4], OFF + 15 / 16, A.add, 16.0, A.mult, r=["nb"], w=["lo"])
-    ts(T.cp4o[:, 3:64:4], T.nb[:, 3:64:4], 16.0, A.mult, cf(11), A.add, r=["nb", "cf11", "cp4o"], w=["cp4q"])
-    scan(wf("spa", 0, 12), T.ms[:, 0:12], T.gn[:, 15:192:16], 0.0, A.add, A.min, ["ms", "gn"], ["spa1"])
-    pause()
-    means(1)
-    tt(T.bt2[:, 0:B], T.ws0[:].indirect(wu("lo", 0, 16)), T.srep[:], A.is_lt, ["ws0a", "ws0b", "lo", "srep"], ["bt2a"])
 
-    ts(T.bt2[:, B:2 * B], T.ps3[:, 0:B], wf("spa", 11, 12), A.is_gt, cf(10), A.mult, r=["ps3", "spa1", "cf10"], w=["bt2b"])
+    tt(T.b1[:], T.gn[:, 8:200].indirect(T.lst[:, 40:56]), T.sexp[:], A.is_lt, ["gn", "lc1", "sexp"], ["b1"])
     scan(T.wa[:], T.ms[:, 0:NA], T.gn[:], 0.0, A.add, A.min, ["ms", "gn", "gn0", "gn1"], ["wa"])
-    quant(T.qb2[:], T.sb2[:], T.bt2[:], ["bt2a", "bt2b"], ["qb2"])
-    mm(2, 128, T.qc[:], T.sc4[:], T.qb2[:], T.sb2[:], True, True, ["qc", "qb2"])
-    unit(3, HB, 3, T.qh[:, HB:B], T.sh[:, HB:B], False, ["qh"])
-    own_plane(3)
+    scan(T.b1s[:], T.rz[:, 0:B], T.b1[:], 0.0, A.mult, A.add, ["rz", "b1"], ["b1s"])
+    hold(T.n0[:], T.ps1[:, 0:64], T.cp4o[:], ["ps1", "cp4o"], ["n0"])
+    own, bucket = T.n0[:, 3:64:4], T.b1s[:, 11:B:16]
     pause()
-    hold(T.n0[:], T.ps2[:, 0:128], T.cp4o[:], ["ps2", "cp4o", "cp4q"], ["n0"])
-    unit(2, HB, 2, T.qh[:, HB:B], T.sh[:, HB:B], False, ["qh"])
+    ts(wu("l1", 0, 16), bucket, 16.0, A.mult, 15.0, A.add, r=["b1s"], w=["l1"])
+    ts(wu("lc", 0, 16), own, OFF, A.add, r=["n0"], w=["lca"])
+    ts(wu("lc", 16, 32), own, OFF + 1, A.add, r=["n0"], w=["lcb"])
+    for k in OPT["s2"]:
+        on_scalar_next(k)
+    near = T.wa[:].indirect(wu("l1", 0, 16))
+    act(T.kl[:], near, F.Copy, ["wa", "l1"], ["near"])
+    act(wf("pre", 0, 16), bucket, F.Identity, ["b1s"], ["pre0"], scale=16.0, bias=AR - 1.0)
+    act(T.fd[:, 1:32:2], own, F.Identity, ["n0"], ["fdc"], bias=OFF)
+    act(T.fd[:, 33:64:2], own, F.Identity, ["n0"], ["fdd"], bias=OFF + 1)
+    act(wf("pre", 32, 48), bucket, F.Identity, ["b1s"], ["pre2"], scale=15.0, bias=OFF - 1)
+    for copy_out in planes:
+        copy_out()
+    for k in OPT["s3"]:
+        on_scalar_next(k)
+    for b in (0, 2, 3):
+        unit(b, HB, b, T.qh[:, HB:B], T.sh[:, HB:B], False, ["qh"])
+    for b in range(3):
+        unit(4 + b, HB, b, T.qh[:, 0:HB], T.sh[:, 0:HB], False, ["qh"])
     pause()
     means(2)
-    own, bucket = T.n0[:, 3:64:4], T.n0[:, 67:128:4]
-    ts(wu("lc", 0, 16), own, OFF, A.add, r=["n0"], w=["lca"])
-    ts(wu("l1", 0, 16), bucket, OFF + 15 / 16, A.add, 16.0, A.mult, r=["n0"], w=["l1"])
-    ts(wu("lc", 16, 32), own, OFF + 1, A.add, r=["n0"], w=["lcb"])
-    ts(wf("pre", 0, 16), bucket, 16.0, A.mult, 16 * OFF - 1 - NA, A.add, r=["n0"], w=["pre0"])
-    act(T.kl[:, 0:B], T.sp[:].indirect(wu("lc", 0, 16)), F.Copy, ends + ["lca"], ["kl"])
-    act(T.kl[:, B:2 * B], T.sp[:].indirect(wu("lc", 16, 32)), F.Copy, ends + ["lcb"], ["ku"])
-    act(T.fd[:, 1:32:2], own, F.Identity, ["n0"], ["fdc"], bias=OFF + NA)
-    act(T.fd[:, 33:64:2], own, F.Identity, ["n0"], ["fdd"], bias=OFF + NA + 1)
-    act(wf("pre", 32, 48), bucket, F.Identity, ["n0"], ["pre2"], scale=15.0, bias=16 * OFF - 1)
-    for t in (1, 2, 3):
-        arrived_entries(t)
-    act(T.cp2[:], T.jm[:, 0:B], F.Identity, ["jm", "cf18"], ["cp2"], scale=K, bias=cf(18))
-    near = T.wa[:].indirect(wu("l1", 0, 16))
-    pause()
     tt(T.bt1[:, B:2 * B], near, T.srep[:], A.is_lt, ["wa", "l1", "srep"], ["bt1b"])
-    tt(T.bt1[:, 0:B], near, T.kl[:, 0:B], A.is_lt, ["wa", "l1", "kl"], ["bt1a"])
-    tt(T.bt1[:, 2 * B:3 * B], near, T.kl[:, B:2 * B], A.is_lt, ["wa", "l1", "ku"], ["bt1c"])
+    pause()
+    tt(T.bt1[:, 0:B], T.sp[:].indirect(wu("lc", 0, 16)), T.kl[:], A.is_gt, ends + ["lca", "near"], ["bt1a"])
+    tt(T.bt1[:, 2 * B:3 * B], T.sp[:].indirect(wu("lc", 16, 32)), T.kl[:], A.is_gt, ends + ["lcb", "near"], ["bt1c"])
     tt(wf("pre", 16, 32), wf("pre", 0, 16), own, A.subtract, ["pre0", "n0"], ["pre1"])
     pause()
     quant(T.qb1[:], T.sb1[:], T.bt1[:], ["bt1a", "bt1b", "bt1c"], ["qb1"])
     mm(1, 192, T.qc[:], T.sc4[:], T.qb1[:], T.sb1[:], True, True, ["qc", "qb1"])
+    unit(7, HB, 3, T.qh[:, 0:HB], T.sh[:, 0:HB], False, ["qh"])
     means(3)
     pause()
     hold(T.n1[:], T.ps1[:, 0:192], T.cp4[:], ["ps1", "cp4"], ["n1"])
@@ -523,7 +543,8 @@ def rank_program(g, core, T, topo):
         send(nxt, half("sa", h), half("sy1", h), "ay%d" % h, ["qy1%d" % h])
 
     def entries(h, t):
-        return T.tb[:, PL * t:PL * t + PL], T.lb[:, B * t + HB * h:B * t + HB * h + HB], ["xs%d" % t, "ds%d" % t, "li"]
+        return (T.tb[:, PL * t:PL * t + AR + NA], T.lb[:, B * t + HB * h:B * t + HB * h + HB],
+                ["xs%d" % k for k in range(t, 4)] + ["ds%d" % k for k in range(t + 1)] + ["li", "gap0", "gap1", "gap2"])
 
     def lower(h, t):
         win, low, have = entries(h, t)
@@ -545,19 +566,22 @@ def rank_program(g, core, T, topo):
     upper(1, 2)
     upper(1, 3)
     results("1", 0, ())
-    ts(wu("bl", 0, 16), T.bin[:], C - 1.0, A.min, r=["bin"], w=["bl0"])
-    ts(wu("bl", 16, 32), T.bin[:], C - 1.0, A.min, 1.0, A.add, r=["bin"], w=["bl1"])
-    quant(T.qv[:], T.sv[:], T.vt[:], ["vt"], ["qv"])
+    fill(T.rz3[:], 1.0, ["rz3"])
     products("1", 1)
-    ts(T.cp2[:, 15:B:16], wu("bl", 0, 16), cf(7), A.add, -1.0, A.add, r=["bl0", "cf7"], w=["cp2"])
+    fill(T.tq[:, 2:3 * B:3], 0.0, ["tqb"])
+    fill(T.rz3[:, 0:C:48], 0.0, ["rz3"])
     pause()
     hand_on(0)
     results("1", 1, OPT["r11"])
-    for k in range(2):
-        act(T.th[:, B * k:B * k + B], T.sp[:].indirect(wu("bl", 16 * k, 16 * k + 16)), F.Copy, ends + ["bl%d" % k], ["th%d" % k])
-    pause()
     hand_on(1)
+    ts(wu("bl", 0, 16), T.bin[:], C - 1.0, A.min, r=["bin"], w=["bl0"])
+    ts(wu("bl", 16, 32), T.bin[:], C - 1.0, A.min, 1.0, A.add, r=["bin"], w=["bl1"])
+    ts(T.tq[:, 2:3 * B:48], T.bin[:], C - 1.0, A.min, -1.0 - NS, A.add, r=["bin"], w=["tqb"])
+    gap()
+    for k in range(2):
+        tt(T.th[:, B * k:B * k + B], T.sp[:].indirect(wu("bl", 16 * k, 16 * k + 16)), T.m0[:, 0:B], A.add, ends + ["bl%d" % k, "m0"], ["th%d" % k])
     gap(99)
+    quant(T.qv[:], T.sv[:], T.vt[:], ["vt"], ["qv"])
 
     def units(h, bs):
         for b in bs:
@@ -566,19 +590,20 @@ def rank_program(g, core, T, topo):
     def stage(h, k, bank=None):
         a, z = HB * h, HB * (h + 1)
         if k == 0:
-            tt(T.tq[:, a:z], T["ps%d" % bank][:, 0:HB], T.th[:, a:z], A.is_ge, ["ps%d" % bank, "th0"], ["tql%d" % h])
-            tt(T.tq[:, B + a:B + z], T["ps%d" % bank][:, 0:HB], T.th[:, B + a:B + z], A.is_gt, ["ps%d" % bank, "th1"], ["tqu%d" % h])
+            tt(T.tq[:, 3 * a:3 * z:3], T["ps%d" % bank][:, 0:HB], T.th[:, a:z], A.is_ge, ["ps%d" % bank, "th0"], ["tql%d" % h])
+            tt(T.tq[:, 3 * a + 1:3 * z:3], T["ps%d" % bank][:, 0:HB], T.th[:, B + a:B + z], A.is_gt, ["ps%d" % bank, "th1"], ["tqu%d" % h])
         if k == 1:
-            tt(T.tq[:, 2 * B + a:2 * B + z], T.tq[:, a:z], T.tq[:, B + a:B + z], A.add, ["tql%d" % h, "tqu%d" % h], ["tq%d" % h])
+            scan(half("p3s", h, 3), T.rz3[:], half("tq", h, 3), 0.0, A.mult, A.add, ["tql%d" % h, "tqu%d" % h, "tqb", "rz3"], ["p3s%d" % h])
         if k == 2:
-            hold(T.p3s[:, a:z], T.tq[:, 2 * B + a:2 * B + z], T.cp2[:, a:z], ["tq%d" % h, "cp2"], ["p3s%d" % h])
-        if k == 3:
-            ts(wu("lp", 8 * h, 8 * h + 8), T.p3s[:, a + 15:z:16], OFF, A.add, r=["p3s%d" % h], w=["lp%d" % h])
+            ts(wu("lp", 8 * h, 8 * h + 8), T.p3s[:, 3 * a + 47:3 * z:48], float(NS), A.add, r=["p3s%d" % h], w=["lp%d" % h])
 
     def picks(h, on_vector, which=range(4)):
         for t in which:
             move(t in on_vector, T.z2[:, 4 * HB * h + t:4 * HB * (h + 1):4], T.zt[:, 400 * t:400 * t + C + 1].indirect(wu("lp", 8 * h, 8 * h + 8)),
                  ["zt%d%d" % (t, k) for k in range(3)] + ["lp%d" % h], ["z2%d%d" % (h, t)])
+
+    def places(h):
+        act(half("pv", h), T.jj[:].indirect(wu("lp", 8 * h, 8 * h + 8)), F.Copy, ["jj", "lp%d" % h], ["pv%d" % h])
 
     def last(h):
         pack("2", h)
@@ -595,21 +620,20 @@ def rank_program(g, core, T, topo):
         stage(0, k, 3)
     keys(2, HB, half("qa", 1), half("sa", 1), ["qa1"])
     units(1, (0, 1, 3))
-    stage(1, 0, 2)
-    stage(0, 3)
-    units(1, (2,))
-    stage(1, 1)
     picks(0, OPT["p0"], (0, 2, 1))
-    stage(1, 2)
+    stage(1, 0, 2)
+    units(1, (2,))
     picks(0, OPT["p0"], (3,))
-    stage(1, 3)
+    places(0)
+    stage(1, 1)
+    stage(1, 2)
     products("2", 0)
     picks(1, OPT["p1"])
-    results("2", 0, ())
+    results("2", 0, OPT["r20"])
     products("2", 1)
+    places(1)
+    dma("Y", T.ov[:], T.pv[0:128:16, :], "so1", r=["pv0", "pv1"])
     last(0)
-    act(T.pv[:], T.jj[:].indirect(wu("lp", 0, 16)), F.Copy, ["jj", "lp0", "lp1"], ["pv"])
-    dma("Y", T.ov[:], T.pv[0:128:16, :], "so1", r=["pv"])
     results("2", 1, OPT["r21"])
     store(0)
     last(1)

@@ -13,11 +13,18 @@ f32, bf, u16, i32, cod, u8 = "float32", "bfloat16", "uint16", "int32", "float8_e
 
 TILES = [(0, 384, [None, 23, 22, 21]), (384, 320, [20, 19, 18, 17]), (704, 256, [16, 15, 14, 13]),
          (960, 192, [12, 11, 10, 9]), (1152, 128, [5, 6, 7, 8]), (1280, 128, [1, 2, 3, 4])]
-OPT = {"low": ((0, 3),), "p0": (3,), "p1": (1, 3), "r11": (1, 3), "r20": (), "r21": (1, 3), "scalar": (23, 22, 21, 12, 11, 10),
-       "gaps": "010100200011", "dma": (0,), "s1": "ac", "s2": "2", "s3": "3bd"}
+ON_SCALAR = (23, 22, 21, 20, 12, 11)
 LO = 208
-WF = {"pre": 0, "br": 48, "cb": 80, "rt": 104, "rowl": 128, "tla": 152, "tlb": 184}
-WU = {"lpos": 0, "lo": 24, "lc": 56, "l1": 88, "li": 104, "lp": 136, "bl": 152, "lm": 184}
+TRACE = []
+SCALARS = False
+PLANE_BANKS = (0, 4, 2, 7)
+ORDER = {
+    "all": "P2 Gg qu P5 Sr qr Ge xa g1 P0 P1 xb Gf Gj Gr Gc Gv ma_ P4 E0 ka qg A06 A07 mb_ A04 A08 kb A02 A09 A19 A01 A03 A17 j3 qh A05 A18 j1 A14 C5 A13 A15 A16 j2 da j0 A20 Kn D0 A12 A10 A11 B12 B10 A22 A23 B11 B22 A21 B23 B13 B21 B18 sr B17 B09 B15 B16 B19 B20 B14 C4 C3 C1 db j6 j5 C2 C0 dj sm rt E2 cr ss rk qc lq E1 mt D2 n0_ kn ks n2_ cq sx s1 mw hs lm s2 sp mb ma la lb lo l0 l2 l1 bb ba w1 nb w0 lw l3 E3 bc bd x0 x1 x2 gn D1 D3 q1 wa nd wb co le n0 x3 e0 p2 p0 e1 k0 k1 n1_ f1 f0 n3_ a2 a1 a0 a3 c10 lc ld c00 c01 c02 c11 c03 c12 d0 c13 c04 c05 c08 c06 c14 U0 U1 c07 c15 L00 c18 c16 l01 l03 l02 u00 u01 c17 u03 u02 l10 l11 l13 l12 br z0 u10 u11 u13 u12 r00 R01 r02 r03 z1 h0 qv m0 r11 r12 R10 R13 m1 m2 K0 h1 b1 b0 b2 t01 t00 t10 s00 s01 s02 t11 K1 V0 s10 s11 K2 s12 g00 g01 g02 g03 g12 g10 y0 o00 v1 o01 o02 G11 G13 y1 o11 o12 o13 O03 Q0 ov O10 w0_ Q1 W1_ sc",
+}
+ORDER = {"all": "P5 Gg qu P2 P4 Sr qr Ge xa g1 P1 xb P0 Gc Gf Gv Gj Gr ma_ E0 ka qg A06 A07 mb_ A05 A09 kb da A13 A14 A17 A03 qh A18 db A02 A20 A01 A15 A08 A04 A16 A19 Kn D0 A12 A11 A10 B09 A22 B12 A23 A21 B23 B22 B20 B21 B11 B18 B17 B16 sr B10 B13 B19 B14 B15 C0 j3 C5 C4 j1 C1 dj j2 j0 C2 j5 rt C3 j6 sm cr ss M0 M4 M1 M5 M2 M3 rk E2 lq E1 mt qc D2 ks n0_ kn cq sx n2_ s1 mw hs lm sp s2 ma mb la lb lo l0 l1 ba l2 bb w1 nb w0 lw E3 l3 bc bd x0 x1 x2 gn D1 D3 q1 wa nd co wb le n0 x3 e0 p0 p2 e1 k0 f0 k1 n1_ n3_ a0 a1 a2 f1 a3 c10 lc ld c00 c01 c02 c11 c03 c12 c13 c04 U1 d0 c05 c06 U0 c14 c08 c07 c15 L00 c18 c16 u00 l01 l03 l02 c17 u01 l10 l13 l12 l11 u03 u02 br z0 u13 u10 u11 u12 r00 r01 R02 r03 z1 h0 m0 m1 qv R13 r10 r11 r12 K0 h1 b1 b2 m2 b0 t01 t00 t10 s00 s01 s02 t11 K1 V0 s10 s11 K2 s12 g01 g02 g03 g00 g10 g12 y0 v1 o00 o02 o01 G11 G13 y1 o11 o12 o13 O03 Q0 ov O10 w0_ Q1 W1_ sc"}
+ORDER = {"all": "P5 Gg Sm Sq St Ss Sb Sa Sc Sg Sd Se P2 Vb Va Vf Ve P0 Vc P1 P4 qu Sh Si Sj r99 qr xa Sn Sf Sk Sl g1 Gf xb Gb Gz Ge Ga Gj Gc Gh Gv Gr ma_ qg ka mb_ A12 A11 A10 A01 kb A05 B12 B11 A21 A23 A22 B23 B22 B21 A20 A04 A02 A18 A03 A07 db A14 A08 B18 B20 A06 A09 A19 C3 C4 j1 A13 da A17 C0 A16 j3 j0 j2 C1 A15 j5 B19 B10 B17 B14 B09 B13 B15 B16 M0 M4 M1 Kn M3 C5 dj j6 M5 E0 C2 rt M2 D0 E1 qh cr E2 rk Vd E3 lq qc mt ks kn n0_ sr cq D1 D2 D3 n1_ So n2_ s1 sm mw ss lm hs n3_ sx sp Sp s2 mb lb ma lo Gd la l1 l0 l2 x0 x1 bb ba w1 gn x2 a3 e0 nb w0 co lw bd bc nd wa U1 U0 q1 le wb m0 c10 n0 c00 ld k0 lc l3 p0 e1 k1 x3 f1 a2 a1 p2 f0 c02 c01 c11 c03 c12 d0 c13 c04 m2 c05 c14 c06 c15 c07 c08 c16 a0 l02 l00 L01 c18 c17 l03 l11 u01 u02 u00 u03 l10 l12 l13 u11 z0 u12 u13 u10 br r00 r01 r03 R02 z1 r10 h0 m1 R11 r12 R13 h1 b1 b0 b2 t01 t00 t10 K0 s00 t11 s01 s02 K1 s10 s11 s12 G12 K2 g00 g01 g02 g03 g11 g10 y0 G13 qv y1 O00 O01 O02 v0 v1 o03 ov O10 Q0 o11 o13 O12 Q1 w0_ W1_ sc"}
+WF = {"pre": 0, "br": 48, "cb": 80, "rt": 104, "rowl": 128, "tla": 152, "off": 184, "hs": 224}
+WU = {"lpos": 0, "lo": 24, "lc": 56, "l1": 72, "li": 104, "lp": 136, "bl": 152, "lm": 184, "ls": 316}
 
 
 def _s(n, d):
@@ -31,19 +38,19 @@ SCRATCH = {
     "qv": _s(128, cod), "sv": _s(128, u8), "qw": _s(512, cod), "sw": _s(512, u8),
     "t32": _s(516, bf), "g1a": _s(512, bf), "g1": _s(512, bf), "c4": _s(512, bf), "et": _s(1040, bf),
     "qg": _s(128, cod), "sg": _s(128, u8), "qc": _s(128, cod), "sc4": _s(128, u8), "qe": _s(512, cod), "se": _s(512, u8),
-    "ci": _s(8, i32), "cf": _s(40, f32), "ic": _s(32, f32), "jm": _s(400, f32), "jm4": _s(192, f32), "jj": _s(400, f32),
-    "m0": _s(C, f32), "rz": _s(C, bf), "rs": _s(C, f32), "ms": _s(C, f32),
-    "cp": _s(400, f32), "cq": _s(400, f32), "cp4": _s(192, f32), "cp4o": _s(64, f32), "rz3": _s(C, bf),
-    "wf": _s(224, f32), "wu": _s(316, u16), "lst": _s(72, u16),
+    "ci": _s(8, i32), "cf": _s(40, f32), "ic": _s(32, f32), "jm": _s(400, f32), "jj": _s(400, f32),
+    "m0": _s(C, f32), "rz": _s(C, bf), "rs": _s(C, f32), "ms": _s(NA, f32),
+    "cp": _s(400, f32), "cp4": _s(160, f32), "rz3": _s(C, bf),
+    "wf": _s(320, f32), "wu": _s(348, u16), "lst": _s(72, u16),
     "fl": _s(64, f32), "fd": _s(64, f32), "ix": _s(64, f32),
     "km": _s(C, f32), "kc": _s(C, f32), "ksb": _s(C + 2, f32), "knb": _s(C, f32), "srep": _s(B, f32),
     "ts": _s(4 * 1408, bf), "qs": _s(1408, cod), "ss": _s(1408, u8), "junk": _s(4416, bf), "dj": _s(C, bf), "sj": _s(768, bf),
-    "rk": _s(C, f32), "mt": _s(400, f32), "sa1": _s(NA, f32), "sa2": _s(NA, f32), "lout": _s(16, u16), "lin": _s(16, u16), "sp": _s(400, f32),
+    "rk": _s(C, f32), "mt": _s(520, f32), "sa1": _s(NA + 16, f32), "sa2": _s(NA + 16, f32), "lout": _s(30, u16), "lin": _s(30, u16), "jm4": _s(160, f32), "sp": _s(400, f32),
     "dn": _s(4 * C, bf), "tb": _s(AR + 3 * PL + NA, bf), "ws0": _s(C, f32),
-    "sm": _s(B, f32), "ssc": _s(B, f32), "sexp": _s(B, f32), "b0": _s(B, bf), "b0s": _s(B, bf), "b1": _s(B, bf), "b1s": _s(B, bf),
-    "bt": _s(768, bf), "qb": _s(192, cod), "sb": _s(192, u8), "n0": _s(64, f32),
+    "bt": _s(4 * B, bf), "qb": _s(128, cod), "sb": _s(128, u8), "n0": _s(64, f32),
+    "sm": _s(B, f32), "ssc": _s(B, f32), "b0s": _s(2 * B, bf), "b1s": _s(B, bf), "r32": _s(2 * B, bf),
     "kl": _s(B, f32), "gn": _s(NA, f32), "mw": _s(400, f32), "wa": _s(NA, f32),
-    "bt1": _s(768, bf), "qb1": _s(192, cod), "sb1": _s(192, u8), "n1": _s(192, f32), "lb": _s(4 * B, bf),
+    "qb1": _s(B, cod), "sb1": _s(B, u8), "n1": _s(192, f32), "lb": _s(4 * B, bf),
     "z1": _s(4 * B, bf), "qz1": _s(B, cod), "sz1": _s(B, u8), "y1": _s(4 * B, bf), "qy1": _s(B, cod), "sy1": _s(B, u8),
     "bout": _s(16, u16), "bin": _s(16, u16), "qa": _s(B, cod), "sa": _s(B, u8),
     "zt": _s(1600, bf), "th": _s(2 * B, f32), "tq": _s(3 * B, bf), "p3s": _s(3 * B, bf), "pv": _s(B, f32),
@@ -68,7 +75,9 @@ def rank_program(g, core, T, topo):
 
     def need(e, r, w):
         want = {}
+        TRACE.append(("need", e, list(r), list(w)))
         for t in list(r) + list(w):
+            assert t in wrote or t in w, t
             ds = [wrote[t]] if t in wrote else []
             if t in w or t.startswith("ps"):
                 ds = ds + read.get(t, [])
@@ -93,6 +102,11 @@ def rank_program(g, core, T, topo):
         cnt[e] += 1
         call().then_inc(T.sem["e" + e], 1)
         note(("e" + e, cnt[e]), r, w)
+
+    def after(*names):
+        TRACE.append(("after", names))
+        for t in names:
+            assert t in wrote, t
 
     dcnt = {}
 
@@ -123,6 +137,9 @@ def rank_program(g, core, T, topo):
     def hold(out, data, row, r, w):
         scan(out, data, row, -1.0, A.max, A.add, r, w)
 
+    def spread(out, keys_, r, w):
+        scan(out, T.ms[:, 0:keys_[1]], keys_[0], 0.0, A.add, A.min, ["ms"] + r, w)
+
     def cpy(out, in_, r, w):
         op("V", lambda: V.tensor_copy(out, in_), r, w)
 
@@ -144,8 +161,8 @@ def rank_program(g, core, T, topo):
         else:
             act(out, in_, F.Copy, r, w)
 
-    def mm(bank, m, lq, ls, rq, rs_, start, stop, r):
-        op("P", lambda: P.matmul_mx(T["ps%d" % bank][:, 0:m], lq, ls, rq, rs_, start, stop), r, ["ps%d" % bank])
+    def mm(bank, m, lq, ls, rq, rs_, start, stop, r, w=()):
+        op("P", lambda: P.matmul_mx(T["ps%d" % bank][:, 0:m], lq, ls, rq, rs_, start, stop), r, ["ps%d" % bank] + list(w))
 
     def by(v):
         return v.bitcast(dt.uint8)
@@ -159,19 +176,11 @@ def rank_program(g, core, T, topo):
     def cf(k):
         return T.cf[:, k:k + 1]
 
-    def unit(bank, m, b, q, s, stop, r):
-        mm(bank, m, T.qe[:, 128 * b:128 * b + 128], T.se[:, 128 * b:128 * b + 128], q, s, True, stop, ["qe%d" % b] + r)
+    def unit(bank, m, b, q, s, stop, r, w=()):
+        mm(bank, m, T.qe[:, 128 * b:128 * b + 128], T.se[:, 128 * b:128 * b + 128], q, s, True, stop, ["qe%d" % b] + r, w)
 
-    def keys(bank, m, q, s, r):
-        mm(bank, m, T.qr[:], T.sr[:], q, s, True, True, ["qr", "sr"] + r)
-
-    spare = []
-
-    def gap(k=4):
-        while spare and k > 0:
-            length, call = spare.pop(0)
-            call()
-            k -= length
+    def keys(bank, m, q, s, r, w=()):
+        mm(bank, m, T.qr[:], T.sr[:], q, s, True, True, ["qr", "sr"] + r, w)
 
     en, ep = len(topo.engines(nxt, core)), len(topo.engines(prv, core))
     wrote["qxn"], wrote["lin"], wrote["bin"] = ("ax", 2 * en), ("al", en), ("ab", ep)
@@ -202,58 +211,54 @@ def rank_program(g, core, T, topo):
     iota(T.ci[:, 0:1], [[0, 1]], 1, ["ci0"], False)
     iota(T.ic[:], [[1, 32]], 0, ["ic"])
     iota(T.jm[:], [[0, 25], [1, 16]], 0, ["jm"])
-    iota(T.g1a[:], [[1, 8], [0, 64]], 0, ["g1a"])
-    for k in range(3):
-        pad(k)
+    fill(T.t32[:], 32.0, ["t32"])
     ts(T.ci[:, 1:2], T.ci[:, 0:1], 15, A.bitwise_and, r=["ci0"], w=["ci1"])
     ts(T.ci[:, 2:3], T.ci[:, 0:1], 15, A.bitwise_and, 2, A.logical_shift_right, r=["ci0"], w=["ci2"])
     ts(T.ci[:, 3:4], T.ci[:, 0:1], 4, A.logical_shift_right, r=["ci0"], w=["ci3"])
     ts(T.lst[:, 0:8], T.ic[:, 0:8], 16.0, A.mult, r=["ic"], w=["lu"])
-    pad(5)
-    cpy(T.cf[:, 1:4], T.ci[:, 1:4], ["ci1", "ci2", "ci3"], ["r"])
-    fill(T.t32[:], 32.0, ["t32"])
-    select(T.et[:, 0:516], T.t32[:], [[-1, 516]], A.is_equal, 2, 4, ["t32"], ["et0"])
-    act(cf(16), cf(1), F.Identity, ["r"], ["cf16"], scale=-2 * H)
-    act(cf(21), cf(1), F.Square, ["r"], ["cf21"], bias=-15.0)
-    act(cf(22), cf(2), F.Square, ["r"], ["cf22"], bias=-3.0)
-    act(cf(18), cf(1), F.Identity, ["r"], ["cf18"], scale=-K, bias=K / 2)
-    act(cf(17), cf(1), F.Identity, ["r"], ["cf17"], scale=4 * H, bias=4 * H)
-    act(T.rs[:], T.jm[:, 0:C], F.Relu, ["jm"], ["rs"], scale=-4 * H, bias=4 * H)
-    act(cf(7), cf(21), F.Identity, ["cf21"], ["cf7"], scale=-K / 2, bias=-OFF)
-    act(cf(5), cf(22), F.Identity, ["cf22"], ["cf5"], scale=-K / 2, bias=-OFF)
-    act(T.m0[:], T.jm[:, 0:C], F.Abs, ["jm", "cf16"], ["m0"], scale=2 * H, bias=cf(16))
-    act(cf(8), cf(1), F.Identity, ["r", "cf7"], ["cf8"], scale=-1.0, bias=cf(7))
-    act(T.rz[:], T.jm[:, 0:C], F.Sign, ["jm"], ["rz"])
-    act(wf("cb", 0, 24), T.ic[:, 1:25], F.Identity, ["ic", "cf8"], ["cb"], scale=16.0, bias=cf(8))
-    act(T.cp[:], T.jm[:], F.Identity, ["jm", "cf18"], ["cp"], scale=K, bias=cf(18))
-    act(T.cq[:], T.jm[:], F.Identity, ["jm", "cf18"], ["cq"], scale=K, bias=cf(18))
-    act(T.ms[:], T.jm[:, 0:C], F.Relu, ["jm", "cf17"], ["ms"], scale=-4 * H, bias=cf(17))
-    act(T.cq[:, 15:400:16], T.ic[:, 0:25], F.Identity, ["ic", "cf7"], ["cq"], scale=0.0, bias=cf(7))
     pad(3)
-    pad(4)
-    fill(T.mt[:, 0:1], float(C), ["mtb"])
-    fill(T.ksb[:, C:C + 1], -H, ["ksa"])
-    fill(T.ksb[:, C + 1:C + 2], 3 * H, ["ksz"])
-    quant(T.qu[:], T.su[:], T.ut[:], ["ut"], ["qu"])
-    ts(wf("tla", 0, 13), T.ic[:, 0:13], 15.0, A.mult, cf(1), A.add, r=["ic", "r"], w=["tla0"])
-    ts(cf(9), cf(1), 11.0, A.is_ge, 1000.0, A.mult, r=["r"], w=["cf9"])
-    ts(cf(10), cf(1), 16.0, A.mult, 7.0, A.add, r=["r"], w=["cf10"])
-    cpy(T.qr[:].bitcast(dt.uint32), T.qu[:].bitcast(dt.uint32).indirect(T.lst[:, 0:8]), ["qu", "lu"], ["qr"])
-    cpy(T.sr[:], T.su[:].indirect(T.lst[:, 0:8]), ["qu", "lu"], ["sr"])
-    ts(wf("tla", 16, 29), wf("tla", 0, 13), 1.0, A.max, float(NS), A.min, r=["tla0"], w=["tla1"])
-    ts(cf(13), cf(1), 32.0, A.mult, cf(9), A.add, r=["r", "cf9"], w=["cf13"])
-    fill(T.mt[:, 384:400], C + 1.0, ["mta"])
-    ts(T.lst[:, 8:24], T.ic[:, 0:16], 16.0, A.mult, 15.0, A.add, r=["ic"], w=["lx"])
+    cpy(T.cf[:, 1:4], T.ci[:, 1:4], ["ci1", "ci2", "ci3"], ["r"])
 
-    quant(T.qx[:, 0:LO], T.sx[:, 0:LO], T.xt[:, 0:4 * LO], ["xta"], ["qxa"])
-    keys(0, LO, T.qx[:, 0:LO], T.sx[:, 0:LO], ["qxa"])
-    keys(2, LO, T.qx[:, 0:LO], T.sx[:, 0:LO], ["qxa"])
-    ts(T.g1[:], T.g1a[:], cf(3), A.is_equal, r=["g1a", "r"], w=["g1"])
-    ts(wf("tlb", 0, 16), T.ic[:, 0:16], 0.0, A.mult, cf(13), A.add, r=["ic", "cf13"], w=["tlb"])
-    ts(wf("tlb", 16, 32), T.ic[:, 0:16], 0.0, A.mult, cf(10), A.add, r=["ic", "cf10"], w=["tlc"])
-    ts(T.lst[:, 56:69], wf("tla", 16, 29), 2.0, A.mult, r=["tla1"], w=["la"])
-    fill(wf("rowl", 0, 1), 0.0, ["rowl0"])
-    quant(T.qg[:], T.sg[:], T.g1[:], ["g1"], ["qg"])
+    def level(out, c, w):
+        op("G", lambda: g.iota(out, [[0, c[1]]], int(c[0]), 0, allow_small_or_imprecise_dtypes=True), (), w)
+
+    const = {
+        "Sa": lambda: act(cf(16), cf(1), F.Identity, ["r"], ["cf16"], scale=-2 * H),
+        "Sb": lambda: act(cf(21), cf(1), F.Square, ["r"], ["cf21"], bias=-15.0),
+        "Sc": lambda: act(cf(22), cf(2), F.Square, ["r"], ["cf22"], bias=-3.0),
+        "Sd": lambda: act(cf(18), cf(1), F.Identity, ["r"], ["cf18"], scale=-K, bias=K / 2),
+        "Se": lambda: act(cf(17), cf(1), F.Identity, ["r"], ["cf17"], scale=4 * H, bias=4 * H),
+        "Sf": lambda: act(T.rs[:], T.jm[:, 0:C], F.Relu, ["jm"], ["rs"], scale=-4 * H, bias=4 * H),
+        "Sg": lambda: act(cf(7), cf(21), F.Identity, ["cf21"], ["cf7"], scale=-K / 2, bias=-OFF),
+        "Sh": lambda: act(cf(5), cf(22), F.Identity, ["cf22"], ["cf5"], scale=-K / 2, bias=-OFF),
+        "Si": lambda: act(T.m0[:], T.jm[:, 0:C], F.Abs, ["jm", "cf16"], ["m0"], scale=2 * H, bias=cf(16)),
+        "Sj": lambda: act(cf(8), cf(1), F.Identity, ["r", "cf7"], ["cf8"], scale=-1.0, bias=cf(7)),
+        "Sk": lambda: act(wf("cb", 0, 24), T.ic[:, 1:25], F.Identity, ["ic", "cf8"], ["cb"], scale=16.0, bias=cf(8)),
+        "Sl": lambda: act(T.cp[:], T.jm[:], F.Identity, ["jm", "cf18"], ["cp"], scale=K, bias=cf(18)),
+        "Sm": lambda: act(cf(19), cf(2), F.Identity, ["r"], ["cf19"], scale=-K, bias=K / 2),
+        "Sn": lambda: act(T.ms[:], T.jm[:, 0:NA], F.Relu, ["jm", "cf17"], ["ms"], scale=-4 * H, bias=cf(17)),
+        "So": lambda: act(T.cp4[:], T.jm4[:], F.Identity, ["jm4", "cf19"], ["cp40"], scale=K, bias=cf(19)),
+        "Sp": lambda: act(T.cp4[:, 3:160:4], T.jm4[:, 0:40], F.Identity, ["jm4", "cf5", "cp40"], ["cp43"], scale=0.0, bias=cf(5)),
+        "Sq": lambda: act(cf(12), cf(1), F.Identity, ["r"], ["cf12"], scale=K, bias=-OFF),
+        "Ss": lambda: act(cf(9), cf(1), F.Relu, ["r"], ["cf9"], scale=2 * H, bias=-24 * H),
+        "St": lambda: act(T.ksb[:, C:C + 2], T.ic[:, 0:2], F.Identity, ["ic"], ["ksa"], scale=4 * H, bias=-H),
+        "Va": lambda: ts(wf("tla", 0, 13), T.ic[:, 0:13], 30.0, A.mult, cf(1), A.add, r=["ic", "r"], w=["tla0"]),
+        "Vb": lambda: ts(wf("tla", 29, 30), cf(1), 1.0, A.add, 30.0, A.mult, r=["r"], w=["tla2"]),
+        "Vc": lambda: ts(wf("tla", 16, 29), wf("tla", 0, 13), cf(1), A.add, 2.0, A.max, r=["tla0"], w=["tla1"]),
+        "Vd": lambda: ts(T.lst[:, 56:70], wf("tla", 16, 30), float(C), A.min, r=["tla1", "tla2"], w=["la"]),
+        "Ve": lambda: ts(T.lst[:, 8:24], T.ic[:, 0:16], 16.0, A.mult, 15.0, A.add, r=["ic"], w=["lx"]),
+        "Vf": lambda: fill(wf("rowl", 0, 1), 0.0, ["rowl0"]),
+        "Ga": lambda: (level(T.mt[:, 0:1], (C, 1), ["mtb"]), level(T.mt[:, C:520], (C + 1, 520 - C), ["mta"])),
+        "Gb": lambda: (level(wf("off", 0, 16), (OFF, 16), ["off"]), level(T.fl[:], (0, 64), ["flz"])),
+        "Gd": lambda: [level(T.tb[:, AR + PL * t + NA:AR + PL * (t + 1)], (0, PL - NA), ["gap%d" % t]) for t in range(3)],
+        "Gh": lambda: iota(T.jm4[:], [[0, 40], [1, 4]], 0, ["jm4"]),
+        "Gz": lambda: select(T.rz[:], T.t32[:, 0:C], [[0, 24], [1, 16]], A.not_equal, 0, 0, ["t32"], ["rz"]),
+    }
+
+    def first_piece():
+        quant(T.qx[:, 0:LO], T.sx[:, 0:LO], T.xt[:, 0:4 * LO], ["xta"], ["qxa"])
+        keys(0, LO, T.qx[:, 0:LO], T.sx[:, 0:LO], ["qxa"])
+        keys(2, LO, T.qx[:, 0:LO], T.sx[:, 0:LO], ["qxa"])
 
     def masked(a, z, bank, name):
         tt(T.km[:, a:z], T["ps%d" % bank][:, a:z], T.m0[:, a:z], A.add, ["ps%d" % bank, "m0"], ["km" + name])
@@ -261,258 +266,261 @@ def rank_program(g, core, T, topo):
     def own_key(a, z, name):
         scan(T.kc[:, a:z], T.rs[:, a:z], T.km[:, a:z], 0.0, A.add, A.min, ["rs", "km" + name], ["kc" + name])
 
-    at, closed = [0], [0]
+    closed = [0]
 
     def close(k):
         lo, wd, blocks = TILES[k]
         quant(T.qs[:, lo:lo + wd], T.ss[:, lo:lo + wd], T.ts[:, 4 * lo:4 * (lo + wd)],
-              ["tz%d" % lo, "dga", "dgb"] + ["t%d_%d" % (lo, t) for t in range(4)], ["qs%d" % lo])
-        closed[0] += 1
-        mm(1, wd, T.qg[:], T.sg[:], T.qs[:, lo:lo + wd], T.ss[:, lo:lo + wd], closed[0] == 1, closed[0] == len(TILES), ["qg", "qs%d" % lo])
+              ["tz%d" % lo] + (["dga", "dgb"] if k == 0 else []) + ["t%d_%d" % (lo, t) for t in range(4) if blocks[t]], ["qs%d" % lo])
 
-    def block(k, t):
+    def columns(k):
         lo, wd, blocks = TILES[k]
-        c, name = blocks[t], "t%d_%d" % (lo, t)
-        m = 16 * c
+        after(*["cs0"] * (k > 0))
+        closed[0] += 1
+        mm(1, wd, T.qg[:], T.sg[:], T.qs[:, lo:lo + wd], T.ss[:, lo:lo + wd], k == 0, closed[0] == len(TILES), ["qg", "qs%d" % lo], ["cs%d" % k])
+
+    def block(c, second):
+        lo, t = [(lo, blocks.index(c)) for lo, wd, blocks in TILES if c in blocks][0]
+        name, m = "t%d_%d" % (lo, t), 16 * c
         kc, mine, theirs = ("kca", "ps0", "ps2") if m < LO else ("kcb", "ps6", "ps7")
-        bits, key, spare_ = T.ts[:, 4 * lo + t:4 * (lo + m):4], T.kc[:, m + 15:m + 16], T.junk[:, at[0]:at[0] + m]
-        at[0] += m
-        if c in OPT["scalar"]:
+        bits, key, spare_ = T.ts[:, 4 * lo + t:4 * (lo + m):4], T.kc[:, m + 15:m + 16], T.junk[:, 8 * c * (c - 1):8 * c * (c + 1)]
+        if c in ON_SCALAR and not second:
             act(spare_, T[theirs][:, 0:m], F.Sign, [theirs, kc], ["sg%d" % c], scale=-1.0, bias=key)
-            return lambda: act(bits, spare_, F.Relu, ["sg%d" % c, "tz%d" % lo], [name, "rowl%d" % c], scale=-1.0, acc=wf("rowl", c, c + 1))
-        ts(bits, T[mine][:, 0:m], key, A.is_gt, r=[mine, kc, "tz%d" % lo], w=[name])
-        if c > 8:
+        elif c in ON_SCALAR:
+            act(bits, spare_, F.Relu, ["sg%d" % c, "tz%d" % lo], [name, "rowl%d" % c], scale=-1.0, acc=wf("rowl", c, c + 1))
+        elif not second:
+            ts(bits, T[mine][:, 0:m], key, A.is_gt, r=[mine, kc, "tz%d" % lo], w=[name, "sg%d" % c])
+        else:
             act(spare_, bits, F.Copy, [name], ["rowl%d" % c], acc=wf("rowl", c, c + 1))
-        return None
 
     def short_rows(t):
         bits = T.ts[:, 4 * 1152 + t:4 * 1344:4]
         scan(T.sj[:, t:768:4], bits, bits, 0.0, A.add, A.max, ["tz1152", "tz1280", "t1152_%d" % t, "t1280_%d" % t], ["sj%d" % t])
 
-    def blocks(k, ts_=range(4)):
-        for t in ts_:
-            block(k, t)
-
-    def on_scalar(k):
-        for second in [block(k, t) for t in range(4) if TILES[k][2][t] in OPT["scalar"]]:
-            second()
-
-    def on_vector(k, a, z):
-        blocks(k, [t for t in range(4) if TILES[k][2][t] not in OPT["scalar"]][a:z])
-
     def diagonal(a, z, bank, name):
         tt(T.ts[:, 4 * a:4 * z:4], T["ps%d" % bank][:, a:z], T.kc[:, a:z], A.is_ge, ["ps%d" % bank, "kc" + name, "tz0"], ["dg" + name])
 
-    masked(0, LO, 0, "a")
-    quant(T.qx[:, LO:C], T.sx[:, LO:C], T.xt[:, 4 * LO:4 * C], ["xt"], ["qx"])
-    keys(6, C, T.qx[:], T.sx[:], ["qxa", "qx"])
-    keys(7, C, T.qx[:], T.sx[:], ["qxa", "qx"])
-    send(prv, by(T.qxn[:]), by(T.qx[:]), "ax", ["qxa", "qx"])
-    send(prv, T.sxn[:], T.sx[:], "ax", ["qxa", "qx"])
-    select(T.et[:, 520:1036], T.t32[:], [[-1, 516]], A.is_equal, 3, 4, ["t32"], ["et1"])
-    iota(T.jj[:], [[1, 400]], 0, ["jj"])
-    iota(T.jm4[:], [[0, 48], [1, 4]], 0, ["jm4"])
-    select(T.c4[:], T.g1[:], [[0, 32], [1, 4], [-1, 4]], A.is_equal, 0, 0, ["g1"], ["c4"])
-    dma("G" if OPT["dma"] else "Y", T.vt[:], T.v[:], "dv", r=["c4"], w=["vt"])
-    own_key(0, LO, "a")
-    ts(T.lst[:, 24:40], wf("tlb", 0, 16), 32.0, A.add, 385.0, A.min, r=["tlb"], w=["lc0"])
-    ts(T.lst[:, 40:56], wf("tlb", 16, 32), NS - 9.0, A.min, r=["tlc"], w=["lc1"])
-    fill(T.lout[:], 0, ["lout"])
-    on_scalar(3)
-    on_vector(3, 0, 4)
-    blocks(4, (3, 2, 1, 0))
-    masked(LO, C, 6, "b")
-    blocks(5, (3, 2, 1, 0))
-    own_key(LO, C, "b")
-    diagonal(0, LO, 0, "a")
-    on_scalar(0)
-    on_vector(1, 0, 2)
-    diagonal(LO, C, 6, "b")
-    on_vector(1, 2, 4)
-    scan(T.dj[:], T.rz[:], T.ts[:, 0:4 * C:4], 0.0, A.mult, A.add, ["rz", "dga", "dgb"], ["dj"])
-    blocks(2, (0,))
-    for t in range(4):
-        short_rows(t)
-    tt(wf("rt", 0, 24), wf("cb", 0, 24), T.dj[:, 15:C:16], A.subtract, ["cb", "dj"], ["rt"])
-    blocks(2, (1,))
+    def second_piece():
+        quant(T.qx[:, LO:C], T.sx[:, LO:C], T.xt[:, 4 * LO:4 * C], ["xt"], ["qx"])
+        keys(6, C, T.qx[:], T.sx[:], ["qxa", "qx"])
+        keys(7, C, T.qx[:], T.sx[:], ["qxa", "qx"])
+        send(prv, by(T.qxn[:]), by(T.qx[:]), "ax", ["qxa", "qx"])
+        send(prv, T.sxn[:], T.sx[:], "ax", ["qxa", "qx"])
+
+    def free(bank):
+        low, high = [c for c in range(1, 24) if 16 * c < LO], [c for c in range(1, 24) if 16 * c >= LO]
+        after(*{0: ["dga"] + ["sg%d" % c for c in low if c not in ON_SCALAR], 2: ["sg%d" % c for c in low if c in ON_SCALAR], 4: [],
+                6: ["dgb"] + ["sg%d" % c for c in high if c not in ON_SCALAR], 7: ["ksb"] + ["sg%d" % c for c in high if c in ON_SCALAR]}[bank])
+
     sj = ["sj%d" % t for t in range(4)]
-    cpy(wf("rowl", 5, 9), T.sj[:, 508:512], sj, ["rowl5"])
-    tt(wf("rowl", 1, 5), T.sj[:, 764:768], T.sj[:, 508:512], A.subtract, sj, ["rowl1"])
-    close(0)
-    close(1)
-    blocks(2, (2,))
-    close(5)
-    close(4)
-    blocks(2, (3,))
-    close(3)
-    close(2)
-    quant(T.qh[:], T.sh[:], T.ht[:], ["ht"], ["qh"])
-    keys(3, B, T.qh[:], T.sh[:], ["qh"])
-    tt(T.cp[:, 15:C:16], wf("rt", 0, 24), wf("rowl", 0, 24), A.subtract, ["rt", "cp"] + ["rowl%d" % c for c in range(24)], ["cp15"])
-    unit_codes(0)
-    unit_codes(2)
-    hold(T.rk[:], T.ps1[:, 0:C], T.cp[:, 0:C], ["ps1", "cp", "cp15"], ["rk"])
-    tt(T.sm[:], T.ps3[:, 0:B], T.m0[:, 0:B], A.add, ["ps3", "m0"], ["sm"])
-    ts(wu("lpos", 0, 24), T.rk[:, 15:C:16], OFF, A.add, r=["rk"], w=["lpos"])
-    unit_codes(1)
-    cpy(T.mt[:].indirect(wu("lpos", 0, 24)), T.jj[:, 0:C], ["lpos", "jj", "mta", "mtb"], ["mt"])
-    scan(T.ssc[:], T.rs[:, 0:B], T.sm[:], 0.0, A.add, A.min, ["rs", "sm"], ["ssc"])
+    step = {
+        "Ge": lambda: select(T.et[:, 0:516], T.t32[:], [[-1, 516]], A.is_equal, 2, 4, ["t32"], ["et0"]),
+        "Gf": lambda: select(T.et[:, 520:1036], T.t32[:], [[-1, 516]], A.is_equal, 3, 4, ["t32"], ["et1"]),
+        "Gg": lambda: iota(T.g1a[:], [[1, 8], [0, 64]], 0, ["g1a"]),
+        "Gr": lambda: select(T.r32[:], T.t32[:, 0:512], [[0, 16], [1, 32]], A.not_equal, 0, 0, ["t32"], ["r32"]),
+        "Gj": lambda: iota(T.jj[:], [[1, 400]], 0, ["jj"]),
+        "Gc": lambda: select(T.c4[:], T.g1[:], [[0, 32], [1, 4], [-1, 4]], A.is_equal, 0, 0, ["g1"], ["c4"]),
+        "Gv": lambda: (after("qx"), dma("G", T.vt[:], T.v[:], "dv", w=["vt"])),
+        "g1": lambda: ts(T.g1[:], T.g1a[:], cf(3), A.is_equal, r=["g1a", "r"], w=["g1"]),
+        "qu": lambda: quant(T.qu[:], T.su[:], T.ut[:], ["ut"], ["qu"]),
+        "qr": lambda: cpy(T.qr[:].bitcast(dt.uint32), T.qu[:].bitcast(dt.uint32).indirect(T.lst[:, 0:8]), ["qu", "lu"], ["qr"]),
+        "Sr": lambda: cpy(T.sr[:], T.su[:].indirect(T.lst[:, 0:8]), ["qu", "lu"], ["sr"]),
+        "P0": lambda: pad(0), "P1": lambda: pad(1), "P2": lambda: pad(2), "P4": lambda: pad(4), "P5": lambda: pad(5),
+        "xa": first_piece,
+        "ma_": lambda: masked(0, LO, 0, "a"), "mb_": lambda: masked(LO, C, 6, "b"), "ka": lambda: own_key(0, LO, "a"), "kb": lambda: own_key(LO, C, "b"),
+        "da": lambda: diagonal(0, LO, 0, "a"), "db": lambda: diagonal(LO, C, 6, "b"), "xb": second_piece,
+        "qg": lambda: quant(T.qg[:], T.sg[:], T.g1[:], ["g1"], ["qg"]),
+        "qc": lambda: quant(T.qc[:], T.sc4[:], T.c4[:], ["c4"], ["qc"]),
+        "dj": lambda: scan(T.dj[:], T.rz[:], T.ts[:, 0:4 * C:4], 0.0, A.min, A.add, ["rz", "dga", "dgb"], ["dj"]),
+        "rt": lambda: tt(wf("rt", 0, 24), wf("cb", 0, 24), T.dj[:, 15:C:16], A.subtract, ["cb", "dj"], ["rt"]),
+        "j5": lambda: cpy(wf("rowl", 5, 9), T.sj[:, 508:512], sj, ["rowl5"]),
+        "j6": lambda: tt(wf("rowl", 1, 5), T.sj[:, 764:768], T.sj[:, 508:512], A.subtract, sj, ["rowl1"]),
+        "cr": lambda: tt(T.cp[:, 15:C:16], wf("rt", 0, 24), wf("rowl", 0, 24), A.subtract,
+                         ["rt", "cp"] + ["rowl%d" % c for c in [0, 1, 5] + list(range(9, 24))], ["cp15"]),
+        "rk": lambda: (after(*["cs%d" % k for k in range(len(TILES))]), hold(T.rk[:], T.ps1[:, 0:C], T.cp[:, 0:C], ["ps1", "cp", "cp15"], ["rk"])),
+        "lq": lambda: ts(wu("lpos", 0, 24), T.rk[:, 15:C:16], OFF, A.add, r=["rk"], w=["lpos"]),
+        "mt": lambda: cpy(T.mt[:].indirect(wu("lpos", 0, 24)), T.jj[:, 0:C], ["lpos", "jj", "mta", "mtb"], ["mt"]),
+        "cq": lambda: act(T.cp[:, 15:400:16], T.ic[:, 0:25], F.Identity, ["ic", "cf7", "rk"], ["cp15", "cq"], scale=0.0, bias=cf(7)),
+        "ks": lambda: act(T.ksb[:, 0:C], T.ps7[:, 0:C], F.Copy, ["ps7"], ["ksb"]),
+        "qh": lambda: (quant(T.qh[:], T.sh[:], T.ht[:], ["ht"], ["qh"]), keys(3, B, T.qh[:], T.sh[:], ["qh"])),
+        "sr": lambda: act(T.srep[:], T.ps3[:, 0:B], F.Copy, ["ps3"], ["srep"]),
+        "Kn": lambda: (after("qx"), keys(5, C, T.qxn[:], T.sxn[:], ["qxn"])),
+        "kn": lambda: act(T.knb[:], T.ps5[:, 0:C], F.Copy, ["ps5"], ["knb"]),
+    }
+    for c in range(1, 24):
+        step["A%02d" % c] = lambda c=c: block(c, False)
+        step["B%02d" % c] = lambda c=c: block(c, True)
+    for k in range(len(TILES)):
+        step["C%d" % k] = lambda k=k: close(k)
+        step["M%d" % k] = lambda k=k: columns(k)
+    for t, bank in enumerate(PLANE_BANKS):
+        step["j%d" % t] = lambda t=t: short_rows(t)
+        step["E%d" % t] = lambda t=t: unit_codes(t)
+        step["D%d" % t] = lambda t=t, bank=bank: (after("qx"), free(bank), unit(bank, C, t, T.qxn[:], T.sxn[:], True, ["qxn"], ["pn%d" % t]))
+        step["n%d_" % t] = lambda t=t, bank=bank: (after("pn%d" % t), act(T.dn[:, C * t:C * t + C], T["ps%d" % bank][:, 0:C], F.Copy, ["ps%d" % bank], ["dn%d" % t], scale=1.0 / 64))
 
-    def arrived_plane(b, bank):
-        unit(bank, C, b, T.qxn[:], T.sxn[:], True, ["qxn"])
-        return lambda: act(T.dn[:, C * b:C * b + C], T["ps%d" % bank][:, 0:C], F.Copy, ["ps%d" % bank], ["dn%d" % b], scale=1.0 / 64)
+    step.update(const)
+    cp, cp4, ks = ["cp", "cq"], ["cp40", "cp43"], ["ksb", "ksa"]
+    own, bucket = T.n0[:, 3:64:4], T.b1s[:, 11:B:16]
 
-    act(cf(19), cf(2), F.Identity, ["r"], ["cf19"], scale=-K, bias=K / 2)
-    act(cf(12), cf(1), F.Identity, ["r"], ["cf12"], scale=K, bias=-OFF)
-    act(T.ksb[:, 0:C], T.ps7[:, 0:C], F.Copy, ["ps7"], ["ksb"])
-    keys(4, B, T.qh[:], T.sh[:], ["qh"])
-    keys(5, C, T.qxn[:], T.sxn[:], ["qxn"])
-    planes = [arrived_plane(b, bank) for b, bank in zip((0, 2), (0, 2))]
-    act(T.cp4[:], T.jm4[:], F.Identity, ["jm4", "cf19"], ["cp4"], scale=K, bias=cf(19))
-    for t in range(3):
-        act(T.tb[:, AR + PL * t + NA:AR + PL * (t + 1)], T.jm4[:], F.Copy, ["jm4"], ["gap%d" % t])
-    act(T.srep[:], T.ps4[:, 0:B], F.Copy, ["ps4"], ["srep"])
-    act(T.cp4[:, 3:192:4], T.jm4[:, 0:48], F.Identity, ["jm4", "cf5"], ["cp4"], scale=0.0, bias=cf(5))
-    act(T.knb[:], T.ps5[:, 0:C], F.Copy, ["ps5"], ["knb"])
-    planes.pop(0)()
-    planes.pop(0)()
-
-    act(T.sa1[:], T.mt[:].indirect(T.lst[:, 56:69]), F.Copy, ["mt", "la"], ["sa1"])
-    act(T.sexp[:], T.ssc[:].indirect(T.lst[:, 8:24]), F.Copy, ["ssc", "lx"], ["sexp"])
-    hold(T.mw[:], T.mt[:], T.cq[:], ["mt", "cq"], ["mw"])
-    unit_codes(3)
-    planes = [arrived_plane(b, bank) for b, bank in zip((1, 3), (6, 7))]
-    ts(wu("lm", 0, 25), T.mw[:, 15:400:16], OFF, A.add, r=["mw"], w=["lm"])
-    hold(T.sa2[:], T.sa1[:], T.cq[:, 0:NA], ["sa1", "cq"], ["sa2"])
-    act(T.sp[:], T.ksb[:].indirect(wu("lm", 0, 25)), F.Copy, ["ksb", "ksa", "ksz", "lm"], ["sp"])
-    ts(T.mw[:, 15:16], T.mt[:, 1:2], cf(12), A.add, T.mw[:, 15:16], A.min, r=["mt", "cf12", "lm"], w=["mwa"])
-    ts(T.mw[:, 399:400], T.mt[:, C:C + 1], -OFF, A.add, r=["mt", "lm"], w=["mwb"])
-    fill(T.fl[:], 0.0, ["flz"])
-    ts(T.lout[:, 0:13], T.sa2[:, 15:NA:16], OFF, A.add, r=["sa2"], w=["lout"])
-    send(prv, T.lin[:], T.lout[:], "al", ["lout"])
-    dma("Y", by(T.qw[:]), T.wc[:], "dw", r=["lin"], w=["qw"])
-    dma("Y", T.sw[:], T.ws[:], "dws", w=["sw"])
-    act(T.cp4o[:], T.cp4[:, 0:64], F.Copy, ["cp4"], ["cp4o"])
-    ends = ["sp"]
-
-    def plane_list(t):
-        ts(wu("lm", 26 * t + 26, 26 * t + 51), T.mw[:, 15:400:16], OFF + t / 4, A.add, 4.0, A.mult, r=["mwa", "mwb"], w=["lm%d" % t])
+    def list_out():
+        ts(T.lout[:, 0:14], T.sa2[:, 15:NA + 16:16], OFF, A.add, r=["sa2"], w=["lout"])
+        ts(T.lout[:, 14:30], wf("off", 0, 16), T.sa2[:, NA + 15:NA + 16], A.add, r=["sa2", "off"], w=["lout2"])
+        send(prv, T.lin[:], T.lout[:], "al", ["lout", "lout2"])
+        dma("Y", by(T.qw[:]), T.wc[:], "dw", r=["lin"], w=["qw"])
+        dma("Y", T.sw[:], T.ws[:], "dws", w=["sw"])
 
     def own_plane(t):
         act(T.tb[:, PL * t:PL * t + PL], T.xt[:].indirect(wu("lm", 26 * t + 26, 26 * t + 51)), F.Copy, ["xt", "lm%d" % t], ["xs%d" % t], scale=0.5)
-        if t % 2 and t // 2 in OPT["dma"]:
+        if t % 2:
+            after("sent")
             a, z, have = PL * (t - 1), PL * (t + 1) - 8, ["xs%d" % (t - 1), "xs%d" % t]
-            made = ["zt%d%d" % (i, k) for i in (t - 1, t) for k in range(3)]
-            select(T.zt[:, a:z], T.tb[:, a:z], [[0, z - a]], A.is_ge, 0, 0, have, made)
-            dma("G", T.zt[:, a:z], T.tb[:, a + 1:z + 1], "dm%d" % (t // 2), r=have, w=made, accum_op=A.add)
+            select(T.zt[:, a:z], T.tb[:, a:z], [[0, z - a]], A.is_ge, 0, 0, have, ["zt%d" % (t // 2)])
+            dma("G", T.zt[:, a:z], T.tb[:, a + 1:z + 1], "dm%d" % (t // 2), r=have, w=["zt%d" % (t // 2)], accum_op=A.add)
 
-    def arrived_keys(between):
-        act(T.gn[:], T.knb[:].indirect(T.lin[:, 0:13]), F.Copy, ["knb", "lin"], ["gn"])
-        between[0]()
+    def signs():
         act(cf(20), T.gn[:, 0:1], F.Sign, ["gn", "sp"], ["xe0"], scale=-1.0, bias=T.sp[:, 1:2])
-        act(T.cf[:, 24:27], T.gn[:, NA - 3:NA], F.Sign, ["gn", "sp"], ["xe1"], scale=-1.0, bias=T.sp[:, C:C + 1])
-        between[1]()
-        act(T.gn[:, 0:1], cf(20), F.Identity, ["xe0"], ["gn0"], scale=H, bias=-2 * H)
-        act(T.gn[:, NA - 3:NA], T.cf[:, 24:27], F.Identity, ["xe1"], ["gn1"], scale=H, bias=2 * H)
+        act(cf(24), T.gn[:, NA - 1:NA], F.Sign, ["gn", "sp"], ["xe1"], scale=-1.0, bias=T.sp[:, C:C + 1])
 
-    def arrived_entries(t):
-        act(T.tb[:, AR + PL * t:AR + PL * t + NA], T.dn[:, C * t:C * t + C].indirect(T.lin[:, 0:13]), F.Copy, ["dn%d" % t, "lin"], ["ds%d" % t])
+    def ends():
+        act(T.sp[:, 0:1], cf(20), F.Identity, ["xe0"], ["sp0"], scale=-H, bias=-1.5 * H)
+        act(T.sp[:, C + 1:C + 2], cf(24), F.Identity, ["xe1"], ["sp1"], scale=-H, bias=2.5 * H)
 
-    def means(t):
-        for k in range(3 if t // 2 not in OPT["dma"] else 0):
-            a, z, o = 129 * k, min(129 * k + 129, C + 1), PL * t
-            spare.append((4, lambda a=a, z=z, o=o, k=k: tt(T.zt[:, 400 * t + a:400 * t + z], T.tb[:, o + a:o + z], T.tb[:, o + a + 1:o + z + 1],
-                                                         A.add, ["xs%d" % t], ["zt%d%d" % (t, k)])))
+    def count_places():
+        quant(T.qb[:], T.sb[:], T.bt[:, B:3 * B], ["btc", "bta", "btb"], ["qb"])
+        mm(1, 128, T.qc[:], T.sc4[:], T.qb[:], T.sb[:], True, True, ["qc", "qb"], ["m1_"])
 
-    def on_scalar_next(k):
-        if k in "abcd":
-            arrived_entries("abcd".index(k))
-        else:
-            own_plane(int(k))
+    def own_offsets(h):
+        for k in range(2):
+            act(T.fd[:, 32 * h + 16 * k + 1:32 * h + 16 * k + 16:2], T["ssc" if SCALARS else "n0"][:, 32 * h + 3:32 * h + 32:4], F.Identity, ["n0"], ["fd%d%d" % (h, k)], bias=OFF + k)
 
-    gaps = list(OPT["gaps"])
+    def queries_in(h, banks):
+        after("knb", "dn0", "dn1", "dn2", "dn3")
+        for b in banks:
+            unit(4 * (1 - h) + b, HB, b, T.qh[:, HB * h:HB * h + HB], T.sh[:, HB * h:HB * h + HB], False, ["qh"], ["d1%d%d" % (h, b)])
 
-    def pause():
-        gap(4 * int(gaps.pop(0)))
+    def note_sent():
+        wrote["sent"] = wrote["lout"]
 
+    step.update({
+        "s1": lambda: act(T.sa1[:], T.mt[:].indirect(T.lst[:, 56:70]), F.Copy, ["mt", "la"], ["sa1"]),
+        "mw": lambda: hold(T.mw[:], T.mt[:, 0:400], T.cp[:], ["mt"] + cp, ["mw"]),
+        "lm": lambda: ts(wu("lm", 0, 25), T.mw[:, 15:400:16], OFF, A.add, r=["mw"], w=["lm"]),
+        "s2": lambda: hold(T.sa2[:], T.sa1[:], T.cp[:, 0:NA + 16], ["sa1"] + cp, ["sa2"]),
+        "lo": lambda: (list_out(), note_sent()),
+        "sp": lambda: act(T.sp[:], T.ksb[:].indirect(wu("lm", 0, 25)), F.Copy, ks + ["lm"], ["sp"]),
+        "ma": lambda: ts(T.mw[:, 15:16], T.mt[:, 1:2], cf(12), A.add, T.mw[:, 15:16], A.min, r=["mt", "cf12", "lm"], w=["mwa"]),
+        "mb": lambda: ts(T.mw[:, 399:400], T.mt[:, C:C + 1], -OFF, A.add, r=["mt", "lm"], w=["mwb"]),
+        "hs": lambda: hold(wf("hs", 0, 32), T.mt[:, 17:520:16], T.cp[:, 0:32], ["mt"] + cp, ["hs"]),
+        "la": lambda: ts(wu("ls", 0, 16), wf("off", 0, 16), wf("hs", 15, 16), A.add, r=["hs", "off"], w=["lsa"]),
+        "lb": lambda: ts(wu("ls", 16, 32), wf("off", 0, 16), wf("hs", 31, 32), A.add, r=["hs", "off"], w=["lsb"]),
+        "sm": lambda: tt(T.sm[:], T.ps3[:, 0:B], T.m0[:, 0:B], A.add, ["ps3", "m0", "srep"], ["sm"]),
+        "ss": lambda: scan(T.ssc[:], T.rs[:, 0:B], T.sm[:], 0.0, A.add, A.min, ["rs", "sm"], ["ssc"]),
+        "sx": lambda: act(T.sm[:], T.ssc[:].indirect(T.lst[:, 8:24]), F.Copy, ["ssc", "lx"], ["sm", "sexp"]),
+        "w0": lambda: spread(T.ws0[:, 0:NS], (T.sp[:, 1:NS + 1], NS), ["sp"], ["ws0a"]),
+        "w1": lambda: spread(T.ws0[:, NS:C], (T.sp[:, NS + 1:C + 1], NS), ["sp"], ["ws0b"]),
+        "ba": lambda: tt(T.bt[:, 0:2 * B:2], T.ksb[:].indirect(wu("ls", 0, 16)), T.sm[:], A.is_lt, ks + ["lsa", "sexp"], ["bta"]),
+        "bb": lambda: tt(T.bt[:, 1:2 * B:2], T.ksb[:].indirect(wu("ls", 16, 32)), T.sm[:], A.is_lt, ks + ["lsb", "sexp"], ["btb"]),
+        "nb": lambda: scan(T.b0s[:], T.r32[:], T.bt[:, 0:2 * B], 0.0, A.min, A.add, ["r32", "bta", "btb"], ["nb"]),
+        "lw": lambda: ts(wu("lo", 0, 16), T.b0s[:, 31:2 * B:32], 16.0, A.mult, 15.0, A.add, r=["nb"], w=["loa"]),
+        "co": lambda: ts(T.cp4[:, 3:64:4], T.b0s[:, 31:2 * B:32], 16.0, A.mult, cf(5), A.add, r=["nb", "cf5", "cp43"], w=["cp4o"]),
+        "bc": lambda: tt(T.bt[:, 2 * B:3 * B], T.ws0[:].indirect(wu("lo", 0, 16)), T.srep[:], A.is_lt, ["ws0a", "ws0b", "loa", "srep"], ["btc"]),
+        "q1": count_places,
+        "n0": lambda: (after("m1_"), hold(T.n0[:], T.ps1[:, 64:128], T.cp4[:, 0:64], ["ps1", "cp4o"] + cp4, ["n0"])),
+        "lc": lambda: ts(wu("lc", 0, 16), own, OFF, A.add, r=["n0"], w=["lca"]),
+        "ld": lambda: ts(wu("lc", 32, 48), own, OFF + 1, A.add, r=["n0"], w=["lcb"]),
+        "gn": lambda: (after("sent"), act(T.gn[:], T.knb[:].indirect(T.lin[:, 0:13]), F.Copy, ["knb", "lin"], ["gn"])),
+        "e0": signs, "e1": ends,
+        "bd": lambda: (after("sent"), tt(T.bt[:, 3 * B:4 * B], T.knb[:].indirect(T.lin[:, 14:30]), T.sm[:], A.is_lt, ["knb", "lin", "sexp"], ["btd"])),
+        "nd": lambda: scan(T.b1s[:], T.rz[:, 0:B], T.bt[:, 3 * B:4 * B], 0.0, A.min, A.add, ["rz", "btd"], ["b1s"]),
+        "le": lambda: ts(wu("l1", 0, 16), bucket, 16.0, A.mult, 15.0, A.add, r=["b1s"], w=["l1"]),
+        "wa": lambda: scan(T.wa[:], T.ms[:], T.gn[:], -6 * H, A.add, A.min, ["ms", "gn"], ["wa0"]),
+        "wb": lambda: ts(T.wa[:, NA - 1:NA], T.wa[:, NA - 1:NA], cf(9), A.add, r=["wa0", "cf9"], w=["wa"]),
+        "p0": lambda: act(wf("pre", 0, 16), bucket, F.Identity, ["b1s"], ["pre0"], scale=16.0, bias=AR - 1.0),
+        "p2": lambda: act(wf("pre", 32, 48), bucket, F.Identity, ["b1s"], ["pre2"], scale=15.0, bias=OFF - 1),
+        "d0": lambda: tt(wf("pre", 16, 32), wf("pre", 0, 16), own, A.subtract, ["pre0", "n0"], ["pre1"]),
+        "U0": lambda: queries_in(0, range(4)), "U1": lambda: queries_in(1, (0, 2)),
+    })
+    def count_buckets():
+        quant(T.qs[:, 0:128], T.ss[:, 0:128], T.bt[:, 0:2 * B], ["bta", "btb"], ["qs0"])
+        mm(1, 128, T.qc[:], T.sc4[:], T.qs[:, 0:128], T.ss[:, 0:128], True, False, ["qc", "qs0", "rk"])
+        mm(1, 128, T.qc[:], T.sc4[:], T.qs[:, 64:192], T.ss[:, 64:192], False, True, ["qc", "qs0"], ["m0_"])
+
+    def count_both():
+        quant(T.qb[:], T.sb[:], T.bt[:, 2 * B:4 * B], ["btc", "btd"], ["qb"])
+        mm(1, 128, T.qc[:], T.sc4[:], T.qb[:], T.sb[:], True, True, ["qc", "qb", "nb"], ["m1_"])
+
+    def short_list():
+        ts(T.lout[:, 0:14], T.sa2[:, 15:NA + 16:16], OFF, A.add, r=["sa2"], w=["lout"])
+        send(prv, T.lin[:, 0:14], T.lout[:, 0:14], "al", ["lout"])
+        dma("Y", by(T.qw[:]), T.wc[:], "dw", r=["lin"], w=["qw"])
+        dma("Y", T.sw[:], T.ws[:], "dws", w=["sw"])
+
+    if SCALARS:
+        own, bucket = T.ssc[:, 3:64:4], T.ssc[:, 67:128:4]
+        step.update({
+            "lo": lambda: (short_list(), note_sent()),
+            "ls": lambda: ts(wu("ls", 0, 2), T.wf[:, WF["hs"] + 15:WF["hs"] + 32:16], OFF, A.add, r=["hs"], w=["ls"]),
+            "gs": lambda: cpy(T.sm[:, 0:32], T.ksb[:].indirect(wu("ls", 0, 2)), ks + ["ls"], ["gs"]),
+            "so": lambda: spread(T.sm[:, 32:56], (T.sm[:, 0:24], 24), ["gs"], ["so"]),
+            "ba": lambda: ts(T.bt[:, 0:B], T.ps3[:, 0:B], T.sm[:, 47:48], A.is_gt, r=["ps3", "so", "srep"], w=["bta"]),
+            "bb": lambda: ts(T.bt[:, B:2 * B], T.ps3[:, 0:B], T.sm[:, 55:56], A.is_gt, r=["ps3", "so", "srep"], w=["btb"]),
+            "q0": count_buckets, "q1": count_both,
+            "nb": lambda: (after("m0_"), hold(T.n0[:], T.ps1[:, 0:64], T.cp4[:, 64:128], ["ps1"] + cp4, ["nb"])),
+            "lw": lambda: ts(wu("lo", 0, 16), T.n0[:, 3:64:4], OFF + 15 / 16, A.add, 16.0, A.mult, r=["nb"], w=["loa"]),
+            "co": lambda: ts(T.cp4[:, 3:64:4], T.n0[:, 3:64:4], 16.0, A.mult, cf(6), A.add, r=["nb", "cf6", "cp43"], w=["cp4o"]),
+            "Su": lambda: act(cf(6), cf(5), F.Identity, ["cf5"], ["cf6"], bias=16 * OFF),
+            "Vg": lambda: ts(cf(10), cf(1), 12.0, A.is_lt, r=["r"], w=["cf10"]),
+            "ga": lambda: (after("sent"), cpy(T.sm[:, 64:96], T.knb[:].indirect(T.lin[:, 12:14]), ["knb", "lin"], ["ga"])),
+            "sa": lambda: spread(T.sm[:, 96:112], (T.sm[:, 80:96], 16), ["ga"], ["sa"]),
+            "bd": lambda: ts(T.bt[:, 3 * B:4 * B], T.ps3[:, 0:B], T.sm[:, 111:112], A.is_gt, cf(10), A.mult, r=["ps3", "sa", "cf10"], w=["btd"]),
+            "n0": lambda: (after("m1_"), hold(T.ssc[:, 0:128], T.ps1[:, 0:128], T.cp4[:, 0:128], ["ps1", "cp4o"], ["n0"])),
+            "le": lambda: ts(wu("l1", 0, 16), bucket, OFF + 15 / 16, A.add, 16.0, A.mult, r=["n0"], w=["l1"]),
+            "p0": lambda: act(wf("pre", 0, 16), bucket, F.Identity, ["n0"], ["pre0"], scale=16.0, bias=16 * OFF + AR - 1.0),
+            "p2": lambda: act(wf("pre", 32, 48), bucket, F.Identity, ["n0"], ["pre2"], scale=15.0, bias=16 * OFF - 1),
+        })
+    step["R99"] = step["Sr"]
+    step["r99"] = lambda: op("S", lambda: S.activation(T.sr[:], T.su[:].indirect(T.lst[:, 0:8]), F.Copy), ["qu", "lu"], ["sr"])
     for t in range(4):
-        plane_list(t)
-    own_plane(0)
-    own_plane(1)
-    planes.pop(0)()
-    fill(T.bt[:, 512:768], 0.0, ["btz"])
-    quant(T.qc[:], T.sc4[:], T.c4[:], ["c4"], ["qc"])
-    tt(T.b0[:], T.sp[:].indirect(T.lst[:, 24:40]), T.sexp[:], A.is_lt, ends + ["lc0", "sexp"], ["b0"])
-    scan(T.ws0[:, 0:NS], T.ms[:, 0:NS], T.sp[:, 1:NS + 1], 0.0, A.add, A.min, ["ms", "sp"], ["ws0a"])
-    scan(T.b0s[:], T.rz[:, 0:B], T.b0[:], 0.0, A.mult, A.add, ["rz", "b0"], ["b0s"])
-    scan(T.ws0[:, NS:C], T.ms[:, 0:NS], T.sp[:, NS + 1:C + 1], 0.0, A.add, A.min, ["ms", "sp"], ["ws0b"])
-    ts(wu("lo", 0, 16), T.b0s[:, 15:B:16], 32.0, A.mult, 15.0, A.add, r=["b0s"], w=["loa"])
-    ts(wu("lo", 16, 32), T.b0s[:, 15:B:16], 32.0, A.mult, 31.0, A.add, r=["b0s"], w=["lob"])
-    ts(T.cp4o[:, 3:64:4], T.b0s[:, 15:B:16], 32.0, A.mult, cf(5), A.add, r=["b0s", "cf5"], w=["cp4o"])
-    arrived_keys([lambda: on_scalar_next(OPT["s1"][0]), lambda: on_scalar_next(OPT["s1"][1])])
-    means(0)
-    pause()
-    tt(T.bt[:, 0:B], T.ws0[:].indirect(wu("lo", 0, 16)), T.srep[:], A.is_lt, ["ws0a", "ws0b", "loa", "srep"], ["bta"])
-    tt(T.bt[:, B:2 * B], T.ws0[:].indirect(wu("lo", 16, 32)), T.srep[:], A.is_lt, ["ws0a", "ws0b", "lob", "srep"], ["btb"])
-    means(1)
-    pause()
-    quant(T.qb[:], T.sb[:], T.bt[:], ["bta", "btb", "btz"], ["qb"])
-    mm(1, 128, T.qc[:], T.sc4[:], T.qb[:, 0:128], T.sb[:, 0:128], True, False, ["qc", "qb"])
-    mm(1, 128, T.qc[:], T.sc4[:], T.qb[:, 64:192], T.sb[:, 64:192], False, True, ["qc", "qb"])
+        step["l%d" % t] = lambda t=t: ts(wu("lm", 26 * t + 26, 26 * t + 51), T.mw[:, 15:400:16], OFF + t / 4, A.add, 4.0, A.mult, r=["mwa", "mwb"], w=["lm%d" % t])
+        step["x%d" % t] = lambda t=t: own_plane(t)
+        step["a%d" % t] = lambda t=t: (after("sent"), act(T.tb[:, AR + PL * t:AR + PL * t + NA], T.dn[:, C * t:C * t + C].indirect(T.lin[:, 0:13]), F.Copy,
+                                                          ["dn%d" % t, "lin"], ["ds%d" % t]))
+    for h in range(2):
+        step["k%d" % h] = lambda h=h: act(T.kl[:, HB * h:HB * h + HB], T.wa[:].indirect(wu("l1", 8 * h, 8 * h + 8)), F.Copy, ["wa", "l1"], ["near%d" % h])
+        step["f%d" % h] = lambda h=h: own_offsets(h)
 
-    tt(T.b1[:], T.gn[:, 8:200].indirect(T.lst[:, 40:56]), T.sexp[:], A.is_lt, ["gn", "lc1", "sexp"], ["b1"])
-    scan(T.wa[:], T.ms[:, 0:NA], T.gn[:], 0.0, A.add, A.min, ["ms", "gn", "gn0", "gn1"], ["wa"])
-    scan(T.b1s[:], T.rz[:, 0:B], T.b1[:], 0.0, A.mult, A.add, ["rz", "b1"], ["b1s"])
-    hold(T.n0[:], T.ps1[:, 0:64], T.cp4o[:], ["ps1", "cp4o"], ["n0"])
-    own, bucket = T.n0[:, 3:64:4], T.b1s[:, 11:B:16]
-    pause()
-    ts(wu("l1", 0, 16), bucket, 16.0, A.mult, 15.0, A.add, r=["b1s"], w=["l1"])
-    ts(wu("lc", 0, 16), own, OFF, A.add, r=["n0"], w=["lca"])
-    ts(wu("lc", 16, 32), own, OFF + 1, A.add, r=["n0"], w=["lcb"])
-    for k in OPT["s2"]:
-        on_scalar_next(k)
-    near = T.wa[:].indirect(wu("l1", 0, 16))
-    act(T.kl[:], near, F.Copy, ["wa", "l1"], ["near"])
-    act(wf("pre", 0, 16), bucket, F.Identity, ["b1s"], ["pre0"], scale=16.0, bias=AR - 1.0)
-    act(T.fd[:, 1:32:2], own, F.Identity, ["n0"], ["fdc"], bias=OFF)
-    act(T.fd[:, 33:64:2], own, F.Identity, ["n0"], ["fdd"], bias=OFF + 1)
-    act(wf("pre", 32, 48), bucket, F.Identity, ["b1s"], ["pre2"], scale=15.0, bias=OFF - 1)
-    for copy_out in planes:
-        copy_out()
-    for k in OPT["s3"]:
-        on_scalar_next(k)
-    for b in (0, 2, 3):
-        unit(b, HB, b, T.qh[:, HB:B], T.sh[:, HB:B], False, ["qh"])
-    for b in range(3):
-        unit(4 + b, HB, b, T.qh[:, 0:HB], T.sh[:, 0:HB], False, ["qh"])
-    pause()
-    means(2)
-    tt(T.bt1[:, B:2 * B], near, T.srep[:], A.is_lt, ["wa", "l1", "srep"], ["bt1b"])
-    pause()
-    tt(T.bt1[:, 0:B], T.sp[:].indirect(wu("lc", 0, 16)), T.kl[:], A.is_gt, ends + ["lca", "near"], ["bt1a"])
-    tt(T.bt1[:, 2 * B:3 * B], T.sp[:].indirect(wu("lc", 16, 32)), T.kl[:], A.is_gt, ends + ["lcb", "near"], ["bt1c"])
-    tt(wf("pre", 16, 32), wf("pre", 0, 16), own, A.subtract, ["pre0", "n0"], ["pre1"])
-    pause()
-    quant(T.qb1[:], T.sb1[:], T.bt1[:], ["bt1a", "bt1b", "bt1c"], ["qb1"])
-    mm(1, 192, T.qc[:], T.sc4[:], T.qb1[:], T.sb1[:], True, True, ["qc", "qb1"])
-    unit(7, HB, 3, T.qh[:, 0:HB], T.sh[:, 0:HB], False, ["qh"])
-    means(3)
-    pause()
-    hold(T.n1[:], T.ps1[:, 0:192], T.cp4[:], ["ps1", "cp4"], ["n1"])
-    unit(1, HB, 1, T.qh[:, HB:B], T.sh[:, HB:B], False, ["qh"])
-    pause()
-    below = T.n1[:, 67:128:4]
-    tt(T.fl[:, 1:64:2], T.n1[:, 3:128:4], T.n1[:, 67:192:4], A.not_equal, ["n1", "flz"], ["fl"])
-    tt(T.fd[:, 0:32:2], below, wf("pre", 16, 32), A.add, ["n1", "pre1"], ["fda"])
-    tt(T.fd[:, 32:64:2], below, wf("pre", 16, 32), A.add, ["n1", "pre1"], ["fdb"])
-    tt(wf("br", 0, 16), below, wf("pre", 32, 48), A.add, ["n1", "pre2"], ["br0"])
-    pause()
-    scan(T.ix[:], T.fl[:], T.fd[:], 0.0, A.mult, A.add, ["fl", "fda", "fdb", "fdc", "fdd"], ["ix"])
-    ts(T.bout[:], wf("br", 0, 16), 2.0, A.mult, 1.0, A.max, r=["br0"], w=["bout"])
-    pause()
-    cpy(wu("li", 0, 32), T.ix[:, 1:64:2], ["ix"], ["li"])
-    send(nxt, T.bin[:], T.bout[:], "ab", ["bout"])
-    pause()
+    def choose(h, k):
+        a, z, o, bank, was = HB * h, HB * (h + 1), 2 * B * h, 1 + 2 * h, [["bta", "btb"], ["btc", "btd"]][h]
+        n1 = lambda s, e: T.n1[:, 96 * h + 32 * s + 3:96 * h + 32 * e:4]
+        if k == 0:
+            tt(T.bt[:, o + HB:o + B], T.wa[:].indirect(wu("l1", 8 * h, 8 * h + 8)), T.srep[:, a:z], A.is_lt, ["wa", "l1", "srep", "qb", "nb"], ["b1b%d" % h])
+        if k in (1, 2):
+            u = k - 1
+            tt(T.bt[:, o + B * u:o + B * u + HB], T.sp[:].indirect(wu("lc", 32 * u + 8 * h, 32 * u + 8 * h + 8)), T.kl[:, a:z], A.is_gt,
+               ["sp", "sp0", "sp1", ["lca", "lcb"][u], "near%d" % h], ["b1%d%d" % (u, h)])
+        if k == 3:
+            quant(T.qb1[:, a:z], T.sb1[:, a:z], T.bt[:, o:o + 2 * B], was + ["b1b%d" % h, "b10%d" % h, "b11%d" % h], ["qb1%d" % h])
+            mm(bank, HB, T.qc[:], T.sc4[:], T.qb1[:, a:z], T.sb1[:, a:z], True, True, ["qc", "qb1%d" % h], ["m2%d" % h])
+        if k == 4:
+            after("m2%d" % h)
+            hold(T.n1[:, 96 * h:96 * h + 96], T["ps%d" % bank][:, 0:96], T.cp4[:, 64:160], ["ps%d" % bank], ["n1%d" % h])
+            queries_in(1, (bank,))
+        if k == 5:
+            tt(T.fl[:, 32 * h + 1:32 * h + 32:2], n1(0, 2), n1(1, 3), A.not_equal, ["n1%d" % h, "flz"], ["fl%d" % h])
+            for u in range(2):
+                tt(T.fd[:, 32 * h + 16 * u:32 * h + 16 * u + 16:2], n1(1, 2), wf("pre", 16 + 8 * h, 24 + 8 * h), A.add, ["n1%d" % h, "pre1"], ["fe%d%d" % (h, u)])
+        if k == 6:
+            scan(T.ix[:, 32 * h:32 * h + 32], T.fl[:, 32 * h:32 * h + 32], T.fd[:, 32 * h:32 * h + 32], 0.0, A.mult, A.add,
+                 ["fl%d" % h] + ["f%s%d%d" % (c, h, u) for c in "de" for u in range(2)], ["ix%d" % h])
+        if k == 7:
+            cpy(wu("li", 16 * h, 16 * h + 16), T.ix[:, 32 * h + 1:32 * h + 32:2], ["ix%d" % h], ["li%d" % h])
+        if k == 8:
+            tt(wf("br", 8 * h, 8 * h + 8), n1(1, 2), wf("pre", 32 + 8 * h, 40 + 8 * h), A.add, ["n1%d" % h, "pre2"], ["br%d" % h])
+
+    def bridges():
+        ts(T.bout[:], wf("br", 0, 16), 2.0, A.mult, 1.0, A.max, r=["br0", "br1"], w=["bout"])
+        send(nxt, T.bin[:], T.bout[:], "ab", ["bout"])
 
     def bank_of(h, b):
         return 4 * (1 - h) + b
@@ -523,16 +531,17 @@ def rank_program(g, core, T, topo):
     def products(s, h):
         quant(half("qz" + s, h), half("sz" + s, h), half("z" + s, h, 4), ["z%s%d%d" % (s, h, t) for t in range(4)], ["qz%s%d" % (s, h)])
         for b in range(4):
+            after("d%s%d%d" % (s, h, b))
             mm(bank_of(h, b), HB, T.qw[:, 128 * b:128 * b + 128], T.sw[:, 128 * b:128 * b + 128], half("qz" + s, h), half("sz" + s, h),
-               False, True, ["qw", "sw", "qz%s%d" % (s, h)])
+               False, True, ["qw", "sw", "qz%s%d" % (s, h)], ["t%s%d%d" % (s, h, b)])
 
-    def results(s, h, on_vector):
-        for b in range(4):
-            bank, out = "ps%d" % bank_of(h, b), T["y" + s][:, 4 * HB * h + b:4 * HB * (h + 1):4]
-            if b in on_vector:
-                ts(out, T[bank][:, 0:HB], 0.03125, A.mult, r=[bank], w=["y%s%d%d" % (s, h, b)])
-            else:
-                act(out, T[bank][:, 0:HB], F.Copy, [bank], ["y%s%d%d" % (s, h, b)], scale=0.03125)
+    def result(s, h, b, on_vector):
+        after("t%s%d%d" % (s, h, b))
+        bank, out = "ps%d" % bank_of(h, b), T["y" + s][:, 4 * HB * h + b:4 * HB * (h + 1):4]
+        if on_vector:
+            ts(out, T[bank][:, 0:HB], 0.03125, A.mult, r=[bank], w=["y%s%d%d" % (s, h, b)])
+        else:
+            act(out, T[bank][:, 0:HB], F.Copy, [bank], ["y%s%d%d" % (s, h, b)], scale=0.03125)
 
     def pack(s, h):
         quant(half("qy" + s, h), half("sy" + s, h), half("y" + s, h, 4), ["y%s%d%d" % (s, h, b) for b in range(4)], ["qy%s%d" % (s, h)])
@@ -544,103 +553,97 @@ def rank_program(g, core, T, topo):
 
     def entries(h, t):
         return (T.tb[:, PL * t:PL * t + AR + NA], T.lb[:, B * t + HB * h:B * t + HB * h + HB],
-                ["xs%d" % k for k in range(t, 4)] + ["ds%d" % k for k in range(t + 1)] + ["li", "gap0", "gap1", "gap2"])
+                ["xs%d" % k for k in range(t, 4)] + ["ds%d" % k for k in range(t + 1)] + ["li%d" % h, "gap0", "gap1", "gap2"])
 
-    def lower(h, t):
+    def lower(h, t, on_vector):
         win, low, have = entries(h, t)
-        move((h, t) in OPT["low"], low, win.indirect(wu("li", 8 * h, 8 * h + 8)), have, ["lb%d%d" % (h, t)])
+        move(on_vector, low, win.indirect(wu("li", 16 * h, 16 * h + 8)), have, ["lb%d%d" % (h, t)])
 
     def upper(h, t):
         win, low, have = entries(h, t)
-        tt(T.z1[:, 4 * HB * h + t:4 * HB * (h + 1):4], win.indirect(wu("li", 16 + 8 * h, 24 + 8 * h)), low, A.add,
+        tt(T.z1[:, 4 * HB * h + t:4 * HB * (h + 1):4], win.indirect(wu("li", 16 * h + 8, 16 * h + 16)), low, A.add,
            have + ["lb%d%d" % (h, t)], ["z1%d%d" % (h, t)])
 
-    for h in range(2):
-        for t in range(4):
-            lower(h, t)
-    for t in sorted(range(4), key=lambda t: (0, t) in OPT["low"]):
-        upper(0, t)
-    upper(1, 0)
-    upper(1, 1)
-    products("1", 0)
-    upper(1, 2)
-    upper(1, 3)
-    results("1", 0, ())
-    fill(T.rz3[:], 1.0, ["rz3"])
-    products("1", 1)
-    fill(T.tq[:, 2:3 * B:3], 0.0, ["tqb"])
-    fill(T.rz3[:, 0:C:48], 0.0, ["rz3"])
-    pause()
-    hand_on(0)
-    results("1", 1, OPT["r11"])
-    hand_on(1)
-    ts(wu("bl", 0, 16), T.bin[:], C - 1.0, A.min, r=["bin"], w=["bl0"])
-    ts(wu("bl", 16, 32), T.bin[:], C - 1.0, A.min, 1.0, A.add, r=["bin"], w=["bl1"])
-    ts(T.tq[:, 2:3 * B:48], T.bin[:], C - 1.0, A.min, -1.0 - NS, A.add, r=["bin"], w=["tqb"])
-    gap()
-    for k in range(2):
-        tt(T.th[:, B * k:B * k + B], T.sp[:].indirect(wu("bl", 16 * k, 16 * k + 16)), T.m0[:, 0:B], A.add, ends + ["bl%d" % k, "m0"], ["th%d" % k])
-    gap(99)
-    quant(T.qv[:], T.sv[:], T.vt[:], ["vt"], ["qv"])
-
-    def units(h, bs):
+    def queries_came(h, bs, bank=None):
+        if bank is not None:
+            after("y11%d" % bank)
+            keys(bank, HB, half("qa", h), half("sa", h), ["qa%d" % h], ["k2%d" % h])
         for b in bs:
-            unit(bank_of(h, b), HB, b, half("qa", h), half("sa", h), False, ["qa%d" % h])
+            after("y1%d%d" % (h, b))
+            unit(bank_of(h, b), HB, b, half("qa", h), half("sa", h), False, ["qa%d" % h], ["d2%d%d" % (h, b)])
 
-    def stage(h, k, bank=None):
-        a, z = HB * h, HB * (h + 1)
+    def bridge_keys(h, k):
+        o = B * k + HB * h
+        tt(T.th[:, o:o + HB], T.sp[:].indirect(wu("bl", 16 * k + 8 * h, 16 * k + 8 * h + 8)), T.m0[:, 0:HB], A.add, ["sp", "sp0", "sp1", "bl%d" % k, "m0"], ["th%d%d" % (h, k)])
+
+    def stage(h, k):
+        a, z, bank = HB * h, HB * (h + 1), "ps%d" % (3 - h)
         if k == 0:
-            tt(T.tq[:, 3 * a:3 * z:3], T["ps%d" % bank][:, 0:HB], T.th[:, a:z], A.is_ge, ["ps%d" % bank, "th0"], ["tql%d" % h])
-            tt(T.tq[:, 3 * a + 1:3 * z:3], T["ps%d" % bank][:, 0:HB], T.th[:, B + a:B + z], A.is_gt, ["ps%d" % bank, "th1"], ["tqu%d" % h])
+            after("k2%d" % h)
+            tt(T.tq[:, 3 * a:3 * z:3], T[bank][:, 0:HB], T.th[:, a:z], A.is_ge, [bank, "th%d0" % h], ["tql%d" % h])
+            tt(T.tq[:, 3 * a + 1:3 * z:3], T[bank][:, 0:HB], T.th[:, B + a:B + z], A.is_gt, [bank, "th%d1" % h], ["tqu%d" % h])
         if k == 1:
-            scan(half("p3s", h, 3), T.rz3[:], half("tq", h, 3), 0.0, A.mult, A.add, ["tql%d" % h, "tqu%d" % h, "tqb", "rz3"], ["p3s%d" % h])
+            scan(half("p3s", h, 3), T.rz3[:], half("tq", h, 3), 0.0, A.mult, A.add, ["tql%d" % h, "tqu%d" % h, "tqb", "rz3b"], ["p3s%d" % h])
         if k == 2:
             ts(wu("lp", 8 * h, 8 * h + 8), T.p3s[:, 3 * a + 47:3 * z:48], float(NS), A.add, r=["p3s%d" % h], w=["lp%d" % h])
 
-    def picks(h, on_vector, which=range(4)):
-        for t in which:
-            move(t in on_vector, T.z2[:, 4 * HB * h + t:4 * HB * (h + 1):4], T.zt[:, 400 * t:400 * t + C + 1].indirect(wu("lp", 8 * h, 8 * h + 8)),
-                 ["zt%d%d" % (t, k) for k in range(3)] + ["lp%d" % h], ["z2%d%d" % (h, t)])
-
-    def places(h):
-        act(half("pv", h), T.jj[:].indirect(wu("lp", 8 * h, 8 * h + 8)), F.Copy, ["jj", "lp%d" % h], ["pv%d" % h])
+    def pick(h, t, on_vector):
+        move(on_vector, T.z2[:, 4 * HB * h + t:4 * HB * (h + 1):4], T.zt[:, 400 * t:400 * t + C + 1].indirect(wu("lp", 8 * h, 8 * h + 8)),
+             ["zt%d" % (t // 2), "lp%d" % h], ["z2%d%d" % (h, t)])
 
     def last(h):
         pack("2", h)
-        mm(4 + h, HB, T.qv[:], T.sv[:], half("qy2", h), half("sy2", h), True, True, ["qv", "qy2%d" % h])
+        after("y20%d" % h)
+        mm(4 + h, HB, T.qv[:], T.sv[:], half("qy2", h), half("sy2", h), True, True, ["qv", "qy2%d" % h], ["yp%d" % h])
         dma("Y", T.oc[:, 4 * HB * h:4 * HB * (h + 1)], by(half("qy2", h)), "so1", r=["qy2%d" % h])
 
-    def store(h):
-        act(half("yo", h), T["ps%d" % (4 + h)][:, 0:HB], F.Copy, ["ps%d" % (4 + h)], ["yo%d" % h])
+    def store(h, on_vector):
+        after("yp%d" % h)
+        move(on_vector, half("yo", h), T["ps%d" % (4 + h)][:, 0:HB], ["ps%d" % (4 + h)], ["yo%d" % h])
         dma("Y", T.y[:, HB * h:HB * (h + 1)], half("yo", h), "so1", r=["yo%d" % h])
 
-    keys(3, HB, half("qa", 0), half("sa", 0), ["qa0"])
-    units(0, range(4))
-    for k in range(3):
-        stage(0, k, 3)
-    keys(2, HB, half("qa", 1), half("sa", 1), ["qa1"])
-    units(1, (0, 1, 3))
-    picks(0, OPT["p0"], (0, 2, 1))
-    stage(1, 0, 2)
-    units(1, (2,))
-    picks(0, OPT["p0"], (3,))
-    places(0)
-    stage(1, 1)
-    stage(1, 2)
-    products("2", 0)
-    picks(1, OPT["p1"])
-    results("2", 0, OPT["r20"])
-    products("2", 1)
-    places(1)
-    dma("Y", T.ov[:], T.pv[0:128:16, :], "so1", r=["pv0", "pv1"])
-    last(0)
-    results("2", 1, OPT["r21"])
-    store(0)
-    last(1)
-    for k in range(4):
-        dma("S", T.osc[4 * k:4 * k + 4, :], T.sy2[32 * k:32 * k + 4, :], "so2", r=["qy20", "qy21"])
-    cpy(half("yo", 1), T.ps5[:, 0:HB], ["ps5"], ["yo1"])
-    dma("Y", T.y[:, HB:B], half("yo", 1), "so1", r=["yo1"])
+    def scales_out():
+        for k in range(4):
+            dma("S", T.osc[4 * k:4 * k + 4, :], T.sy2[32 * k:32 * k + 4, :], "so2", r=["qy20", "qy21"])
+
+    step.update({
+        "br": bridges,
+        "m0": lambda: fill(T.rz3[:], 1.0, ["rz3"]),
+        "m1": lambda: fill(T.tq[:, 2:3 * B:3], 0.0, ["tqz"]),
+        "m2": lambda: op("V", lambda: V.memset(T.rz3[:, 0:C:48], 0.0), ["rz3"], ["rz3b"]),
+        "b0": lambda: (after("bout"), ts(wu("bl", 0, 16), T.bin[:], C - 1.0, A.min, r=["bin"], w=["bl0"])),
+        "b1": lambda: (after("bout"), ts(wu("bl", 16, 32), T.bin[:], C - 1.0, A.min, 1.0, A.add, r=["bin"], w=["bl1"])),
+        "b2": lambda: (after("bout"), ts(T.tq[:, 2:3 * B:48], T.bin[:], C - 1.0, A.min, -1.0 - NS, A.add, r=["bin", "tqz"], w=["tqb"])),
+        "qv": lambda: quant(T.qv[:], T.sv[:], T.vt[:], ["vt"], ["qv"]),
+        "K0": lambda: (after("qy10"), queries_came(0, range(4), 3)),
+        "K1": lambda: (after("tql0", "qy11"), queries_came(1, (0, 1, 3), 2)),
+        "K2": lambda: (after("tql1"), queries_came(1, (2,))),
+        "ov": lambda: dma("Y", T.ov[:], T.pv[0:128:16, :], "so1", r=["pv0", "pv1"]),
+        "sc": scales_out,
+    })
+    for h in range(2):
+        step.update({"z%d" % h: lambda h=h: products("1", h), "h%d" % h: lambda h=h: hand_on(h), "y%d" % h: lambda h=h: products("2", h), "Q%d" % h: lambda h=h: last(h)})
+        for k in range(9):
+            step["c%d%d" % (h, k)] = lambda h=h, k=k: choose(h, k)
+        for k in range(3):
+            step["s%d%d" % (h, k)] = lambda h=h, k=k: stage(h, k)
+        for k in range(2):
+            step["t%d%d" % (h, k)] = lambda h=h, k=k: bridge_keys(h, k)
+        for v in range(2):
+            step["wW"[v] + "%d_" % h] = lambda h=h, v=v: store(h, v)
+            step["vV"[v] + "%d" % h] = lambda h=h, v=v: move(v, half("pv", h), T.jj[:].indirect(wu("lp", 8 * h, 8 * h + 8)), ["jj", "lp%d" % h], ["pv%d" % h])
+            for t in range(4):
+                step["lL"[v] + "%d%d" % (h, t)] = lambda h=h, t=t, v=v: lower(h, t, v)
+                step["rR"[v] + "%d%d" % (h, t)] = lambda h=h, t=t, v=v: result("1", h, t, v)
+                step["oO"[v] + "%d%d" % (h, t)] = lambda h=h, t=t, v=v: result("2", h, t, v)
+                step["gG"[v] + "%d%d" % (h, t)] = lambda h=h, t=t, v=v: pick(h, t, v)
+        for t in range(4):
+            step["u%d%d" % (h, t)] = lambda h=h, t=t: upper(h, t)
+
+    for phase in ORDER.values():
+        for name in phase.split():
+            TRACE.append(("step", name))
+            step[name]()
 
     for e in cnt:
         g.wait_ge(T.sem["e" + e], cnt[e])

from concourse.mybir import dt, AluOpType as A, ActivationFunctionType as F

C, B = 384, 256
HB = B // 2
NS = C // 2
H = 2.0 ** 80
NA = 208
PL = 400
AR = 4 * PL
K = 1024.0
OFF = 2048.0
f32, bf, u16, i32, cod, u8 = "float32", "bfloat16", "uint16", "int32", "float8_e4m3fn_x4", "uint8"

TILES = [(0, 384, [None, 23, 22, 21]), (384, 320, [20, 19, 18, 17]), (704, 256, [16, 15, 14, 13]),
         (960, 192, [12, 11, 10, 9]), (1152, 128, [5, 6, 7, 8]), (1280, 128, [1, 2, 3, 4])]
ON_SCALAR = (23, 22, 21, 20, 12, 11)
LO = 208
TRACE = []
SCALARS = False
PLANE_BANKS = (0, 4, 2, 7)
ORDER = {
    "all": "P2 Gg qu P5 Sr qr Ge xa g1 P0 P1 xb Gf Gj Gr Gc Gv ma_ P4 E0 ka qg A06 A07 mb_ A04 A08 kb A02 A09 A19 A01 A03 A17 j3 qh A05 A18 j1 A14 C5 A13 A15 A16 j2 da j0 A20 Kn D0 A12 A10 A11 B12 B10 A22 A23 B11 B22 A21 B23 B13 B21 B18 sr B17 B09 B15 B16 B19 B20 B14 C4 C3 C1 db j6 j5 C2 C0 dj sm rt E2 cr ss rk qc lq E1 mt D2 n0_ kn ks n2_ cq sx s1 mw hs lm s2 sp mb ma la lb lo l0 l2 l1 bb ba w1 nb w0 lw l3 E3 bc bd x0 x1 x2 gn D1 D3 q1 wa nd wb co le n0 x3 e0 p2 p0 e1 k0 k1 n1_ f1 f0 n3_ a2 a1 a0 a3 c10 lc ld c00 c01 c02 c11 c03 c12 d0 c13 c04 c05 c08 c06 c14 U0 U1 c07 c15 L00 c18 c16 l01 l03 l02 u00 u01 c17 u03 u02 l10 l11 l13 l12 br z0 u10 u11 u13 u12 r00 R01 r02 r03 z1 h0 qv m0 r11 r12 R10 R13 m1 m2 K0 h1 b1 b0 b2 t01 t00 t10 s00 s01 s02 t11 K1 V0 s10 s11 K2 s12 g00 g01 g02 g03 g12 g10 y0 o00 v1 o01 o02 G11 G13 y1 o11 o12 o13 O03 Q0 ov O10 w0_ Q1 W1_ sc",
}
ORDER = {"all": "P5 Gg qu P2 P4 Sr qr Ge xa g1 P1 xb P0 Gc Gf Gv Gj Gr ma_ E0 ka qg A06 A07 mb_ A05 A09 kb da A13 A14 A17 A03 qh A18 db A02 A20 A01 A15 A08 A04 A16 A19 Kn D0 A12 A11 A10 B09 A22 B12 A23 A21 B23 B22 B20 B21 B11 B18 B17 B16 sr B10 B13 B19 B14 B15 C0 j3 C5 C4 j1 C1 dj j2 j0 C2 j5 rt C3 j6 sm cr ss M0 M4 M1 M5 M2 M3 rk E2 lq E1 mt qc D2 ks n0_ kn cq sx n2_ s1 mw hs lm sp s2 ma mb la lb lo l0 l1 ba l2 bb w1 nb w0 lw E3 l3 bc bd x0 x1 x2 gn D1 D3 q1 wa nd co wb le n0 x3 e0 p0 p2 e1 k0 f0 k1 n1_ n3_ a0 a1 a2 f1 a3 c10 lc ld c00 c01 c02 c11 c03 c12 c13 c04 U1 d0 c05 c06 U0 c14 c08 c07 c15 L00 c18 c16 u00 l01 l03 l02 c17 u01 l10 l13 l12 l11 u03 u02 br z0 u13 u10 u11 u12 r00 r01 R02 r03 z1 h0 m0 m1 qv R13 r10 r11 r12 K0 h1 b1 b2 m2 b0 t01 t00 t10 s00 s01 s02 t11 K1 V0 s10 s11 K2 s12 g01 g02 g03 g00 g10 g12 y0 v1 o00 o02 o01 G11 G13 y1 o11 o12 o13 O03 Q0 ov O10 w0_ Q1 W1_ sc"}
ORDER = {"all": "P5 Gg Sm Sq St Ss Sb Sa Sc Sg Sd Se P2 Vb Va Vf Ve P0 Vc P1 P4 qu Sh Si Sj r99 qr xa Sn Sf Sk Sl g1 Gf xb Gb Gz Ge Ga Gj Gc Gh Gv Gr ma_ qg ka mb_ A12 A11 A10 A01 kb A05 B12 B11 A21 A23 A22 B23 B22 B21 A20 A04 A02 A18 A03 A07 db A14 A08 B18 B20 A06 A09 A19 C3 C4 j1 A13 da A17 C0 A16 j3 j0 j2 C1 A15 j5 B19 B10 B17 B14 B09 B13 B15 B16 M0 M4 M1 Kn M3 C5 dj j6 M5 E0 C2 rt M2 D0 E1 qh cr E2 rk Vd E3 lq qc mt ks kn n0_ sr cq D1 D2 D3 n1_ So n2_ s1 sm mw ss lm hs n3_ sx sp Sp s2 mb lb ma lo Gd la l1 l0 l2 x0 x1 bb ba w1 gn x2 a3 e0 nb w0 co lw bd bc nd wa U1 U0 q1 le wb m0 c10 n0 c00 ld k0 lc l3 p0 e1 k1 x3 f1 a2 a1 p2 f0 c02 c01 c11 c03 c12 d0 c13 c04 m2 c05 c14 c06 c15 c07 c08 c16 a0 l02 l00 L01 c18 c17 l03 l11 u01 u02 u00 u03 l10 l12 l13 u11 z0 u12 u13 u10 br r00 r01 r03 R02 z1 r10 h0 m1 R11 r12 R13 h1 b1 b0 b2 t01 t00 t10 K0 s00 t11 s01 s02 K1 s10 s11 s12 G12 K2 g00 g01 g02 g03 g11 g10 y0 G13 qv y1 O00 O01 O02 v0 v1 o03 ov O10 Q0 o11 o13 O12 Q1 w0_ W1_ sc"}
WF = {"pre": 0, "br": 48, "cb": 80, "rt": 104, "rowl": 128, "tla": 152, "off": 184, "hs": 224}
WU = {"lpos": 0, "lo": 24, "lc": 56, "l1": 72, "li": 104, "lp": 136, "bl": 152, "lm": 184, "ls": 316}


def _s(n, d):
    return ("sbuf", [128, n], d)


SCRATCH = {
    "xt": _s(4 * C, bf), "ht": _s(4 * B, bf), "ut": _s(512, bf), "vt": _s(512, bf),
    "qx": _s(C, cod), "sx": _s(C, u8), "qxn": _s(C, cod), "sxn": _s(C, u8),
    "qh": _s(B, cod), "sh": _s(B, u8), "qu": _s(128, cod), "su": _s(128, u8), "qr": _s(128, cod), "sr": _s(128, u8),
    "qv": _s(128, cod), "sv": _s(128, u8), "qw": _s(512, cod), "sw": _s(512, u8),
    "t32": _s(516, bf), "g1a": _s(512, bf), "g1": _s(512, bf), "c4": _s(512, bf), "et": _s(1040, bf),
    "qg": _s(128, cod), "sg": _s(128, u8), "qc": _s(128, cod), "sc4": _s(128, u8), "qe": _s(512, cod), "se": _s(512, u8),
    "ci": _s(8, i32), "cf": _s(40, f32), "ic": _s(32, f32), "jm": _s(400, f32), "jj": _s(400, f32),
    "m0": _s(C, f32), "rz": _s(C, bf), "rs": _s(C, f32), "ms": _s(NA, f32),
    "cp": _s(400, f32), "cp4": _s(160, f32), "rz3": _s(C, bf),
    "wf": _s(320, f32), "wu": _s(348, u16), "lst": _s(72, u16),
    "fl": _s(64, f32), "fd": _s(64, f32), "ix": _s(64, f32),
    "km": _s(C, f32), "kc": _s(C, f32), "ksb": _s(C + 2, f32), "knb": _s(C, f32), "srep": _s(B, f32),
    "ts": _s(4 * 1408, bf), "qs": _s(1408, cod), "ss": _s(1408, u8), "junk": _s(4416, bf), "dj": _s(C, bf), "sj": _s(768, bf),
    "rk": _s(C, f32), "mt": _s(520, f32), "sa1": _s(NA + 16, f32), "sa2": _s(NA + 16, f32), "lout": _s(30, u16), "lin": _s(30, u16), "jm4": _s(160, f32), "sp": _s(400, f32),
    "dn": _s(4 * C, bf), "tb": _s(AR + 3 * PL + NA, bf), "ws0": _s(C, f32),
    "bt": _s(4 * B, bf), "qb": _s(128, cod), "sb": _s(128, u8), "n0": _s(64, f32),
    "sm": _s(B, f32), "ssc": _s(B, f32), "b0s": _s(2 * B, bf), "b1s": _s(B, bf), "r32": _s(2 * B, bf),
    "kl": _s(B, f32), "gn": _s(NA, f32), "mw": _s(400, f32), "wa": _s(NA, f32),
    "qb1": _s(B, cod), "sb1": _s(B, u8), "n1": _s(192, f32), "lb": _s(4 * B, bf),
    "z1": _s(4 * B, bf), "qz1": _s(B, cod), "sz1": _s(B, u8), "y1": _s(4 * B, bf), "qy1": _s(B, cod), "sy1": _s(B, u8),
    "bout": _s(16, u16), "bin": _s(16, u16), "qa": _s(B, cod), "sa": _s(B, u8),
    "zt": _s(1600, bf), "th": _s(2 * B, f32), "tq": _s(3 * B, bf), "p3s": _s(3 * B, bf), "pv": _s(B, f32),
    "z2": _s(4 * B, bf), "qz2": _s(B, cod), "sz2": _s(B, u8), "y2": _s(4 * B, bf), "qy2": _s(B, cod), "sy2": _s(B, u8), "yo": _s(B, f32),
}
for _b in range(8):
    SCRATCH["ps%d" % _b] = ("psum", [128, 512], f32)

SEMAPHORES = ["eV", "eS", "eP", "eG", "dx", "dx2", "du", "dh", "dv", "dw", "dws", "dm0", "dm1", "ax", "al", "ab", "ay0", "ay1", "left", "so1", "so2"]


def rank_program(g, core, T, topo):
    rank = T.rank_of(core)
    if rank is None:
        return
    n = len(T.cores)
    nxt, prv = T.cores[(rank + 1) % n], T.cores[(rank - 1) % n]
    V, S, P = g.vector, g.scalar, g.tensor
    Q = {"V": V, "S": S, "P": P, "G": g, "Y": g.sync}
    cnt = {"V": 0, "S": 0, "P": 0, "G": 0}
    wrote, read, waited = {}, {}, {e: {} for e in Q}

    def need(e, r, w):
        want = {}
        TRACE.append(("need", e, list(r), list(w)))
        for t in list(r) + list(w):
            assert t in wrote or t in w, t
            ds = [wrote[t]] if t in wrote else []
            if t in w or t.startswith("ps"):
                ds = ds + read.get(t, [])
            for sem, c in ds:
                if t.startswith("ps") and sem == "e" + e:
                    continue
                want[sem] = max(want.get(sem, 0), c)
        for sem, c in want.items():
            if waited[e].get(sem, 0) < c:
                Q[e].wait_ge(T.sem[sem], c)
                waited[e][sem] = c

    def note(mark, r, w):
        for t in r:
            read.setdefault(t, []).append(mark)
        for t in w:
            wrote[t] = mark
            read[t] = []

    def op(e, call, r=(), w=()):
        need(e, r, w)
        cnt[e] += 1
        call().then_inc(T.sem["e" + e], 1)
        note(("e" + e, cnt[e]), r, w)

    def after(*names):
        TRACE.append(("after", names))
        for t in names:
            assert t in wrote, t

    dcnt = {}

    def dma(e, out, in_, sem, r=(), w=(), **how):
        need(e, r, w)
        dcnt[sem] = dcnt.get(sem, 0) + 16
        Q[e].dma_start(out, in_, **how).then_inc(T.sem[sem], 16)
        note((sem, dcnt[sem]), r, w)

    def send(dst, out, in_, sem, r):
        need("G", r, ())
        rid, pid = topo.addr(dst)[:2]
        g.remote_dma(out, in_, T.sem[sem], T.sem.left, pid, rid, topo.mask(core, dst))
        dcnt["left"] = dcnt.get("left", 0) + len(topo.engines(core, dst))

    def ts(out, in0, s1, op0, s2=None, op1=None, r=(), w=()):
        if op1 is None:
            op("V", lambda: V.tensor_scalar(out, in0, s1, None, op0), r, w)
        else:
            op("V", lambda: V.tensor_scalar(out, in0, s1, s2, op0, op1), r, w)

    def tt(out, a, b, o, r, w):
        op("V", lambda: V.tensor_tensor(out, a, b, o), r, w)

    def scan(out, d0, d1, init, o0, o1, r, w):
        op("V", lambda: V.tensor_tensor_scan(out, d0, d1, init, o0, o1), r, w)

    def hold(out, data, row, r, w):
        scan(out, data, row, -1.0, A.max, A.add, r, w)

    def spread(out, keys_, r, w):
        scan(out, T.ms[:, 0:keys_[1]], keys_[0], 0.0, A.add, A.min, ["ms"] + r, w)

    def cpy(out, in_, r, w):
        op("V", lambda: V.tensor_copy(out, in_), r, w)

    def fill(ap, c, w):
        op("V", lambda: V.memset(ap, c), (), w)

    def quant(q, s, t, r, w):
        op("V", lambda: V.quantize_mx(q, s, t), r, w)

    def act(out, in_, func, r, w, bias=0.0, scale=1.0, acc=None):
        if func == F.Copy:
            op("S", lambda: S.activation(out, in_, func, scale=scale, accum_out=acc), r, w)
        else:
            op("S", lambda: S.activation(out, in_, func, bias=bias, scale=scale, accum_out=acc), r, w)

    def move(on_vector, out, in_, r, w):
        if on_vector:
            cpy(out, in_, r, w)
        else:
            act(out, in_, F.Copy, r, w)

    def mm(bank, m, lq, ls, rq, rs_, start, stop, r, w=()):
        op("P", lambda: P.matmul_mx(T["ps%d" % bank][:, 0:m], lq, ls, rq, rs_, start, stop), r, ["ps%d" % bank] + list(w))

    def by(v):
        return v.bitcast(dt.uint8)

    def wf(k, a, b):
        return T.wf[:, WF[k] + a:WF[k] + b]

    def wu(k, a, b):
        return T.wu[:, WU[k] + a:WU[k] + b]

    def cf(k):
        return T.cf[:, k:k + 1]

    def unit(bank, m, b, q, s, stop, r, w=()):
        mm(bank, m, T.qe[:, 128 * b:128 * b + 128], T.se[:, 128 * b:128 * b + 128], q, s, True, stop, ["qe%d" % b] + r, w)

    def keys(bank, m, q, s, r, w=()):
        mm(bank, m, T.qr[:], T.sr[:], q, s, True, True, ["qr", "sr"] + r, w)

    en, ep = len(topo.engines(nxt, core)), len(topo.engines(prv, core))
    wrote["qxn"], wrote["lin"], wrote["bin"] = ("ax", 2 * en), ("al", en), ("ab", ep)
    wrote["qa0"], wrote["qa1"] = ("ay0", 2 * ep), ("ay1", 2 * ep)

    dma("S", T.ut[:], T.u[:], "du", w=["ut"])
    dma("Y", T.xt[:, 0:4 * LO], T.x[:, 0:4 * LO], "dx", w=["xta"])
    dma("Y", T.xt[:, 4 * LO:4 * C], T.x[:, 4 * LO:4 * C], "dx2", w=["xt"])
    dma("Y", T.ht[:], T.h[:], "dh", r=["xt"], w=["ht"])

    def iota(out, pat, cm, w, small=True):
        if small:
            op("G", lambda: g.iota(out, pat, 0, cm, allow_small_or_imprecise_dtypes=True), (), w)
        else:
            op("G", lambda: g.iota(out, pat, 0, cm), (), w)

    def select(out, in_, pat, cmp_, base, cm, r, w):
        op("G", lambda: g.affine_select(out, in_, pat, cmp_, 0.0, base, cm), r, w)

    def unit_codes(b):
        o = 520 * (b % 2) + 2 - 2 * (b // 2)
        quant(T.qe[:, 128 * b:128 * b + 128], T.se[:, 128 * b:128 * b + 128], T.et[:, o:o + 512], ["et%d" % (b % 2)], ["qe%d" % b])

    def pad(k):
        lo, wd, blocks = TILES[k]
        fill(T.ts[:, 4 * (lo + 16 * min(c for c in blocks if c)):4 * (lo + wd)], 0.0, ["tz%d" % lo])

    iota(T.ci[:, 0:1], [[0, 1]], 1, ["ci0"], False)
    iota(T.ic[:], [[1, 32]], 0, ["ic"])
    iota(T.jm[:], [[0, 25], [1, 16]], 0, ["jm"])
    fill(T.t32[:], 32.0, ["t32"])
    ts(T.ci[:, 1:2], T.ci[:, 0:1], 15, A.bitwise_and, r=["ci0"], w=["ci1"])
    ts(T.ci[:, 2:3], T.ci[:, 0:1], 15, A.bitwise_and, 2, A.logical_shift_right, r=["ci0"], w=["ci2"])
    ts(T.ci[:, 3:4], T.ci[:, 0:1], 4, A.logical_shift_right, r=["ci0"], w=["ci3"])
    ts(T.lst[:, 0:8], T.ic[:, 0:8], 16.0, A.mult, r=["ic"], w=["lu"])
    pad(3)
    cpy(T.cf[:, 1:4], T.ci[:, 1:4], ["ci1", "ci2", "ci3"], ["r"])

    def level(out, c, w):
        op("G", lambda: g.iota(out, [[0, c[1]]], int(c[0]), 0, allow_small_or_imprecise_dtypes=True), (), w)

    const = {
        "Sa": lambda: act(cf(16), cf(1), F.Identity, ["r"], ["cf16"], scale=-2 * H),
        "Sb": lambda: act(cf(21), cf(1), F.Square, ["r"], ["cf21"], bias=-15.0),
        "Sc": lambda: act(cf(22), cf(2), F.Square, ["r"], ["cf22"], bias=-3.0),
        "Sd": lambda: act(cf(18), cf(1), F.Identity, ["r"], ["cf18"], scale=-K, bias=K / 2),
        "Se": lambda: act(cf(17), cf(1), F.Identity, ["r"], ["cf17"], scale=4 * H, bias=4 * H),
        "Sf": lambda: act(T.rs[:], T.jm[:, 0:C], F.Relu, ["jm"], ["rs"], scale=-4 * H, bias=4 * H),
        "Sg": lambda: act(cf(7), cf(21), F.Identity, ["cf21"], ["cf7"], scale=-K / 2, bias=-OFF),
        "Sh": lambda: act(cf(5), cf(22), F.Identity, ["cf22"], ["cf5"], scale=-K / 2, bias=-OFF),
        "Si": lambda: act(T.m0[:], T.jm[:, 0:C], F.Abs, ["jm", "cf16"], ["m0"], scale=2 * H, bias=cf(16)),
        "Sj": lambda: act(cf(8), cf(1), F.Identity, ["r", "cf7"], ["cf8"], scale=-1.0, bias=cf(7)),
        "Sk": lambda: act(wf("cb", 0, 24), T.ic[:, 1:25], F.Identity, ["ic", "cf8"], ["cb"], scale=16.0, bias=cf(8)),
        "Sl": lambda: act(T.cp[:], T.jm[:], F.Identity, ["jm", "cf18"], ["cp"], scale=K, bias=cf(18)),
        "Sm": lambda: act(cf(19), cf(2), F.Identity, ["r"], ["cf19"], scale=-K, bias=K / 2),
        "Sn": lambda: act(T.ms[:], T.jm[:, 0:NA], F.Relu, ["jm", "cf17"], ["ms"], scale=-4 * H, bias=cf(17)),
        "So": lambda: act(T.cp4[:], T.jm4[:], F.Identity, ["jm4", "cf19"], ["cp40"], scale=K, bias=cf(19)),
        "Sp": lambda: act(T.cp4[:, 3:160:4], T.jm4[:, 0:40], F.Identity, ["jm4", "cf5", "cp40"], ["cp43"], scale=0.0, bias=cf(5)),
        "Sq": lambda: act(cf(12), cf(1), F.Identity, ["r"], ["cf12"], scale=K, bias=-OFF),
        "Ss": lambda: act(cf(9), cf(1), F.Relu, ["r"], ["cf9"], scale=2 * H, bias=-24 * H),
        "St": lambda: act(T.ksb[:, C:C + 2], T.ic[:, 0:2], F.Identity, ["ic"], ["ksa"], scale=4 * H, bias=-H),
        "Va": lambda: ts(wf("tla", 0, 13), T.ic[:, 0:13], 30.0, A.mult, cf(1), A.add, r=["ic", "r"], w=["tla0"]),
        "Vb": lambda: ts(wf("tla", 29, 30), cf(1), 1.0, A.add, 30.0, A.mult, r=["r"], w=["tla2"]),
        "Vc": lambda: ts(wf("tla", 16, 29), wf("tla", 0, 13), cf(1), A.add, 2.0, A.max, r=["tla0"], w=["tla1"]),
        "Vd": lambda: ts(T.lst[:, 56:70], wf("tla", 16, 30), float(C), A.min, r=["tla1", "tla2"], w=["la"]),
        "Ve": lambda: ts(T.lst[:, 8:24], T.ic[:, 0:16], 16.0, A.mult, 15.0, A.add, r=["ic"], w=["lx"]),
        "Vf": lambda: fill(wf("rowl", 0, 1), 0.0, ["rowl0"]),
        "Ga": lambda: (level(T.mt[:, 0:1], (C, 1), ["mtb"]), level(T.mt[:, C:520], (C + 1, 520 - C), ["mta"])),
        "Gb": lambda: (level(wf("off", 0, 16), (OFF, 16), ["off"]), level(T.fl[:], (0, 64), ["flz"])),
        "Gd": lambda: [level(T.tb[:, AR + PL * t + NA:AR + PL * (t + 1)], (0, PL - NA), ["gap%d" % t]) for t in range(3)],
        "Gh": lambda: iota(T.jm4[:], [[0, 40], [1, 4]], 0, ["jm4"]),
        "Gz": lambda: select(T.rz[:], T.t32[:, 0:C], [[0, 24], [1, 16]], A.not_equal, 0, 0, ["t32"], ["rz"]),
    }

    def first_piece():
        quant(T.qx[:, 0:LO], T.sx[:, 0:LO], T.xt[:, 0:4 * LO], ["xta"], ["qxa"])
        keys(0, LO, T.qx[:, 0:LO], T.sx[:, 0:LO], ["qxa"])
        keys(2, LO, T.qx[:, 0:LO], T.sx[:, 0:LO], ["qxa"])

    def masked(a, z, bank, name):
        tt(T.km[:, a:z], T["ps%d" % bank][:, a:z], T.m0[:, a:z], A.add, ["ps%d" % bank, "m0"], ["km" + name])

    def own_key(a, z, name):
        scan(T.kc[:, a:z], T.rs[:, a:z], T.km[:, a:z], 0.0, A.add, A.min, ["rs", "km" + name], ["kc" + name])

    closed = [0]

    def close(k):
        lo, wd, blocks = TILES[k]
        quant(T.qs[:, lo:lo + wd], T.ss[:, lo:lo + wd], T.ts[:, 4 * lo:4 * (lo + wd)],
              ["tz%d" % lo] + (["dga", "dgb"] if k == 0 else []) + ["t%d_%d" % (lo, t) for t in range(4) if blocks[t]], ["qs%d" % lo])

    def columns(k):
        lo, wd, blocks = TILES[k]
        after(*["cs0"] * (k > 0))
        closed[0] += 1
        mm(1, wd, T.qg[:], T.sg[:], T.qs[:, lo:lo + wd], T.ss[:, lo:lo + wd], k == 0, closed[0] == len(TILES), ["qg", "qs%d" % lo], ["cs%d" % k])

    def block(c, second):
        lo, t = [(lo, blocks.index(c)) for lo, wd, blocks in TILES if c in blocks][0]
        name, m = "t%d_%d" % (lo, t), 16 * c
        kc, mine, theirs = ("kca", "ps0", "ps2") if m < LO else ("kcb", "ps6", "ps7")
        bits, key, spare_ = T.ts[:, 4 * lo + t:4 * (lo + m):4], T.kc[:, m + 15:m + 16], T.junk[:, 8 * c * (c - 1):8 * c * (c + 1)]
        if c in ON_SCALAR and not second:
            act(spare_, T[theirs][:, 0:m], F.Sign, [theirs, kc], ["sg%d" % c], scale=-1.0, bias=key)
        elif c in ON_SCALAR:
            act(bits, spare_, F.Relu, ["sg%d" % c, "tz%d" % lo], [name, "rowl%d" % c], scale=-1.0, acc=wf("rowl", c, c + 1))
        elif not second:
            ts(bits, T[mine][:, 0:m], key, A.is_gt, r=[mine, kc, "tz%d" % lo], w=[name, "sg%d" % c])
        else:
            act(spare_, bits, F.Copy, [name], ["rowl%d" % c], acc=wf("rowl", c, c + 1))

    def short_rows(t):
        bits = T.ts[:, 4 * 1152 + t:4 * 1344:4]
        scan(T.sj[:, t:768:4], bits, bits, 0.0, A.add, A.max, ["tz1152", "tz1280", "t1152_%d" % t, "t1280_%d" % t], ["sj%d" % t])

    def diagonal(a, z, bank, name):
        tt(T.ts[:, 4 * a:4 * z:4], T["ps%d" % bank][:, a:z], T.kc[:, a:z], A.is_ge, ["ps%d" % bank, "kc" + name, "tz0"], ["dg" + name])

    def second_piece():
        quant(T.qx[:, LO:C], T.sx[:, LO:C], T.xt[:, 4 * LO:4 * C], ["xt"], ["qx"])
        keys(6, C, T.qx[:], T.sx[:], ["qxa", "qx"])
        keys(7, C, T.qx[:], T.sx[:], ["qxa", "qx"])
        send(prv, by(T.qxn[:]), by(T.qx[:]), "ax", ["qxa", "qx"])
        send(prv, T.sxn[:], T.sx[:], "ax", ["qxa", "qx"])

    def free(bank):
        low, high = [c for c in range(1, 24) if 16 * c < LO], [c for c in range(1, 24) if 16 * c >= LO]
        after(*{0: ["dga"] + ["sg%d" % c for c in low if c not in ON_SCALAR], 2: ["sg%d" % c for c in low if c in ON_SCALAR], 4: [],
                6: ["dgb"] + ["sg%d" % c for c in high if c not in ON_SCALAR], 7: ["ksb"] + ["sg%d" % c for c in high if c in ON_SCALAR]}[bank])

    sj = ["sj%d" % t for t in range(4)]
    step = {
        "Ge": lambda: select(T.et[:, 0:516], T.t32[:], [[-1, 516]], A.is_equal, 2, 4, ["t32"], ["et0"]),
        "Gf": lambda: select(T.et[:, 520:1036], T.t32[:], [[-1, 516]], A.is_equal, 3, 4, ["t32"], ["et1"]),
        "Gg": lambda: iota(T.g1a[:], [[1, 8], [0, 64]], 0, ["g1a"]),
        "Gr": lambda: select(T.r32[:], T.t32[:, 0:512], [[0, 16], [1, 32]], A.not_equal, 0, 0, ["t32"], ["r32"]),
        "Gj": lambda: iota(T.jj[:], [[1, 400]], 0, ["jj"]),
        "Gc": lambda: select(T.c4[:], T.g1[:], [[0, 32], [1, 4], [-1, 4]], A.is_equal, 0, 0, ["g1"], ["c4"]),
        "Gv": lambda: (after("qx"), dma("G", T.vt[:], T.v[:], "dv", w=["vt"])),
        "g1": lambda: ts(T.g1[:], T.g1a[:], cf(3), A.is_equal, r=["g1a", "r"], w=["g1"]),
        "qu": lambda: quant(T.qu[:], T.su[:], T.ut[:], ["ut"], ["qu"]),
        "qr": lambda: cpy(T.qr[:].bitcast(dt.uint32), T.qu[:].bitcast(dt.uint32).indirect(T.lst[:, 0:8]), ["qu", "lu"], ["qr"]),
        "Sr": lambda: cpy(T.sr[:], T.su[:].indirect(T.lst[:, 0:8]), ["qu", "lu"], ["sr"]),
        "P0": lambda: pad(0), "P1": lambda: pad(1), "P2": lambda: pad(2), "P4": lambda: pad(4), "P5": lambda: pad(5),
        "xa": first_piece,
        "ma_": lambda: masked(0, LO, 0, "a"), "mb_": lambda: masked(LO, C, 6, "b"), "ka": lambda: own_key(0, LO, "a"), "kb": lambda: own_key(LO, C, "b"),
        "da": lambda: diagonal(0, LO, 0, "a"), "db": lambda: diagonal(LO, C, 6, "b"), "xb": second_piece,
        "qg": lambda: quant(T.qg[:], T.sg[:], T.g1[:], ["g1"], ["qg"]),
        "qc": lambda: quant(T.qc[:], T.sc4[:], T.c4[:], ["c4"], ["qc"]),
        "dj": lambda: scan(T.dj[:], T.rz[:], T.ts[:, 0:4 * C:4], 0.0, A.min, A.add, ["rz", "dga", "dgb"], ["dj"]),
        "rt": lambda: tt(wf("rt", 0, 24), wf("cb", 0, 24), T.dj[:, 15:C:16], A.subtract, ["cb", "dj"], ["rt"]),
        "j5": lambda: cpy(wf("rowl", 5, 9), T.sj[:, 508:512], sj, ["rowl5"]),
        "j6": lambda: tt(wf("rowl", 1, 5), T.sj[:, 764:768], T.sj[:, 508:512], A.subtract, sj, ["rowl1"]),
        "cr": lambda: tt(T.cp[:, 15:C:16], wf("rt", 0, 24), wf("rowl", 0, 24), A.subtract,
                         ["rt", "cp"] + ["rowl%d" % c for c in [0, 1, 5] + list(range(9, 24))], ["cp15"]),
        "rk": lambda: (after(*["cs%d" % k for k in range(len(TILES))]), hold(T.rk[:], T.ps1[:, 0:C], T.cp[:, 0:C], ["ps1", "cp", "cp15"], ["rk"])),
        "lq": lambda: ts(wu("lpos", 0, 24), T.rk[:, 15:C:16], OFF, A.add, r=["rk"], w=["lpos"]),
        "mt": lambda: cpy(T.mt[:].indirect(wu("lpos", 0, 24)), T.jj[:, 0:C], ["lpos", "jj", "mta", "mtb"], ["mt"]),
        "cq": lambda: act(T.cp[:, 15:400:16], T.ic[:, 0:25], F.Identity, ["ic", "cf7", "rk"], ["cp15", "cq"], scale=0.0, bias=cf(7)),
        "ks": lambda: act(T.ksb[:, 0:C], T.ps7[:, 0:C], F.Copy, ["ps7"], ["ksb"]),
        "qh": lambda: (quant(T.qh[:], T.sh[:], T.ht[:], ["ht"], ["qh"]), keys(3, B, T.qh[:], T.sh[:], ["qh"])),
        "sr": lambda: act(T.srep[:], T.ps3[:, 0:B], F.Copy, ["ps3"], ["srep"]),
        "Kn": lambda: (after("qx"), keys(5, C, T.qxn[:], T.sxn[:], ["qxn"])),
        "kn": lambda: act(T.knb[:], T.ps5[:, 0:C], F.Copy, ["ps5"], ["knb"]),
    }
    for c in range(1, 24):
        step["A%02d" % c] = lambda c=c: block(c, False)
        step["B%02d" % c] = lambda c=c: block(c, True)
    for k in range(len(TILES)):
        step["C%d" % k] = lambda k=k: close(k)
        step["M%d" % k] = lambda k=k: columns(k)
    for t, bank in enumerate(PLANE_BANKS):
        step["j%d" % t] = lambda t=t: short_rows(t)
        step["E%d" % t] = lambda t=t: unit_codes(t)
        step["D%d" % t] = lambda t=t, bank=bank: (after("qx"), free(bank), unit(bank, C, t, T.qxn[:], T.sxn[:], True, ["qxn"], ["pn%d" % t]))
        step["n%d_" % t] = lambda t=t, bank=bank: (after("pn%d" % t), act(T.dn[:, C * t:C * t + C], T["ps%d" % bank][:, 0:C], F.Copy, ["ps%d" % bank], ["dn%d" % t], scale=1.0 / 64))

    step.update(const)
    cp, cp4, ks = ["cp", "cq"], ["cp40", "cp43"], ["ksb", "ksa"]
    own, bucket = T.n0[:, 3:64:4], T.b1s[:, 11:B:16]

    def list_out():
        ts(T.lout[:, 0:14], T.sa2[:, 15:NA + 16:16], OFF, A.add, r=["sa2"], w=["lout"])
        ts(T.lout[:, 14:30], wf("off", 0, 16), T.sa2[:, NA + 15:NA + 16], A.add, r=["sa2", "off"], w=["lout2"])
        send(prv, T.lin[:], T.lout[:], "al", ["lout", "lout2"])
        dma("Y", by(T.qw[:]), T.wc[:], "dw", r=["lin"], w=["qw"])
        dma("Y", T.sw[:], T.ws[:], "dws", w=["sw"])

    def own_plane(t):
        act(T.tb[:, PL * t:PL * t + PL], T.xt[:].indirect(wu("lm", 26 * t + 26, 26 * t + 51)), F.Copy, ["xt", "lm%d" % t], ["xs%d" % t], scale=0.5)
        if t % 2:
            after("sent")
            a, z, have = PL * (t - 1), PL * (t + 1) - 8, ["xs%d" % (t - 1), "xs%d" % t]
            select(T.zt[:, a:z], T.tb[:, a:z], [[0, z - a]], A.is_ge, 0, 0, have, ["zt%d" % (t // 2)])
            dma("G", T.zt[:, a:z], T.tb[:, a + 1:z + 1], "dm%d" % (t // 2), r=have, w=["zt%d" % (t // 2)], accum_op=A.add)

    def signs():
        act(cf(20), T.gn[:, 0:1], F.Sign, ["gn", "sp"], ["xe0"], scale=-1.0, bias=T.sp[:, 1:2])
        act(cf(24), T.gn[:, NA - 1:NA], F.Sign, ["gn", "sp"], ["xe1"], scale=-1.0, bias=T.sp[:, C:C + 1])

    def ends():
        act(T.sp[:, 0:1], cf(20), F.Identity, ["xe0"], ["sp0"], scale=-H, bias=-1.5 * H)
        act(T.sp[:, C + 1:C + 2], cf(24), F.Identity, ["xe1"], ["sp1"], scale=-H, bias=2.5 * H)

    def count_places():
        quant(T.qb[:], T.sb[:], T.bt[:, B:3 * B], ["btc", "bta", "btb"], ["qb"])
        mm(1, 128, T.qc[:], T.sc4[:], T.qb[:], T.sb[:], True, True, ["qc", "qb"], ["m1_"])

    def own_offsets(h):
        for k in range(2):
            act(T.fd[:, 32 * h + 16 * k + 1:32 * h + 16 * k + 16:2], T["ssc" if SCALARS else "n0"][:, 32 * h + 3:32 * h + 32:4], F.Identity, ["n0"], ["fd%d%d" % (h, k)], bias=OFF + k)

    def queries_in(h, banks):
        after("knb", "dn0", "dn1", "dn2", "dn3")
        for b in banks:
            unit(4 * (1 - h) + b, HB, b, T.qh[:, HB * h:HB * h + HB], T.sh[:, HB * h:HB * h + HB], False, ["qh"], ["d1%d%d" % (h, b)])

    def note_sent():
        wrote["sent"] = wrote["lout"]

    step.update({
        "s1": lambda: act(T.sa1[:], T.mt[:].indirect(T.lst[:, 56:70]), F.Copy, ["mt", "la"], ["sa1"]),
        "mw": lambda: hold(T.mw[:], T.mt[:, 0:400], T.cp[:], ["mt"] + cp, ["mw"]),
        "lm": lambda: ts(wu("lm", 0, 25), T.mw[:, 15:400:16], OFF, A.add, r=["mw"], w=["lm"]),
        "s2": lambda: hold(T.sa2[:], T.sa1[:], T.cp[:, 0:NA + 16], ["sa1"] + cp, ["sa2"]),
        "lo": lambda: (list_out(), note_sent()),
        "sp": lambda: act(T.sp[:], T.ksb[:].indirect(wu("lm", 0, 25)), F.Copy, ks + ["lm"], ["sp"]),
        "ma": lambda: ts(T.mw[:, 15:16], T.mt[:, 1:2], cf(12), A.add, T.mw[:, 15:16], A.min, r=["mt", "cf12", "lm"], w=["mwa"]),
        "mb": lambda: ts(T.mw[:, 399:400], T.mt[:, C:C + 1], -OFF, A.add, r=["mt", "lm"], w=["mwb"]),
        "hs": lambda: hold(wf("hs", 0, 32), T.mt[:, 17:520:16], T.cp[:, 0:32], ["mt"] + cp, ["hs"]),
        "la": lambda: ts(wu("ls", 0, 16), wf("off", 0, 16), wf("hs", 15, 16), A.add, r=["hs", "off"], w=["lsa"]),
        "lb": lambda: ts(wu("ls", 16, 32), wf("off", 0, 16), wf("hs", 31, 32), A.add, r=["hs", "off"], w=["lsb"]),
        "sm": lambda: tt(T.sm[:], T.ps3[:, 0:B], T.m0[:, 0:B], A.add, ["ps3", "m0", "srep"], ["sm"]),
        "ss": lambda: scan(T.ssc[:], T.rs[:, 0:B], T.sm[:], 0.0, A.add, A.min, ["rs", "sm"], ["ssc"]),
        "sx": lambda: act(T.sm[:], T.ssc[:].indirect(T.lst[:, 8:24]), F.Copy, ["ssc", "lx"], ["sm", "sexp"]),
        "w0": lambda: spread(T.ws0[:, 0:NS], (T.sp[:, 1:NS + 1], NS), ["sp"], ["ws0a"]),
        "w1": lambda: spread(T.ws0[:, NS:C], (T.sp[:, NS + 1:C + 1], NS), ["sp"], ["ws0b"]),
        "ba": lambda: tt(T.bt[:, 0:2 * B:2], T.ksb[:].indirect(wu("ls", 0, 16)), T.sm[:], A.is_lt, ks + ["lsa", "sexp"], ["bta"]),
        "bb": lambda: tt(T.bt[:, 1:2 * B:2], T.ksb[:].indirect(wu("ls", 16, 32)), T.sm[:], A.is_lt, ks + ["lsb", "sexp"], ["btb"]),
        "nb": lambda: scan(T.b0s[:], T.r32[:], T.bt[:, 0:2 * B], 0.0, A.min, A.add, ["r32", "bta", "btb"], ["nb"]),
        "lw": lambda: ts(wu("lo", 0, 16), T.b0s[:, 31:2 * B:32], 16.0, A.mult, 15.0, A.add, r=["nb"], w=["loa"]),
        "co": lambda: ts(T.cp4[:, 3:64:4], T.b0s[:, 31:2 * B:32], 16.0, A.mult, cf(5), A.add, r=["nb", "cf5", "cp43"], w=["cp4o"]),
        "bc": lambda: tt(T.bt[:, 2 * B:3 * B], T.ws0[:].indirect(wu("lo", 0, 16)), T.srep[:], A.is_lt, ["ws0a", "ws0b", "loa", "srep"], ["btc"]),
        "q1": count_places,
        "n0": lambda: (after("m1_"), hold(T.n0[:], T.ps1[:, 64:128], T.cp4[:, 0:64], ["ps1", "cp4o"] + cp4, ["n0"])),
        "lc": lambda: ts(wu("lc", 0, 16), own, OFF, A.add, r=["n0"], w=["lca"]),
        "ld": lambda: ts(wu("lc", 32, 48), own, OFF + 1, A.add, r=["n0"], w=["lcb"]),
        "gn": lambda: (after("sent"), act(T.gn[:], T.knb[:].indirect(T.lin[:, 0:13]), F.Copy, ["knb", "lin"], ["gn"])),
        "e0": signs, "e1": ends,
        "bd": lambda: (after("sent"), tt(T.bt[:, 3 * B:4 * B], T.knb[:].indirect(T.lin[:, 14:30]), T.sm[:], A.is_lt, ["knb", "lin", "sexp"], ["btd"])),
        "nd": lambda: scan(T.b1s[:], T.rz[:, 0:B], T.bt[:, 3 * B:4 * B], 0.0, A.min, A.add, ["rz", "btd"], ["b1s"]),
        "le": lambda: ts(wu("l1", 0, 16), bucket, 16.0, A.mult, 15.0, A.add, r=["b1s"], w=["l1"]),
        "wa": lambda: scan(T.wa[:], T.ms[:], T.gn[:], -6 * H, A.add, A.min, ["ms", "gn"], ["wa0"]),
        "wb": lambda: ts(T.wa[:, NA - 1:NA], T.wa[:, NA - 1:NA], cf(9), A.add, r=["wa0", "cf9"], w=["wa"]),
        "p0": lambda: act(wf("pre", 0, 16), bucket, F.Identity, ["b1s"], ["pre0"], scale=16.0, bias=AR - 1.0),
        "p2": lambda: act(wf("pre", 32, 48), bucket, F.Identity, ["b1s"], ["pre2"], scale=15.0, bias=OFF - 1),
        "d0": lambda: tt(wf("pre", 16, 32), wf("pre", 0, 16), own, A.subtract, ["pre0", "n0"], ["pre1"]),
        "U0": lambda: queries_in(0, range(4)), "U1": lambda: queries_in(1, (0, 2)),
    })
    def count_buckets():
        quant(T.qs[:, 0:128], T.ss[:, 0:128], T.bt[:, 0:2 * B], ["bta", "btb"], ["qs0"])
        mm(1, 128, T.qc[:], T.sc4[:], T.qs[:, 0:128], T.ss[:, 0:128], True, False, ["qc", "qs0", "rk"])
        mm(1, 128, T.qc[:], T.sc4[:], T.qs[:, 64:192], T.ss[:, 64:192], False, True, ["qc", "qs0"], ["m0_"])

    def count_both():
        quant(T.qb[:], T.sb[:], T.bt[:, 2 * B:4 * B], ["btc", "btd"], ["qb"])
        mm(1, 128, T.qc[:], T.sc4[:], T.qb[:], T.sb[:], True, True, ["qc", "qb", "nb"], ["m1_"])

    def short_list():
        ts(T.lout[:, 0:14], T.sa2[:, 15:NA + 16:16], OFF, A.add, r=["sa2"], w=["lout"])
        send(prv, T.lin[:, 0:14], T.lout[:, 0:14], "al", ["lout"])
        dma("Y", by(T.qw[:]), T.wc[:], "dw", r=["lin"], w=["qw"])
        dma("Y", T.sw[:], T.ws[:], "dws", w=["sw"])

    if SCALARS:
        own, bucket = T.ssc[:, 3:64:4], T.ssc[:, 67:128:4]
        step.update({
            "lo": lambda: (short_list(), note_sent()),
            "ls": lambda: ts(wu("ls", 0, 2), T.wf[:, WF["hs"] + 15:WF["hs"] + 32:16], OFF, A.add, r=["hs"], w=["ls"]),
            "gs": lambda: cpy(T.sm[:, 0:32], T.ksb[:].indirect(wu("ls", 0, 2)), ks + ["ls"], ["gs"]),
            "so": lambda: spread(T.sm[:, 32:56], (T.sm[:, 0:24], 24), ["gs"], ["so"]),
            "ba": lambda: ts(T.bt[:, 0:B], T.ps3[:, 0:B], T.sm[:, 47:48], A.is_gt, r=["ps3", "so", "srep"], w=["bta"]),
            "bb": lambda: ts(T.bt[:, B:2 * B], T.ps3[:, 0:B], T.sm[:, 55:56], A.is_gt, r=["ps3", "so", "srep"], w=["btb"]),
            "q0": count_buckets, "q1": count_both,
            "nb": lambda: (after("m0_"), hold(T.n0[:], T.ps1[:, 0:64], T.cp4[:, 64:128], ["ps1"] + cp4, ["nb"])),
            "lw": lambda: ts(wu("lo", 0, 16), T.n0[:, 3:64:4], OFF + 15 / 16, A.add, 16.0, A.mult, r=["nb"], w=["loa"]),
            "co": lambda: ts(T.cp4[:, 3:64:4], T.n0[:, 3:64:4], 16.0, A.mult, cf(6), A.add, r=["nb", "cf6", "cp43"], w=["cp4o"]),
            "Su": lambda: act(cf(6), cf(5), F.Identity, ["cf5"], ["cf6"], bias=16 * OFF),
            "Vg": lambda: ts(cf(10), cf(1), 12.0, A.is_lt, r=["r"], w=["cf10"]),
            "ga": lambda: (after("sent"), cpy(T.sm[:, 64:96], T.knb[:].indirect(T.lin[:, 12:14]), ["knb", "lin"], ["ga"])),
            "sa": lambda: spread(T.sm[:, 96:112], (T.sm[:, 80:96], 16), ["ga"], ["sa"]),
            "bd": lambda: ts(T.bt[:, 3 * B:4 * B], T.ps3[:, 0:B], T.sm[:, 111:112], A.is_gt, cf(10), A.mult, r=["ps3", "sa", "cf10"], w=["btd"]),
            "n0": lambda: (after("m1_"), hold(T.ssc[:, 0:128], T.ps1[:, 0:128], T.cp4[:, 0:128], ["ps1", "cp4o"], ["n0"])),
            "le": lambda: ts(wu("l1", 0, 16), bucket, OFF + 15 / 16, A.add, 16.0, A.mult, r=["n0"], w=["l1"]),
            "p0": lambda: act(wf("pre", 0, 16), bucket, F.Identity, ["n0"], ["pre0"], scale=16.0, bias=16 * OFF + AR - 1.0),
            "p2": lambda: act(wf("pre", 32, 48), bucket, F.Identity, ["n0"], ["pre2"], scale=15.0, bias=16 * OFF - 1),
        })
    step["R99"] = step["Sr"]
    step["r99"] = lambda: op("S", lambda: S.activation(T.sr[:], T.su[:].indirect(T.lst[:, 0:8]), F.Copy), ["qu", "lu"], ["sr"])
    for t in range(4):
        step["l%d" % t] = lambda t=t: ts(wu("lm", 26 * t + 26, 26 * t + 51), T.mw[:, 15:400:16], OFF + t / 4, A.add, 4.0, A.mult, r=["mwa", "mwb"], w=["lm%d" % t])
        step["x%d" % t] = lambda t=t: own_plane(t)
        step["a%d" % t] = lambda t=t: (after("sent"), act(T.tb[:, AR + PL * t:AR + PL * t + NA], T.dn[:, C * t:C * t + C].indirect(T.lin[:, 0:13]), F.Copy,
                                                          ["dn%d" % t, "lin"], ["ds%d" % t]))
    for h in range(2):
        step["k%d" % h] = lambda h=h: act(T.kl[:, HB * h:HB * h + HB], T.wa[:].indirect(wu("l1", 8 * h, 8 * h + 8)), F.Copy, ["wa", "l1"], ["near%d" % h])
        step["f%d" % h] = lambda h=h: own_offsets(h)

    def choose(h, k):
        a, z, o, bank, was = HB * h, HB * (h + 1), 2 * B * h, 1 + 2 * h, [["bta", "btb"], ["btc", "btd"]][h]
        n1 = lambda s, e: T.n1[:, 96 * h + 32 * s + 3:96 * h + 32 * e:4]
        if k == 0:
            tt(T.bt[:, o + HB:o + B], T.wa[:].indirect(wu("l1", 8 * h, 8 * h + 8)), T.srep[:, a:z], A.is_lt, ["wa", "l1", "srep", "qb", "nb"], ["b1b%d" % h])
        if k in (1, 2):
            u = k - 1
            tt(T.bt[:, o + B * u:o + B * u + HB], T.sp[:].indirect(wu("lc", 32 * u + 8 * h, 32 * u + 8 * h + 8)), T.kl[:, a:z], A.is_gt,
               ["sp", "sp0", "sp1", ["lca", "lcb"][u], "near%d" % h], ["b1%d%d" % (u, h)])
        if k == 3:
            quant(T.qb1[:, a:z], T.sb1[:, a:z], T.bt[:, o:o + 2 * B], was + ["b1b%d" % h, "b10%d" % h, "b11%d" % h], ["qb1%d" % h])
            mm(bank, HB, T.qc[:], T.sc4[:], T.qb1[:, a:z], T.sb1[:, a:z], True, True, ["qc", "qb1%d" % h], ["m2%d" % h])
        if k == 4:
            after("m2%d" % h)
            hold(T.n1[:, 96 * h:96 * h + 96], T["ps%d" % bank][:, 0:96], T.cp4[:, 64:160], ["ps%d" % bank], ["n1%d" % h])
            queries_in(1, (bank,))
        if k == 5:
            tt(T.fl[:, 32 * h + 1:32 * h + 32:2], n1(0, 2), n1(1, 3), A.not_equal, ["n1%d" % h, "flz"], ["fl%d" % h])
            for u in range(2):
                tt(T.fd[:, 32 * h + 16 * u:32 * h + 16 * u + 16:2], n1(1, 2), wf("pre", 16 + 8 * h, 24 + 8 * h), A.add, ["n1%d" % h, "pre1"], ["fe%d%d" % (h, u)])
        if k == 6:
            scan(T.ix[:, 32 * h:32 * h + 32], T.fl[:, 32 * h:32 * h + 32], T.fd[:, 32 * h:32 * h + 32], 0.0, A.mult, A.add,
                 ["fl%d" % h] + ["f%s%d%d" % (c, h, u) for c in "de" for u in range(2)], ["ix%d" % h])
        if k == 7:
            cpy(wu("li", 16 * h, 16 * h + 16), T.ix[:, 32 * h + 1:32 * h + 32:2], ["ix%d" % h], ["li%d" % h])
        if k == 8:
            tt(wf("br", 8 * h, 8 * h + 8), n1(1, 2), wf("pre", 32 + 8 * h, 40 + 8 * h), A.add, ["n1%d" % h, "pre2"], ["br%d" % h])

    def bridges():
        ts(T.bout[:], wf("br", 0, 16), 2.0, A.mult, 1.0, A.max, r=["br0", "br1"], w=["bout"])
        send(nxt, T.bin[:], T.bout[:], "ab", ["bout"])

    def bank_of(h, b):
        return 4 * (1 - h) + b

    def half(name, h, k=1):
        return T[name][:, k * HB * h:k * HB * (h + 1)]

    def products(s, h):
        quant(half("qz" + s, h), half("sz" + s, h), half("z" + s, h, 4), ["z%s%d%d" % (s, h, t) for t in range(4)], ["qz%s%d" % (s, h)])
        for b in range(4):
            after("d%s%d%d" % (s, h, b))
            mm(bank_of(h, b), HB, T.qw[:, 128 * b:128 * b + 128], T.sw[:, 128 * b:128 * b + 128], half("qz" + s, h), half("sz" + s, h),
               False, True, ["qw", "sw", "qz%s%d" % (s, h)], ["t%s%d%d" % (s, h, b)])

    def result(s, h, b, on_vector):
        after("t%s%d%d" % (s, h, b))
        bank, out = "ps%d" % bank_of(h, b), T["y" + s][:, 4 * HB * h + b:4 * HB * (h + 1):4]
        if on_vector:
            ts(out, T[bank][:, 0:HB], 0.03125, A.mult, r=[bank], w=["y%s%d%d" % (s, h, b)])
        else:
            act(out, T[bank][:, 0:HB], F.Copy, [bank], ["y%s%d%d" % (s, h, b)], scale=0.03125)

    def pack(s, h):
        quant(half("qy" + s, h), half("sy" + s, h), half("y" + s, h, 4), ["y%s%d%d" % (s, h, b) for b in range(4)], ["qy%s%d" % (s, h)])

    def hand_on(h):
        pack("1", h)
        send(nxt, by(half("qa", h)), by(half("qy1", h)), "ay%d" % h, ["qy1%d" % h])
        send(nxt, half("sa", h), half("sy1", h), "ay%d" % h, ["qy1%d" % h])

    def entries(h, t):
        return (T.tb[:, PL * t:PL * t + AR + NA], T.lb[:, B * t + HB * h:B * t + HB * h + HB],
                ["xs%d" % k for k in range(t, 4)] + ["ds%d" % k for k in range(t + 1)] + ["li%d" % h, "gap0", "gap1", "gap2"])

    def lower(h, t, on_vector):
        win, low, have = entries(h, t)
        move(on_vector, low, win.indirect(wu("li", 16 * h, 16 * h + 8)), have, ["lb%d%d" % (h, t)])

    def upper(h, t):
        win, low, have = entries(h, t)
        tt(T.z1[:, 4 * HB * h + t:4 * HB * (h + 1):4], win.indirect(wu("li", 16 * h + 8, 16 * h + 16)), low, A.add,
           have + ["lb%d%d" % (h, t)], ["z1%d%d" % (h, t)])

    def queries_came(h, bs, bank=None):
        if bank is not None:
            after("y11%d" % bank)
            keys(bank, HB, half("qa", h), half("sa", h), ["qa%d" % h], ["k2%d" % h])
        for b in bs:
            after("y1%d%d" % (h, b))
            unit(bank_of(h, b), HB, b, half("qa", h), half("sa", h), False, ["qa%d" % h], ["d2%d%d" % (h, b)])

    def bridge_keys(h, k):
        o = B * k + HB * h
        tt(T.th[:, o:o + HB], T.sp[:].indirect(wu("bl", 16 * k + 8 * h, 16 * k + 8 * h + 8)), T.m0[:, 0:HB], A.add, ["sp", "sp0", "sp1", "bl%d" % k, "m0"], ["th%d%d" % (h, k)])

    def stage(h, k):
        a, z, bank = HB * h, HB * (h + 1), "ps%d" % (3 - h)
        if k == 0:
            after("k2%d" % h)
            tt(T.tq[:, 3 * a:3 * z:3], T[bank][:, 0:HB], T.th[:, a:z], A.is_ge, [bank, "th%d0" % h], ["tql%d" % h])
            tt(T.tq[:, 3 * a + 1:3 * z:3], T[bank][:, 0:HB], T.th[:, B + a:B + z], A.is_gt, [bank, "th%d1" % h], ["tqu%d" % h])
        if k == 1:
            scan(half("p3s", h, 3), T.rz3[:], half("tq", h, 3), 0.0, A.mult, A.add, ["tql%d" % h, "tqu%d" % h, "tqb", "rz3b"], ["p3s%d" % h])
        if k == 2:
            ts(wu("lp", 8 * h, 8 * h + 8), T.p3s[:, 3 * a + 47:3 * z:48], float(NS), A.add, r=["p3s%d" % h], w=["lp%d" % h])

    def pick(h, t, on_vector):
        move(on_vector, T.z2[:, 4 * HB * h + t:4 * HB * (h + 1):4], T.zt[:, 400 * t:400 * t + C + 1].indirect(wu("lp", 8 * h, 8 * h + 8)),
             ["zt%d" % (t // 2), "lp%d" % h], ["z2%d%d" % (h, t)])

    def last(h):
        pack("2", h)
        after("y20%d" % h)
        mm(4 + h, HB, T.qv[:], T.sv[:], half("qy2", h), half("sy2", h), True, True, ["qv", "qy2%d" % h], ["yp%d" % h])
        dma("Y", T.oc[:, 4 * HB * h:4 * HB * (h + 1)], by(half("qy2", h)), "so1", r=["qy2%d" % h])

    def store(h, on_vector):
        after("yp%d" % h)
        move(on_vector, half("yo", h), T["ps%d" % (4 + h)][:, 0:HB], ["ps%d" % (4 + h)], ["yo%d" % h])
        dma("Y", T.y[:, HB * h:HB * (h + 1)], half("yo", h), "so1", r=["yo%d" % h])

    def scales_out():
        for k in range(4):
            dma("S", T.osc[4 * k:4 * k + 4, :], T.sy2[32 * k:32 * k + 4, :], "so2", r=["qy20", "qy21"])

    step.update({
        "br": bridges,
        "m0": lambda: fill(T.rz3[:], 1.0, ["rz3"]),
        "m1": lambda: fill(T.tq[:, 2:3 * B:3], 0.0, ["tqz"]),
        "m2": lambda: op("V", lambda: V.memset(T.rz3[:, 0:C:48], 0.0), ["rz3"], ["rz3b"]),
        "b0": lambda: (after("bout"), ts(wu("bl", 0, 16), T.bin[:], C - 1.0, A.min, r=["bin"], w=["bl0"])),
        "b1": lambda: (after("bout"), ts(wu("bl", 16, 32), T.bin[:], C - 1.0, A.min, 1.0, A.add, r=["bin"], w=["bl1"])),
        "b2": lambda: (after("bout"), ts(T.tq[:, 2:3 * B:48], T.bin[:], C - 1.0, A.min, -1.0 - NS, A.add, r=["bin", "tqz"], w=["tqb"])),
        "qv": lambda: quant(T.qv[:], T.sv[:], T.vt[:], ["vt"], ["qv"]),
        "K0": lambda: (after("qy10"), queries_came(0, range(4), 3)),
        "K1": lambda: (after("tql0", "qy11"), queries_came(1, (0, 1, 3), 2)),
        "K2": lambda: (after("tql1"), queries_came(1, (2,))),
        "ov": lambda: dma("Y", T.ov[:], T.pv[0:128:16, :], "so1", r=["pv0", "pv1"]),
        "sc": scales_out,
    })
    for h in range(2):
        step.update({"z%d" % h: lambda h=h: products("1", h), "h%d" % h: lambda h=h: hand_on(h), "y%d" % h: lambda h=h: products("2", h), "Q%d" % h: lambda h=h: last(h)})
        for k in range(9):
            step["c%d%d" % (h, k)] = lambda h=h, k=k: choose(h, k)
        for k in range(3):
            step["s%d%d" % (h, k)] = lambda h=h, k=k: stage(h, k)
        for k in range(2):
            step["t%d%d" % (h, k)] = lambda h=h, k=k: bridge_keys(h, k)
        for v in range(2):
            step["wW"[v] + "%d_" % h] = lambda h=h, v=v: store(h, v)
            step["vV"[v] + "%d" % h] = lambda h=h, v=v: move(v, half("pv", h), T.jj[:].indirect(wu("lp", 8 * h, 8 * h + 8)), ["jj", "lp%d" % h], ["pv%d" % h])
            for t in range(4):
                step["lL"[v] + "%d%d" % (h, t)] = lambda h=h, t=t, v=v: lower(h, t, v)
                step["rR"[v] + "%d%d" % (h, t)] = lambda h=h, t=t, v=v: result("1", h, t, v)
                step["oO"[v] + "%d%d" % (h, t)] = lambda h=h, t=t, v=v: result("2", h, t, v)
                step["gG"[v] + "%d%d" % (h, t)] = lambda h=h, t=t, v=v: pick(h, t, v)
        for t in range(4):
            step["u%d%d" % (h, t)] = lambda h=h, t=t: upper(h, t)

    for phase in ORDER.values():
        for name in phase.split():
            TRACE.append(("step", name))
            step[name]()

    for e in cnt:
        g.wait_ge(T.sem["e" + e], cnt[e])
    for sem in ("left", "so1", "so2"):
        g.wait_ge(T.sem[sem], dcnt[sem])
